import numpy as np
import ml_dtypes


def mxq(x, axis, fmt="e4m3"):
    dtype, down = {"e4m3": (ml_dtypes.float8_e4m3fn, 7), "e5m2": (ml_dtypes.float8_e5m2, 14)}[fmt]
    v = np.moveaxis(np.asarray(x, np.float32).astype(ml_dtypes.bfloat16).astype(np.float64), axis, -1)
    blocks = v.reshape(v.shape[:-1] + (-1, 32))
    amax = np.abs(blocks).max(-1, keepdims=True)
    byte = np.maximum(np.where(amax > 0, np.frexp(amax)[1] - 1 + 127, 0) - down, 1)
    scale = np.exp2(byte - 127.0)
    codes = (blocks / scale).astype(np.float32).astype(dtype).astype(np.float64)
    return np.moveaxis((codes * scale).reshape(v.shape), -1, axis)


WIDE = False


def mx_kscale(k):
    if not WIDE:
        return np.ones(k)
    levels = np.array([10, -10, 5, -5, 0])
    if k % 512:
        return np.exp2(np.random.permutation(np.resize(levels, k // 32))).repeat(32)
    a = np.empty((k // 512, 16))
    for p in range(k // 512):
        a[p, :8] = np.random.permutation(np.resize(levels, 8))
        for g in range(8):
            far = levels[np.abs(levels - a[p, g]) >= 10]
            a[p, g + 8] = far[np.random.randint(len(far))]
    return np.exp2(a.ravel()).repeat(32)


def f64(x):
    return np.asarray(x).astype(np.float64)


def striped(idx):
    return np.tile(idx.reshape(-1, 16).T, (8, 1)).astype(np.uint16)


def unstriped(offs):
    return offs[:16].T.reshape(-1).astype(np.int64)


E2M1 = np.array([0.0, 0.5, 1.0, 1.5, 2.0, 3.0, 4.0, 6.0, -0.0, -0.5, -1.0, -1.5, -2.0, -3.0, -4.0, -6.0])


def pack_weight(w, fmt):
    k, n = w.shape
    w = f64(np.asarray(w, np.float32).astype(ml_dtypes.bfloat16)).reshape(k // 32, 32, n)
    amax = np.abs(w).max(1)
    if fmt == "e4m3":
        byte = np.frexp(amax)[1] - 1 + 127 - 7
    else:
        mant, ex = np.frexp(amax / 6.0)
        byte = np.where(mant > 0.5, ex, ex - 1) + 127
    byte = np.clip(np.where(amax > 0, byte, 1), 1, 254)
    scaled = (w * np.exp2(127.0 - byte)[:, None, :]).reshape(k, n).astype(np.float32)
    by_word = np.ascontiguousarray(scaled.reshape(k // 512, 128, 4, n).transpose(0, 1, 3, 2))
    if fmt == "e4m3":
        words = by_word.astype(ml_dtypes.float8_e4m3fn).view(np.uint8)
    else:
        c = by_word.astype(ml_dtypes.float4_e2m1fn).view(np.uint8) & 0xF
        words = (c[..., 0::2] | (c[..., 1::2] << 4)).reshape(k // 512, 128, 2 * n)
    return np.ascontiguousarray(words), np.ascontiguousarray(byte.astype(np.uint8).reshape(k // 512, 16, n))


def unpack_weight(words, scales, fmt):
    g, _, n = scales.shape
    words = np.ascontiguousarray(words).reshape(g, 128, n, -1)
    if fmt == "e4m3":
        vals = words.view(ml_dtypes.float8_e4m3fn).astype(np.float64)
    else:
        nib = np.empty((g, 128, n, 4), np.uint8)
        nib[..., 0::2] = words & 0xF
        nib[..., 1::2] = words >> 4
        vals = E2M1[nib]
    vals = vals * np.repeat(np.exp2(scales.astype(np.float64) - 127.0), 8, axis=1)[..., None]
    return vals.transpose(0, 1, 3, 2).reshape(g * 512, n)


def gelu(v):
    return 0.5 * v * (1.0 + np.tanh(np.sqrt(2.0 / np.pi) * (v + 0.044715 * v**3)))


def bf(x):
    return np.asarray(x, np.float32).astype(ml_dtypes.bfloat16)

def planes(Y):
    n, m = Y.shape
    b = f64(bf(Y)).reshape(n // 32, 32, m)
    amax = np.abs(b).max(1)
    byte = np.clip(np.where(amax > 0, np.frexp(amax)[1] - 1 + 127 - 7, 1), 1, 254)
    codes = (b * np.exp2(127.0 - byte)[:, None, :]).reshape(n, m).astype(np.float32).astype(ml_dtypes.float8_e4m3fn).view(np.uint8)
    words = codes.reshape(n // 512, 128, 4, m).transpose(0, 1, 3, 2)
    return np.ascontiguousarray(words), np.ascontiguousarray(byte.astype(np.uint8).reshape(n // 512, 16, m))


K, T, S, T2, S2, N = 1024, 2048, 1024, 4096, 1024, 512

def setup_inputs():
    n = np.random.standard_normal
    s = mx_kscale(K)[:, None]
    u = mx_kscale(S)[:, None]
    r = np.exp(0.8 * n(N))
    tab_words, tab_scales = pack_weight(n((K, T)) / np.sqrt(K) / s, "e4m3")
    tab2_words, tab2_scales = pack_weight(n((K, T2)) * s, "e4m3")
    w4_words, w4_scales = pack_weight(0.7 * n((K, N)) / np.sqrt(K) * r / s, "e2m1")
    return {
        "tab_words": tab_words, "tab_scales": tab_scales,
        "tab2_words": tab2_words, "tab2_scales": tab2_scales,
        "w4_words": w4_words, "w4_scales": w4_scales,
        "w": (n((S, N)) / np.sqrt(S) * r / u).astype(np.float32),
        "lam": (0.5 * np.exp(0.2 * n(S))).astype(np.float32),
        "g": (np.exp(0.3 * n(S)) * u[:, 0]).astype(np.float32),
        "b": (0.4 * n(N) * r).astype(np.float32),
        "offs": striped(np.random.permutation(T)[:S]),
        "offs2": striped(np.random.permutation(T2)[:S2]),
    }

def reference(tab_words, tab_scales, tab2_words, tab2_scales, w4_words, w4_scales, w, lam, g, b, offs, offs2):
    v = unpack_weight(tab_words, tab_scales, "e4m3")[:, unstriped(offs)]
    v2 = unpack_weight(tab2_words, tab2_scales, "e4m3")[:, unstriped(offs2)]
    w4 = unpack_weight(w4_words, w4_scales, "e2m1")
    a = v.T @ v2
    th = f64(lam)[:, None]
    h = (a - np.minimum(np.maximum(a, -th), th)) * f64(g)[:, None]
    y = mxq(f64(w), 0, "e4m3").T @ mxq(h, 0, "e4m3") + w4.T @ v2
    y = y + f64(b)[:, None]
    words, scales = planes(y)
    return y, words, scales

@@ -1,0 +1,285 @@
+from contextlib import ExitStack
+
+import concourse.mybir as mybir
+
+K, T, S, T2, S2, N = 1024, 2048, 1024, 4096, 1024, 512
+FLOPS = 2 * (K * S * S2 + S * N * S2 + K * N * S2)
+
+F32 = mybir.dt.float32
+BF16 = mybir.dt.bfloat16
+I32 = mybir.dt.int32
+U32 = mybir.dt.uint32
+U16 = mybir.dt.uint16
+U8 = mybir.dt.uint8
+FP8X4 = mybir.dt.float8_e4m3fn_x4
+FP4X4 = mybir.dt.float4_e2m1fn_x4
+ALU = mybir.AluOpType
+ACT = mybir.ActivationFunctionType
+
+P = 128
+PACK = 4
+PASS = P * PACK
+BANK = 512
+CHUNKS = [512,256,256]
+CLAMP_ON_VECTOR = [[0,0,0,0],[0,0,0,1],[0,0,0,1],[0,0,1,1],[0,0,1,1],[0,1,1,1]]
+Y_ON_VECTOR = [[0,0,0,0],[0,0,0,0],[0,0,1,1]]
+
+
+def tile_list_sparse_code_synthesis_kernel(
+    tc, tab_words, tab_scales, tab2_words, tab2_scales, w4_words, w4_scales, w, lam, g, b, offs, offs2,
+    out_0, out_1, out_2,
+):
+    nc = tc.nc
+    with ExitStack() as ctx:
+        lists = ctx.enter_context(tc.tile_pool(name="lists", bufs=1))
+        keep = ctx.enter_context(tc.tile_pool(name="keep", bufs=1))
+        work = ctx.enter_context(tc.tile_pool(name="work", bufs=2))
+        psum = ctx.enter_context(tc.psum_pool(name="psum", bufs=4))
+
+        idx2 = lists.tile([P, S2 // 16], U16, name="idx2")
+        idx = lists.tile([P, S // 16], U16, name="idx")
+        nc.sync.dma_start(idx2[:], offs2)
+        nc.sync.dma_start(idx[:], offs)
+
+        v2s_win = keep.tile([P, T2], U8, name="v2s_win", tag="slot_a", align_bytes=64)
+        vs_win = keep.tile([P, T], U8, name="vs_win", tag="slot_c", align_bytes=64)
+        w4s_raw = keep.tile([P, 2 * N], U8, name="w4s_raw", align_bytes=64)
+        v2s_one = keep.tile([P, S2], U8, name="v2s_one", align_bytes=64)
+        for plane in (v2s_win, vs_win, w4s_raw, v2s_one):
+            nc.vector.memset(plane[:].bitcast(I32), 0)
+
+        w4_raw = keep.tile([P, 2, 2 * N], U8, name="w4_raw", align_bytes=64)
+        nc.sync.dma_start(w4_raw[:].bitcast(I32), w4_words.rearrange("a p c -> p a c").bitcast(I32))
+
+        v_win = [
+            keep.tile([P, T], I32, name="v_win0", tag="slot_b", align_bytes=64),
+            keep.tile([P, T], I32, name="v_win1", align_bytes=64),
+        ]
+        v2_win = [
+            keep.tile([P, T2], I32, name="v2_win0", tag="slot_e", align_bytes=64),
+            keep.tile([P, T2], I32, name="v2_win1", tag="slot_f", align_bytes=64),
+        ]
+
+        def load_words(win, words):
+            nc.sync.dma_start(win[:], words.rearrange("p t i -> p (t i)").bitcast(I32))
+
+        load_words(v_win[0], tab_words[0])
+        for q in range(4):
+            nc.gpsimd.dma_start(
+                v2s_win[32 * q : 32 * q + 8, :].bitcast(I32), tab2_scales[:, 4 * q : 4 * q + 4, :].bitcast(I32)
+            )
+        for q in range(4):
+            nc.gpsimd.dma_start(
+                vs_win[32 * q + 8 : 32 * q + 16, :].bitcast(I32), tab_scales[:, 4 * q : 4 * q + 4, :].bitcast(I32)
+            )
+        load_words(v2_win[0], tab2_words[0])
+        load_words(v2_win[1], tab2_words[1])
+        load_words(v_win[1], tab_words[1])
+        lam_sb = keep.tile([P, 2, PACK], F32, name="lam_sb")
+        gain = keep.tile([P, 2, PACK], F32, name="gain")
+        bias = keep.tile([P, PACK], F32, name="bias")
+        nc.scalar.dma_start(lam_sb[:], lam.rearrange("(h p t) -> p h t", h=2, t=PACK))
+        nc.scalar.dma_start(gain[:], g.rearrange("(h p t) -> p h t", h=2, t=PACK))
+        for q in range(4):
+            nc.gpsimd.dma_start(
+                w4s_raw[32 * q : 32 * q + 4, :].bitcast(I32).rearrange("r (a c) -> r a c", a=2),
+                w4_scales[:, 4 * q : 4 * q + 4, :].rearrange("a r c -> r a c").bitcast(I32),
+            )
+        nc.scalar.dma_start(bias[:], b.rearrange("(p t) -> p t", t=PACK))
+
+        gain_lam = keep.tile([P, 2, PACK], F32, name="gain_lam")
+        cut = keep.tile([P, 2, PACK], F32, name="cut")
+        neg_cut = keep.tile([P, 2, PACK], F32, name="neg_cut")
+        neg_gain = keep.tile([P, 2, PACK], F32, name="neg_gain")
+        nc.gpsimd.tensor_tensor(gain_lam[:], gain[:], lam_sb[:], ALU.mult)
+        nc.scalar.activation(cut[:], gain_lam[:], ACT.Abs)
+        nc.scalar.activation(neg_cut[:], cut[:], ACT.Copy, scale=-1.0)
+        nc.scalar.activation(neg_gain[:], gain[:], ACT.Copy, scale=-1.0)
+
+        w4_codes = keep.tile([P, 2, 2 * N], U8, name="w4_codes", align_bytes=64)
+        w4_sc = keep.tile([P, 2 * N], U8, name="w4_sc", align_bytes=64)
+        nc.vector.tensor_copy(
+            w4_codes[:].rearrange("p a (t m e) -> p a m t e", t=PACK, e=2),
+            w4_raw[:].rearrange("p a (m t e) -> p a m t e", t=PACK, e=2),
+        )
+
+        v_codes = [keep.tile([P, S], U32, name="v_codes0", align_bytes=64)]
+        v2_codes = []
+
+        def gather_v(a, h0, h1):
+            nc.vector.tensor_copy(
+                v_codes[a][:, PASS * h0 : PASS * h1].rearrange("p (h t m) -> p h m t", t=PACK, m=P),
+                v_win[a][:].bitcast(U32).indirect(idx[:, 32 * h0 : 32 * h1]),
+            )
+
+        def gather_v2(a, j0, j1):
+            nc.vector.tensor_copy(
+                v2_codes[a][:, j0:j1], v2_win[a][:].bitcast(U32).indirect(idx2[:, j0 // 16 : j1 // 16])
+            )
+
+        gather_v(0, 0, 2)
+        v2s = keep.tile([P, S2], U8, name="v2s", align_bytes=64)
+        nc.vector.tensor_copy(v2s[:], v2s_win[:].indirect(idx2[:]))
+        nc.scalar.dma_start(v2s_one[0:112, :].bitcast(I32), v2s[4:116, :].bitcast(I32))
+        v2_codes.append(keep.tile([P, S2], U32, name="v2_codes0", tag="slot_a", align_bytes=64))
+        gather_v2(0, 0, S2)
+        vs_listed = keep.tile([P, S], U8, name="vs_listed", tag="slot_d", align_bytes=64)
+        vs = keep.tile([P, S], U8, name="vs", align_bytes=64)
+        nc.vector.tensor_copy(vs_listed[:], vs_win[:].indirect(idx[:]))
+        nc.vector.tensor_copy(
+            vs[:].rearrange("p (h t m) -> p h m t", t=PACK, m=P),
+            vs_listed[:].rearrange("p (h m t) -> p h m t", t=PACK, m=P),
+        )
+        v2_codes.append(keep.tile([P, S2], U32, name="v2_codes1", tag="slot_c", align_bytes=64))
+        v_codes.append(keep.tile([P, S], U32, name="v_codes1", tag="slot_d", align_bytes=64))
+        gather_v2(1, 0, S2 // 2)
+        gather_v(1, 0, 1)
+        gather_v(1, 1, 2)
+        nc.vector.tensor_copy(
+            w4_sc[:].rearrange("p (a t m) -> p a m t", t=PACK, m=P),
+            w4s_raw[:].rearrange("p (a m t) -> p a m t", t=PACK, m=P),
+        )
+        gather_v2(1, S2 // 2, S2)
+
+        w_raw = [
+            keep.tile([P, PACK, N], F32, name="w_raw0", tag="slot_b", align_bytes=64),
+            keep.tile([P, PACK, N], F32, name="w_raw1", tag="slot_e", align_bytes=64),
+        ]
+        for h in range(2):
+            nc.sync.dma_start(w_raw[h][:], w[PASS * h : PASS * (h + 1), :].rearrange("(p e) n -> p e n", e=PACK))
+        w_codes = [keep.tile([P, N], U32, name="w_codes%d" % h, align_bytes=64) for h in range(2)]
+        w_sc = [keep.tile([P, N], U8, name="w_sc%d" % h, align_bytes=64) for h in range(2)]
+
+        def quantise_w(h):
+            w_bf = keep.tile([P, PACK * N], BF16, name="w_bf", tag="slot_f", align_bytes=64)
+            nc.vector.tensor_copy(
+                w_bf[:].rearrange("p (t m e) -> p m e t", t=PACK, e=PACK),
+                w_raw[h][:].rearrange("p e (m t) -> p m e t", t=PACK),
+            )
+            nc.vector.quantize_mx(w_codes[h][:].bitcast(FP8X4), w_sc[h][:], w_bf[:])
+
+        v2_planes = [v2s, v2s_one]
+        y_sc = keep.tile([P, S2], U8, name="y_sc", align_bytes=64)
+        y_rows = out_0.rearrange("(p t) j -> p t j", t=PACK)
+        y_words = out_1[0].rearrange("p m t -> p (m t)").bitcast(I32)
+
+        def bank_views(tag, width):
+            per_bank = BANK // width
+            views = []
+            for k in range(PACK // per_bank):
+                bank = psum.tile([P, BANK], F32, name=tag)
+                views.extend([bank[:, width * s : width * (s + 1)] for s in range(per_bank)])
+            return views
+
+        def open_y(j0, width):
+            acc = bank_views("y_bank", width)
+            per_bank = BANK // width
+            step = BANK if width == BANK else P
+            for a in range(2):
+                for t in range(PACK):
+                    for c in range(0, width, step):
+                        nc.tensor.matmul_mx(
+                            acc[t][:, c : c + step],
+                            lhsT=w4_codes[:, a, 2 * P * t : 2 * P * (t + 1)].bitcast(FP4X4),
+                            lhsT_scale=w4_sc[:, N * a + P * t : N * a + P * (t + 1)],
+                            rhs=v2_codes[a][:, j0 + c : j0 + c + step].bitcast(FP8X4),
+                            rhs_scale=v2_planes[a][:, j0 + c : j0 + c + step],
+                            start=(a == 0 and c == 0 and t % per_bank == 0),
+                            stop=False,
+                        )
+            return acc
+
+        def codes_of(j0, width, h, on_vector):
+            acc = bank_views("a_bank", width)
+            lhs = work.tile([P, PACK, width], F32, name="lhs")
+            rhs = work.tile([P, PACK, width], F32, name="rhs")
+            for t in range(PACK):
+                cols = slice(PASS * h + P * t, PASS * h + P * (t + 1))
+                for a in range(2):
+                    nc.tensor.matmul_mx(
+                        acc[t],
+                        lhsT=v_codes[a][:, cols].bitcast(FP8X4),
+                        lhsT_scale=vs[8 + 4 * a : P, cols],
+                        rhs=v2_codes[a][:, j0 : j0 + width].bitcast(FP8X4),
+                        rhs_scale=v2_planes[a][:, j0 : j0 + width],
+                        start=(a == 0),
+                        stop=(a == 1),
+                    )
+            for t in range(PACK):
+                one = slice(t, t + 1)
+                if on_vector[t]:
+                    nc.scalar.activation(lhs[:, t, :], acc[t], ACT.Copy, scale=gain[:, h, one])
+                    nc.vector.tensor_scalar(
+                        rhs[:, t, :], lhs[:, t, :], neg_cut[:, h, one], cut[:, h, one], ALU.max, ALU.min
+                    )
+                else:
+                    nc.scalar.activation(
+                        lhs[:, t, :], acc[t], ACT.Relu, bias=neg_cut[:, h, one], scale=gain[:, h, one]
+                    )
+                    nc.scalar.activation(
+                        rhs[:, t, :], acc[t], ACT.Relu, bias=neg_cut[:, h, one], scale=neg_gain[:, h, one]
+                    )
+            h_bf = work.tile([P, PACK * width], BF16, name="h_bf", align_bytes=64)
+            nc.vector.tensor_tensor(
+                h_bf[:].rearrange("p (c i t) -> p c t i", i=2, t=PACK),
+                lhs[:].rearrange("p t (c i) -> p c t i", i=2),
+                rhs[:].rearrange("p t (c i) -> p c t i", i=2),
+                ALU.subtract,
+            )
+            h_codes = work.tile([P, width], U32, name="h_codes", align_bytes=64)
+            h_sc = work.tile([P, width], U8, name="h_sc", align_bytes=64)
+            nc.vector.quantize_mx(h_codes[:].bitcast(FP8X4), h_sc[:], h_bf[:])
+            return h_codes, h_sc
+
+        def add_codes(acc, width, h, h_codes, h_sc):
+            per_bank = BANK // width
+            for t in range(PACK):
+                nc.tensor.matmul_mx(
+                    acc[t],
+                    lhsT=w_codes[h][:, P * t : P * (t + 1)].bitcast(FP8X4),
+                    lhsT_scale=w_sc[h][:, P * t : P * (t + 1)],
+                    rhs=h_codes[:].bitcast(FP8X4),
+                    rhs_scale=h_sc[:],
+                    start=False,
+                    stop=(h == 1 and t % per_bank == per_bank - 1),
+                )
+
+        def finish(acc, j0, width, on_vector):
+            y = work.tile([P, PACK, width], F32, name="y")
+            for t in range(PACK):
+                if on_vector[t]:
+                    nc.vector.tensor_scalar(y[:, t, :], acc[t], bias[:, t : t + 1], None, ALU.add)
+                else:
+                    nc.scalar.activation(y[:, t, :], acc[t], ACT.Identity, bias=bias[:, t : t + 1])
+                if t % 2 == 1:
+                    nc.sync.dma_start(y_rows[:, t - 1 : t + 1, j0 : j0 + width], y[:, t - 1 : t + 1, :])
+            y_bf = work.tile([P, PACK * width], BF16, name="y_bf", align_bytes=64)
+            nc.vector.tensor_copy(
+                y_bf[:].rearrange("p (c i t) -> p c t i", i=2, t=PACK),
+                y[:].rearrange("p t (c i) -> p c t i", i=2),
+            )
+            y_codes = work.tile([P, width], U32, name="y_codes", align_bytes=64)
+            nc.vector.quantize_mx(y_codes[:].bitcast(FP8X4), y_sc[:, j0 : j0 + width], y_bf[:])
+            nc.sync.dma_start(y_words[:, j0 : j0 + width], y_codes[:].bitcast(I32))
+
+        j0 = 0
+        pending = None
+        for n, width in enumerate(CHUNKS):
+            first = codes_of(j0, width, 0, CLAMP_ON_VECTOR[2 * n])
+            if pending is not None:
+                finish(*pending)
+            acc = open_y(j0, width)
+            if n == 0:
+                quantise_w(0)
+            add_codes(acc, width, 0, *first)
+            second = codes_of(j0, width, 1, CLAMP_ON_VECTOR[2 * n + 1])
+            if n == 0:
+                quantise_w(1)
+            add_codes(acc, width, 1, *second)
+            pending = (acc, j0, width, Y_ON_VECTOR[n])
+            j0 = j0 + width
+        finish(*pending)
+        for q in range(4):
+            (nc.sync if q % 2 == 0 else nc.scalar).dma_start(
+                out_2[0, 4 * q : 4 * q + 4, :].bitcast(I32), y_sc[32 * q : 32 * q + 4, :].bitcast(I32)
+            )

@@ -21,7 +21,7 @@ PACK = 4
 PASS = P * PACK
 BANK = 512
 CHUNKS = [512,256,256]
-CLAMP_ON_VECTOR = [[0,0,0,0],[0,0,0,1],[0,0,0,1],[0,0,1,1],[0,0,1,1],[0,1,1,1]]
+CLAMP_ON_VECTOR = [[0,0,1,1],[0,0,1,1],[0,0,1,1],[0,0,1,1],[0,0,1,1],[1,1,1,1]]
 Y_ON_VECTOR = [[0,0,0,0],[0,0,0,0],[0,0,1,1]]
 
 
@@ -41,6 +41,12 @@ def tile_list_sparse_code_synthesis_kernel(
         nc.sync.dma_start(idx2[:], offs2)
         nc.sync.dma_start(idx[:], offs)
 
+        lam_sb = keep.tile([P, 2, PACK], F32, name="lam_sb")
+        gain = keep.tile([P, 2, PACK], F32, name="gain")
+        bias = keep.tile([P, PACK], F32, name="bias")
+        nc.gpsimd.dma_start(lam_sb[:], lam.rearrange("(h p t) -> p h t", h=2, t=PACK))
+        nc.gpsimd.dma_start(gain[:], g.rearrange("(h p t) -> p h t", h=2, t=PACK))
+
         v2s_win = keep.tile([P, T2], U8, name="v2s_win", tag="slot_a", align_bytes=64)
         vs_win = keep.tile([P, T], U8, name="vs_win", tag="slot_c", align_bytes=64)
         w4s_raw = keep.tile([P, 2 * N], U8, name="w4s_raw", align_bytes=64)
@@ -48,53 +54,28 @@ def tile_list_sparse_code_synthesis_kernel(
         for plane in (v2s_win, vs_win, w4s_raw, v2s_one):
             nc.vector.memset(plane[:].bitcast(I32), 0)
 
-        w4_raw = keep.tile([P, 2, 2 * N], U8, name="w4_raw", align_bytes=64)
-        nc.sync.dma_start(w4_raw[:].bitcast(I32), w4_words.rearrange("a p c -> p a c").bitcast(I32))
-
-        v_win = [
-            keep.tile([P, T], I32, name="v_win0", tag="slot_b", align_bytes=64),
-            keep.tile([P, T], I32, name="v_win1", align_bytes=64),
-        ]
-        v2_win = [
-            keep.tile([P, T2], I32, name="v2_win0", tag="slot_e", align_bytes=64),
-            keep.tile([P, T2], I32, name="v2_win1", tag="slot_f", align_bytes=64),
-        ]
-
         def load_words(win, words):
             nc.sync.dma_start(win[:], words.rearrange("p t i -> p (t i)").bitcast(I32))
 
+        v_win = [keep.tile([P, T], I32, name="v_win0", tag="slot_b", align_bytes=64)]
+        v2_win = [keep.tile([P, T2], I32, name="v2_win0", tag="slot_e", align_bytes=64)]
         load_words(v_win[0], tab_words[0])
-        for q in range(4):
-            nc.gpsimd.dma_start(
-                v2s_win[32 * q : 32 * q + 8, :].bitcast(I32), tab2_scales[:, 4 * q : 4 * q + 4, :].bitcast(I32)
-            )
+        load_words(v2_win[0], tab2_words[0])
+        w4_raw = keep.tile([P, 2, 2 * N], U8, name="w4_raw", align_bytes=64)
+        nc.scalar.dma_start(w4_raw[:].bitcast(I32), w4_words.rearrange("a p c -> p a c").bitcast(I32))
+        nc.scalar.dma_start(bias[:], b.rearrange("(p t) -> p t", t=PACK))
+        v2s_rows = tab2_scales.rearrange("a (q r) t -> r q a t", r=4)
+        for r in range(4):
+            nc.scalar.dma_start(v2s_win[r:P:16, :].bitcast(I32), v2s_rows[r].bitcast(I32))
         for q in range(4):
             nc.gpsimd.dma_start(
                 vs_win[32 * q + 8 : 32 * q + 16, :].bitcast(I32), tab_scales[:, 4 * q : 4 * q + 4, :].bitcast(I32)
             )
-        load_words(v2_win[0], tab2_words[0])
-        load_words(v2_win[1], tab2_words[1])
-        load_words(v_win[1], tab_words[1])
-        lam_sb = keep.tile([P, 2, PACK], F32, name="lam_sb")
-        gain = keep.tile([P, 2, PACK], F32, name="gain")
-        bias = keep.tile([P, PACK], F32, name="bias")
-        nc.scalar.dma_start(lam_sb[:], lam.rearrange("(h p t) -> p h t", h=2, t=PACK))
-        nc.scalar.dma_start(gain[:], g.rearrange("(h p t) -> p h t", h=2, t=PACK))
         for q in range(4):
-            nc.gpsimd.dma_start(
+            nc.scalar.dma_start(
                 w4s_raw[32 * q : 32 * q + 4, :].bitcast(I32).rearrange("r (a c) -> r a c", a=2),
                 w4_scales[:, 4 * q : 4 * q + 4, :].rearrange("a r c -> r a c").bitcast(I32),
             )
-        nc.scalar.dma_start(bias[:], b.rearrange("(p t) -> p t", t=PACK))
-
-        gain_lam = keep.tile([P, 2, PACK], F32, name="gain_lam")
-        cut = keep.tile([P, 2, PACK], F32, name="cut")
-        neg_cut = keep.tile([P, 2, PACK], F32, name="neg_cut")
-        neg_gain = keep.tile([P, 2, PACK], F32, name="neg_gain")
-        nc.gpsimd.tensor_tensor(gain_lam[:], gain[:], lam_sb[:], ALU.mult)
-        nc.scalar.activation(cut[:], gain_lam[:], ACT.Abs)
-        nc.scalar.activation(neg_cut[:], cut[:], ACT.Copy, scale=-1.0)
-        nc.scalar.activation(neg_gain[:], gain[:], ACT.Copy, scale=-1.0)
 
         w4_codes = keep.tile([P, 2, 2 * N], U8, name="w4_codes", align_bytes=64)
         w4_sc = keep.tile([P, 2 * N], U8, name="w4_sc", align_bytes=64)
@@ -103,7 +84,16 @@ def tile_list_sparse_code_synthesis_kernel(
             w4_raw[:].rearrange("p a (m t e) -> p a m t e", t=PACK, e=2),
         )
 
-        v_codes = [keep.tile([P, S], U32, name="v_codes0", align_bytes=64)]
+        gain_lam = keep.tile([P, 2, PACK], F32, name="gain_lam")
+        cut = keep.tile([P, 2, PACK], F32, name="cut")
+        neg_cut = keep.tile([P, 2, PACK], F32, name="neg_cut")
+        neg_gain = keep.tile([P, 2, PACK], F32, name="neg_gain")
+        nc.vector.tensor_tensor(gain_lam[:], gain[:], lam_sb[:], ALU.mult)
+        nc.scalar.activation(cut[:], gain_lam[:], ACT.Abs)
+        nc.scalar.activation(neg_cut[:], cut[:], ACT.Copy, scale=-1.0)
+        nc.scalar.activation(neg_gain[:], gain[:], ACT.Copy, scale=-1.0)
+
+        v_codes = [keep.tile([P, S], U32, name="v_codes%d" % a, align_bytes=64) for a in range(2)]
         v2_codes = []
 
         def gather_v(a, h0, h1):
@@ -118,11 +108,15 @@ def tile_list_sparse_code_synthesis_kernel(
             )
 
         gather_v(0, 0, 2)
+        v2_win.append(keep.tile([P, T2], I32, name="v2_win1", tag="slot_b", align_bytes=64))
+        load_words(v2_win[1], tab2_words[1])
         v2s = keep.tile([P, S2], U8, name="v2s", align_bytes=64)
         nc.vector.tensor_copy(v2s[:], v2s_win[:].indirect(idx2[:]))
-        nc.scalar.dma_start(v2s_one[0:112, :].bitcast(I32), v2s[4:116, :].bitcast(I32))
+        nc.scalar.dma_start(v2s_one[0:112, :].bitcast(I32), v2s[16:P, :].bitcast(I32))
         v2_codes.append(keep.tile([P, S2], U32, name="v2_codes0", tag="slot_a", align_bytes=64))
         gather_v2(0, 0, S2)
+        v_win.append(keep.tile([P, T], I32, name="v_win1", tag="slot_e", align_bytes=64))
+        load_words(v_win[1], tab_words[1])
         vs_listed = keep.tile([P, S], U8, name="vs_listed", tag="slot_d", align_bytes=64)
         vs = keep.tile([P, S], U8, name="vs", align_bytes=64)
         nc.vector.tensor_copy(vs_listed[:], vs_win[:].indirect(idx[:]))
@@ -131,7 +125,6 @@ def tile_list_sparse_code_synthesis_kernel(
             vs_listed[:].rearrange("p (h m t) -> p h m t", t=PACK, m=P),
         )
         v2_codes.append(keep.tile([P, S2], U32, name="v2_codes1", tag="slot_c", align_bytes=64))
-        v_codes.append(keep.tile([P, S], U32, name="v_codes1", tag="slot_d", align_bytes=64))
         gather_v2(1, 0, S2 // 2)
         gather_v(1, 0, 1)
         gather_v(1, 1, 2)
@@ -142,7 +135,7 @@ def tile_list_sparse_code_synthesis_kernel(
         gather_v2(1, S2 // 2, S2)
 
         w_raw = [
-            keep.tile([P, PACK, N], F32, name="w_raw0", tag="slot_b", align_bytes=64),
+            keep.tile([P, PACK, N], F32, name="w_raw0", tag="slot_d", align_bytes=64),
             keep.tile([P, PACK, N], F32, name="w_raw1", tag="slot_e", align_bytes=64),
         ]
         for h in range(2):
@@ -151,7 +144,7 @@ def tile_list_sparse_code_synthesis_kernel(
         w_sc = [keep.tile([P, N], U8, name="w_sc%d" % h, align_bytes=64) for h in range(2)]
 
         def quantise_w(h):
-            w_bf = keep.tile([P, PACK * N], BF16, name="w_bf", tag="slot_f", align_bytes=64)
+            w_bf = keep.tile([P, PACK * N], BF16, name="w_bf", tag="slot_b", align_bytes=64)
             nc.vector.tensor_copy(
                 w_bf[:].rearrange("p (t m e) -> p m e t", t=PACK, e=PACK),
                 w_raw[h][:].rearrange("p e (m t) -> p m e t", t=PACK),
@@ -191,8 +184,8 @@ def tile_list_sparse_code_synthesis_kernel(
 
         def codes_of(j0, width, h, on_vector):
             acc = bank_views("a_bank", width)
-            lhs = work.tile([P, PACK, width], F32, name="lhs")
-            rhs = work.tile([P, PACK, width], F32, name="rhs")
+            lhs = work.tile([P, PACK, width], F32, name="lhs", bufs=3)
+            rhs = work.tile([P, PACK, width], F32, name="rhs", bufs=3)
             for t in range(PACK):
                 cols = slice(PASS * h + P * t, PASS * h + P * (t + 1))
                 for a in range(2):
@@ -226,8 +219,8 @@ def tile_list_sparse_code_synthesis_kernel(
                 rhs[:].rearrange("p t (c i) -> p c t i", i=2),
                 ALU.subtract,
             )
-            h_codes = work.tile([P, width], U32, name="h_codes", align_bytes=64)
-            h_sc = work.tile([P, width], U8, name="h_sc", align_bytes=64)
+            h_codes = work.tile([P, width], U32, name="h_codes", bufs=3, align_bytes=64)
+            h_sc = work.tile([P, width], U8, name="h_sc", bufs=3, align_bytes=64)
             nc.vector.quantize_mx(h_codes[:].bitcast(FP8X4), h_sc[:], h_bf[:])
             return h_codes, h_sc
 
@@ -266,15 +259,17 @@ def tile_list_sparse_code_synthesis_kernel(
         pending = None
         for n, width in enumerate(CHUNKS):
             first = codes_of(j0, width, 0, CLAMP_ON_VECTOR[2 * n])
-            if pending is not None:
-                finish(*pending)
-            acc = open_y(j0, width)
-            if n == 0:
+            if pending is None:
+                acc = open_y(j0, width)
                 quantise_w(0)
-            add_codes(acc, width, 0, *first)
-            second = codes_of(j0, width, 1, CLAMP_ON_VECTOR[2 * n + 1])
-            if n == 0:
+                add_codes(acc, width, 0, *first)
+                second = codes_of(j0, width, 1, CLAMP_ON_VECTOR[2 * n + 1])
                 quantise_w(1)
+            else:
+                second = codes_of(j0, width, 1, CLAMP_ON_VECTOR[2 * n + 1])
+                finish(*pending)
+                acc = open_y(j0, width)
+                add_codes(acc, width, 0, *first)
             add_codes(acc, width, 1, *second)
             pending = (acc, j0, width, Y_ON_VECTOR[n])
             j0 = j0 + width

@@ -20,9 +20,9 @@ P = 128
 PACK = 4
 PASS = P * PACK
 BANK = 512
-CHUNKS = [512,256,256]
-CLAMP_ON_VECTOR = [[0,0,1,1],[0,0,1,1],[0,0,1,1],[0,0,1,1],[0,0,1,1],[1,1,1,1]]
-Y_ON_VECTOR = [[0,0,0,0],[0,0,0,0],[0,0,1,1]]
+CHUNKS = [512,512]
+CLAMP_ON_VECTOR = [[0,0,1,1],[0,0,1,1],[0,0,1,1],[0,0,1,1]]
+Y_ON_VECTOR = [[0,0,0,0],[0,0,1,1]]
 
 
 def tile_list_sparse_code_synthesis_kernel(
@@ -46,31 +46,27 @@ def tile_list_sparse_code_synthesis_kernel(
         bias = keep.tile([P, PACK], F32, name="bias")
         nc.gpsimd.dma_start(lam_sb[:], lam.rearrange("(h p t) -> p h t", h=2, t=PACK))
         nc.gpsimd.dma_start(gain[:], g.rearrange("(h p t) -> p h t", h=2, t=PACK))
+        nc.gpsimd.dma_start(bias[:], b.rearrange("(p t) -> p t", t=PACK))
 
         v2s_win = keep.tile([P, T2], U8, name="v2s_win", tag="slot_a", align_bytes=64)
         vs_win = keep.tile([P, T], U8, name="vs_win", tag="slot_c", align_bytes=64)
         w4s_raw = keep.tile([P, 2 * N], U8, name="w4s_raw", align_bytes=64)
         v2s_one = keep.tile([P, S2], U8, name="v2s_one", align_bytes=64)
-        for plane in (v2s_win, vs_win, w4s_raw, v2s_one):
+        vs_one = keep.tile([P, S], U8, name="vs_one", align_bytes=64)
+        for plane in (v2s_win, vs_win, w4s_raw, v2s_one, vs_one):
             nc.vector.memset(plane[:].bitcast(I32), 0)
 
         def load_words(win, words):
             nc.sync.dma_start(win[:], words.rearrange("p t i -> p (t i)").bitcast(I32))
 
+        w4_raw = keep.tile([P, 2, 2 * N], U8, name="w4_raw", tag="slot_e", align_bytes=64)
+        nc.sync.dma_start(w4_raw[:].bitcast(I32), w4_words.rearrange("a p c -> p a c").bitcast(I32))
         v_win = [keep.tile([P, T], I32, name="v_win0", tag="slot_b", align_bytes=64)]
-        v2_win = [keep.tile([P, T2], I32, name="v2_win0", tag="slot_e", align_bytes=64)]
         load_words(v_win[0], tab_words[0])
-        load_words(v2_win[0], tab2_words[0])
-        w4_raw = keep.tile([P, 2, 2 * N], U8, name="w4_raw", align_bytes=64)
-        nc.scalar.dma_start(w4_raw[:].bitcast(I32), w4_words.rearrange("a p c -> p a c").bitcast(I32))
-        nc.scalar.dma_start(bias[:], b.rearrange("(p t) -> p t", t=PACK))
-        v2s_rows = tab2_scales.rearrange("a (q r) t -> r q a t", r=4)
-        for r in range(4):
-            nc.scalar.dma_start(v2s_win[r:P:16, :].bitcast(I32), v2s_rows[r].bitcast(I32))
-        for q in range(4):
-            nc.gpsimd.dma_start(
-                vs_win[32 * q + 8 : 32 * q + 16, :].bitcast(I32), tab_scales[:, 4 * q : 4 * q + 4, :].bitcast(I32)
-            )
+        for win, first, scales in ((v2s_win, 0, tab2_scales), (vs_win, 8, tab_scales)):
+            rows = scales.rearrange("a (q r) t -> r q a t", r=4)
+            for r in range(4):
+                nc.scalar.dma_start(win[first + r : P : 16, :].bitcast(I32), rows[r].bitcast(I32))
         for q in range(4):
             nc.scalar.dma_start(
                 w4s_raw[32 * q : 32 * q + 4, :].bitcast(I32).rearrange("r (a c) -> r a c", a=2),
@@ -80,9 +76,12 @@ def tile_list_sparse_code_synthesis_kernel(
         w4_codes = keep.tile([P, 2, 2 * N], U8, name="w4_codes", align_bytes=64)
         w4_sc = keep.tile([P, 2 * N], U8, name="w4_sc", align_bytes=64)
         nc.vector.tensor_copy(
-            w4_codes[:].rearrange("p a (t m e) -> p a m t e", t=PACK, e=2),
-            w4_raw[:].rearrange("p a (m t e) -> p a m t e", t=PACK, e=2),
+            w4_codes[:].rearrange("p a (t m e) -> p a t m e", t=PACK, e=2),
+            w4_raw[:].rearrange("p a (m t e) -> p a t m e", t=PACK, e=2),
         )
+
+        v2_win = [keep.tile([P, T2], I32, name="v2_win0", tag="slot_e", align_bytes=64)]
+        load_words(v2_win[0], tab2_words[0])
 
         gain_lam = keep.tile([P, 2, PACK], F32, name="gain_lam")
         cut = keep.tile([P, 2, PACK], F32, name="cut")
@@ -93,13 +92,13 @@ def tile_list_sparse_code_synthesis_kernel(
         nc.scalar.activation(neg_cut[:], cut[:], ACT.Copy, scale=-1.0)
         nc.scalar.activation(neg_gain[:], gain[:], ACT.Copy, scale=-1.0)
 
-        v_codes = [keep.tile([P, S], U32, name="v_codes%d" % a, align_bytes=64) for a in range(2)]
+        v_codes = [keep.tile([P, S], U32, name="v_codes0", align_bytes=64)]
         v2_codes = []
 
-        def gather_v(a, h0, h1):
+        def gather_v(a):
             nc.vector.tensor_copy(
-                v_codes[a][:, PASS * h0 : PASS * h1].rearrange("p (h t m) -> p h m t", t=PACK, m=P),
-                v_win[a][:].bitcast(U32).indirect(idx[:, 32 * h0 : 32 * h1]),
+                v_codes[a][:].rearrange("p (h t m) -> p h m t", t=PACK, m=P),
+                v_win[a][:].bitcast(U32).indirect(idx[:]),
             )
 
         def gather_v2(a, j0, j1):
@@ -107,36 +106,37 @@ def tile_list_sparse_code_synthesis_kernel(
                 v2_codes[a][:, j0:j1], v2_win[a][:].bitcast(U32).indirect(idx2[:, j0 // 16 : j1 // 16])
             )
 
-        gather_v(0, 0, 2)
-        v2_win.append(keep.tile([P, T2], I32, name="v2_win1", tag="slot_b", align_bytes=64))
-        load_words(v2_win[1], tab2_words[1])
+        gather_v(0)
+        v_win.append(keep.tile([P, T], I32, name="v_win1", tag="slot_b", align_bytes=64))
+        load_words(v_win[1], tab_words[1])
         v2s = keep.tile([P, S2], U8, name="v2s", align_bytes=64)
         nc.vector.tensor_copy(v2s[:], v2s_win[:].indirect(idx2[:]))
         nc.scalar.dma_start(v2s_one[0:112, :].bitcast(I32), v2s[16:P, :].bitcast(I32))
-        v2_codes.append(keep.tile([P, S2], U32, name="v2_codes0", tag="slot_a", align_bytes=64))
-        gather_v2(0, 0, S2)
-        v_win.append(keep.tile([P, T], I32, name="v_win1", tag="slot_e", align_bytes=64))
-        load_words(v_win[1], tab_words[1])
+        v2_win.append(keep.tile([P, T2], I32, name="v2_win1", tag="slot_a", align_bytes=64))
+        load_words(v2_win[1], tab2_words[1])
         vs_listed = keep.tile([P, S], U8, name="vs_listed", tag="slot_d", align_bytes=64)
         vs = keep.tile([P, S], U8, name="vs", align_bytes=64)
         nc.vector.tensor_copy(vs_listed[:], vs_win[:].indirect(idx[:]))
         nc.vector.tensor_copy(
-            vs[:].rearrange("p (h t m) -> p h m t", t=PACK, m=P),
-            vs_listed[:].rearrange("p (h m t) -> p h m t", t=PACK, m=P),
+            vs[:].rearrange("p (h t m) -> p h t m", t=PACK, m=P),
+            vs_listed[:].rearrange("p (h m t) -> p h t m", t=PACK, m=P),
         )
-        v2_codes.append(keep.tile([P, S2], U32, name="v2_codes1", tag="slot_c", align_bytes=64))
-        gather_v2(1, 0, S2 // 2)
-        gather_v(1, 0, 1)
-        gather_v(1, 1, 2)
+        nc.scalar.dma_start(vs_one[0:112, :].bitcast(I32), vs[16:P, :].bitcast(I32))
+        v2_codes.append(keep.tile([P, S2], U32, name="v2_codes0", tag="slot_d", align_bytes=64))
+        gather_v2(0, 0, S2)
+        v_codes.append(keep.tile([P, S], U32, name="v_codes1", tag="slot_c", align_bytes=64))
+        gather_v(1)
         nc.vector.tensor_copy(
-            w4_sc[:].rearrange("p (a t m) -> p a m t", t=PACK, m=P),
-            w4s_raw[:].rearrange("p (a m t) -> p a m t", t=PACK, m=P),
+            w4_sc[:].rearrange("p (a t m) -> p a t m", t=PACK, m=P),
+            w4s_raw[:].rearrange("p (a m t) -> p a t m", t=PACK, m=P),
         )
+        v2_codes.append(keep.tile([P, S2], U32, name="v2_codes1", align_bytes=64))
+        gather_v2(1, 0, S2 // 2)
         gather_v2(1, S2 // 2, S2)
 
         w_raw = [
-            keep.tile([P, PACK, N], F32, name="w_raw0", tag="slot_d", align_bytes=64),
-            keep.tile([P, PACK, N], F32, name="w_raw1", tag="slot_e", align_bytes=64),
+            keep.tile([P, PACK, N], F32, name="w_raw0", tag="slot_e", align_bytes=64),
+            keep.tile([P, PACK, N], F32, name="w_raw1", tag="slot_b", align_bytes=64),
         ]
         for h in range(2):
             nc.sync.dma_start(w_raw[h][:], w[PASS * h : PASS * (h + 1), :].rearrange("(p e) n -> p e n", e=PACK))
@@ -144,13 +144,14 @@ def tile_list_sparse_code_synthesis_kernel(
         w_sc = [keep.tile([P, N], U8, name="w_sc%d" % h, align_bytes=64) for h in range(2)]
 
         def quantise_w(h):
-            w_bf = keep.tile([P, PACK * N], BF16, name="w_bf", tag="slot_b", align_bytes=64)
-            nc.vector.tensor_copy(
-                w_bf[:].rearrange("p (t m e) -> p m e t", t=PACK, e=PACK),
-                w_raw[h][:].rearrange("p e (m t) -> p m e t", t=PACK),
-            )
+            w_bf = keep.tile([P, PACK * N], BF16, name="w_bf", tag="slot_a", align_bytes=64)
+            dealt = w_bf[:].rearrange("p (t m e) -> p m e t", t=PACK, e=PACK)
+            rows = w_raw[h][:].rearrange("p e (m t) -> p m e t", t=PACK)
+            for t in (0, 2):
+                nc.vector.tensor_copy(dealt[:, :, :, t : t + 2], rows[:, :, :, t : t + 2])
             nc.vector.quantize_mx(w_codes[h][:].bitcast(FP8X4), w_sc[h][:], w_bf[:])
 
+        v_planes = [vs, vs_one]
         v2_planes = [v2s, v2s_one]
         y_sc = keep.tile([P, S2], U8, name="y_sc", align_bytes=64)
         y_rows = out_0.rearrange("(p t) j -> p t j", t=PACK)
@@ -192,7 +193,7 @@ def tile_list_sparse_code_synthesis_kernel(
                     nc.tensor.matmul_mx(
                         acc[t],
                         lhsT=v_codes[a][:, cols].bitcast(FP8X4),
-                        lhsT_scale=vs[8 + 4 * a : P, cols],
+                        lhsT_scale=v_planes[a][8:P, cols],
                         rhs=v2_codes[a][:, j0 : j0 + width].bitcast(FP8X4),
                         rhs_scale=v2_planes[a][:, j0 : j0 + width],
                         start=(a == 0),
@@ -237,7 +238,7 @@ def tile_list_sparse_code_synthesis_kernel(
                     stop=(h == 1 and t % per_bank == per_bank - 1),
                 )
 
-        def finish(acc, j0, width, on_vector):
+        def finish(acc, j0, width, on_vector, round_y):
             y = work.tile([P, PACK, width], F32, name="y")
             for t in range(PACK):
                 if on_vector[t]:
@@ -247,7 +248,7 @@ def tile_list_sparse_code_synthesis_kernel(
                 if t % 2 == 1:
                     nc.sync.dma_start(y_rows[:, t - 1 : t + 1, j0 : j0 + width], y[:, t - 1 : t + 1, :])
             y_bf = work.tile([P, PACK * width], BF16, name="y_bf", align_bytes=64)
-            nc.vector.tensor_copy(
+            round_y(
                 y_bf[:].rearrange("p (c i t) -> p c t i", i=2, t=PACK),
                 y[:].rearrange("p t (c i) -> p c t i", i=2),
             )
@@ -271,7 +272,8 @@ def tile_list_sparse_code_synthesis_kernel(
                 acc = open_y(j0, width)
                 add_codes(acc, width, 0, *first)
             add_codes(acc, width, 1, *second)
-            pending = (acc, j0, width, Y_ON_VECTOR[n])
+            last = n == len(CHUNKS) - 1
+            pending = (acc, j0, width, Y_ON_VECTOR[n], nc.vector.tensor_copy if last else nc.scalar.copy)
             j0 = j0 + width
         finish(*pending)
         for q in range(4):

@@ -1,6 +1,7 @@
 from contextlib import ExitStack
 
 import concourse.mybir as mybir
+from concourse.masks import make_identity
 
 K, T, S, T2, S2, N = 1024, 2048, 1024, 4096, 1024, 512
 FLOPS = 2 * (K * S * S2 + S * N * S2 + K * N * S2)
@@ -21,7 +22,7 @@ PACK = 4
 PASS = P * PACK
 BANK = 512
 CHUNKS = [512,512]
-CLAMP_ON_VECTOR = [[0,0,1,1],[0,0,1,1],[0,0,1,1],[0,0,1,1]]
+CLAMP_ON_VECTOR = [[0,0,1,1],[0,0,0,1],[0,0,0,1],[0,0,0,1]]
 Y_ON_VECTOR = [[0,0,0,0],[0,0,1,1]]
 
 
@@ -41,11 +42,16 @@ def tile_list_sparse_code_synthesis_kernel(
         nc.sync.dma_start(idx2[:], offs2)
         nc.sync.dma_start(idx[:], offs)
 
-        lam_sb = keep.tile([P, 2, PACK], F32, name="lam_sb")
-        gain = keep.tile([P, 2, PACK], F32, name="gain")
         bias = keep.tile([P, PACK], F32, name="bias")
-        nc.gpsimd.dma_start(lam_sb[:], lam.rearrange("(h p t) -> p h t", h=2, t=PACK))
-        nc.gpsimd.dma_start(gain[:], g.rearrange("(h p t) -> p h t", h=2, t=PACK))
+        by_slot = keep.tile([P, P], F32, name="by_slot")
+        ident = keep.tile([P, P], F32, name="ident")
+        nc.gpsimd.memset(by_slot[:], 0.0)
+        for k, vec in enumerate((lam, g)):
+            nc.gpsimd.dma_start(
+                by_slot[8 * k : 8 * k + 8, :].rearrange("s (u q) -> s u q", q=8),
+                vec.rearrange("(u s q) -> s u q", s=8, q=8),
+            )
+        make_identity(nc, ident[:])
         nc.gpsimd.dma_start(bias[:], b.rearrange("(p t) -> p t", t=PACK))
 
         v2s_win = keep.tile([P, T2], U8, name="v2s_win", tag="slot_a", align_bytes=64)
@@ -83,21 +89,26 @@ def tile_list_sparse_code_synthesis_kernel(
         v2_win = [keep.tile([P, T2], I32, name="v2_win0", tag="slot_e", align_bytes=64)]
         load_words(v2_win[0], tab2_words[0])
 
+        turned = psum.tile([P, BANK], F32, name="a_bank")
+        nc.tensor.transpose(turned[:, 0:P], by_slot[:], ident[:])
+        lam_gain = keep.tile([P, 2, 2, PACK], F32, name="lam_gain")
+        nc.scalar.copy(lam_gain[:].rearrange("p v h t -> p (v h t)"), turned[:, 0:16])
+        gain = lam_gain[:, 1]
         gain_lam = keep.tile([P, 2, PACK], F32, name="gain_lam")
         cut = keep.tile([P, 2, PACK], F32, name="cut")
         neg_cut = keep.tile([P, 2, PACK], F32, name="neg_cut")
         neg_gain = keep.tile([P, 2, PACK], F32, name="neg_gain")
-        nc.vector.tensor_tensor(gain_lam[:], gain[:], lam_sb[:], ALU.mult)
+        nc.vector.tensor_tensor(gain_lam[:], gain, lam_gain[:, 0], ALU.mult)
         nc.scalar.activation(cut[:], gain_lam[:], ACT.Abs)
         nc.scalar.activation(neg_cut[:], cut[:], ACT.Copy, scale=-1.0)
-        nc.scalar.activation(neg_gain[:], gain[:], ACT.Copy, scale=-1.0)
+        nc.scalar.activation(neg_gain[:], gain, ACT.Copy, scale=-1.0)
 
         v_codes = [keep.tile([P, S], U32, name="v_codes0", align_bytes=64)]
         v2_codes = []
 
         def gather_v(a):
             nc.vector.tensor_copy(
-                v_codes[a][:].rearrange("p (h t m) -> p h m t", t=PACK, m=P),
+                v_codes[a][:].rearrange("p (s u q) -> p u s q", s=8, q=8),
                 v_win[a][:].bitcast(U32).indirect(idx[:]),
             )
 
@@ -118,8 +129,8 @@ def tile_list_sparse_code_synthesis_kernel(
         vs = keep.tile([P, S], U8, name="vs", align_bytes=64)
         nc.vector.tensor_copy(vs_listed[:], vs_win[:].indirect(idx[:]))
         nc.vector.tensor_copy(
-            vs[:].rearrange("p (h t m) -> p h t m", t=PACK, m=P),
-            vs_listed[:].rearrange("p (h m t) -> p h t m", t=PACK, m=P),
+            vs[:].bitcast(I32).rearrange("p (s u e) -> p s u e", s=8, e=2),
+            vs_listed[:].bitcast(I32).rearrange("p (u s e) -> p s u e", s=8, e=2),
         )
         nc.scalar.dma_start(vs_one[0:112, :].bitcast(I32), vs[16:P, :].bitcast(I32))
         v2_codes.append(keep.tile([P, S2], U32, name="v2_codes0", tag="slot_d", align_bytes=64))
@@ -138,8 +149,10 @@ def tile_list_sparse_code_synthesis_kernel(
             keep.tile([P, PACK, N], F32, name="w_raw0", tag="slot_e", align_bytes=64),
             keep.tile([P, PACK, N], F32, name="w_raw1", tag="slot_b", align_bytes=64),
         ]
+        w_rows = w.rearrange("(u h t q) n -> h t u q n", h=2, t=PACK, q=8)
         for h in range(2):
-            nc.sync.dma_start(w_raw[h][:], w[PASS * h : PASS * (h + 1), :].rearrange("(p e) n -> p e n", e=PACK))
+            for t in range(PACK):
+                nc.sync.dma_start(w_raw[h][:, t, :], w_rows[h, t])
         w_codes = [keep.tile([P, N], U32, name="w_codes%d" % h, align_bytes=64) for h in range(2)]
         w_sc = [keep.tile([P, N], U8, name="w_sc%d" % h, align_bytes=64) for h in range(2)]
 

@@ -20,10 +20,13 @@ ACT = mybir.ActivationFunctionType
 P = 128
 PACK = 4
 PASS = P * PACK
+PASSES = 2
+BLOCK_P = 8
 BANK = 512
-CHUNKS = [512,512]
-CLAMP_ON_VECTOR = [[0,0,1,1],[0,0,0,1],[0,0,0,1],[0,0,0,1]]
-Y_ON_VECTOR = [[0,0,0,0],[0,0,1,1]]
+LIST_ROWS = 16
+PASS_SHIFT = 16
+V_ROW = 8
+CHUNKS = (256, 512, 256)
 
 
 def tile_list_sparse_code_synthesis_kernel(
@@ -37,69 +40,69 @@ def tile_list_sparse_code_synthesis_kernel(
         work = ctx.enter_context(tc.tile_pool(name="work", bufs=2))
         psum = ctx.enter_context(tc.psum_pool(name="psum", bufs=4))
 
-        idx2 = lists.tile([P, S2 // 16], U16, name="idx2")
-        idx = lists.tile([P, S // 16], U16, name="idx")
+        idx2 = lists.tile([P, S2 // LIST_ROWS], U16, name="idx2")
+        idx = lists.tile([P, S // LIST_ROWS], U16, name="idx")
         nc.sync.dma_start(idx2[:], offs2)
         nc.sync.dma_start(idx[:], offs)
 
         bias = keep.tile([P, PACK], F32, name="bias")
-        by_slot = keep.tile([P, P], F32, name="by_slot")
+        by_place = keep.tile([P, P], F32, name="by_place")
         ident = keep.tile([P, P], F32, name="ident")
-        nc.gpsimd.memset(by_slot[:], 0.0)
+        places = PASSES * PACK
+        nc.gpsimd.memset(by_place[:], 0.0)
         for k, vec in enumerate((lam, g)):
             nc.gpsimd.dma_start(
-                by_slot[8 * k : 8 * k + 8, :].rearrange("s (u q) -> s u q", q=8),
-                vec.rearrange("(u s q) -> s u q", s=8, q=8),
+                by_place[places * k : places * (k + 1), :].rearrange("s (u q) -> s u q", q=BLOCK_P),
+                vec.rearrange("(u s q) -> s u q", s=places, q=BLOCK_P),
             )
         make_identity(nc, ident[:])
         nc.gpsimd.dma_start(bias[:], b.rearrange("(p t) -> p t", t=PACK))
 
-        v2s_win = keep.tile([P, T2], U8, name="v2s_win", tag="slot_a", align_bytes=64)
-        vs_win = keep.tile([P, T], U8, name="vs_win", tag="slot_c", align_bytes=64)
-        w4s_raw = keep.tile([P, 2 * N], U8, name="w4s_raw", align_bytes=64)
-        v2s_one = keep.tile([P, S2], U8, name="v2s_one", align_bytes=64)
-        vs_one = keep.tile([P, S], U8, name="vs_one", align_bytes=64)
-        for plane in (v2s_win, vs_win, w4s_raw, v2s_one, vs_one):
+        v2s_table = keep.tile([P, T2], U8, name="v2s_table", tag="slot_a", align_bytes=64)
+        vs_table = keep.tile([P, T], U8, name="vs_table", tag="slot_c", align_bytes=64)
+        w4s_raw = keep.tile([P, PASSES * N], U8, name="w4s_raw", align_bytes=64)
+        v2s_pass1 = keep.tile([P, S2], U8, name="v2s_pass1", align_bytes=64)
+        vs_pass1 = keep.tile([P, S], U8, name="vs_pass1", align_bytes=64)
+        for plane in (v2s_table, vs_table, w4s_raw, v2s_pass1, vs_pass1):
             nc.vector.memset(plane[:].bitcast(I32), 0)
 
-        def load_words(win, words):
-            nc.sync.dma_start(win[:], words.rearrange("p t i -> p (t i)").bitcast(I32))
+        def load_words(table, words):
+            nc.sync.dma_start(table[:], words.rearrange("p t i -> p (t i)").bitcast(I32))
 
-        w4_raw = keep.tile([P, 2, 2 * N], U8, name="w4_raw", tag="slot_e", align_bytes=64)
+        w4_raw = keep.tile([P, PASSES, 2 * N], U8, name="w4_raw", tag="slot_e", align_bytes=64)
         nc.sync.dma_start(w4_raw[:].bitcast(I32), w4_words.rearrange("a p c -> p a c").bitcast(I32))
-        v_win = [keep.tile([P, T], I32, name="v_win0", tag="slot_b", align_bytes=64)]
-        load_words(v_win[0], tab_words[0])
-        for win, first, scales in ((v2s_win, 0, tab2_scales), (vs_win, 8, tab_scales)):
-            rows = scales.rearrange("a (q r) t -> r q a t", r=4)
+        v_table = [keep.tile([P, T], I32, name="v_table0", tag="slot_b", align_bytes=64)]
+        load_words(v_table[0], tab_words[0])
+        for table, first, scales in ((v2s_table, 0, tab2_scales), (vs_table, V_ROW, tab_scales)):
+            scale_rows = scales.rearrange("a (q r) t -> r q a t", r=4)
             for r in range(4):
-                nc.scalar.dma_start(win[first + r : P : 16, :].bitcast(I32), rows[r].bitcast(I32))
+                nc.scalar.dma_start(table[first + r : P : PASS_SHIFT, :].bitcast(I32), scale_rows[r].bitcast(I32))
         for q in range(4):
             nc.scalar.dma_start(
-                w4s_raw[32 * q : 32 * q + 4, :].bitcast(I32).rearrange("r (a c) -> r a c", a=2),
+                w4s_raw[32 * q : 32 * q + 4, :].bitcast(I32).rearrange("r (a c) -> r a c", a=PASSES),
                 w4_scales[:, 4 * q : 4 * q + 4, :].rearrange("a r c -> r a c").bitcast(I32),
             )
 
-        w4_codes = keep.tile([P, 2, 2 * N], U8, name="w4_codes", align_bytes=64)
-        w4_sc = keep.tile([P, 2 * N], U8, name="w4_sc", align_bytes=64)
+        w4_codes = keep.tile([P, PASSES, 2 * N], U8, name="w4_codes", align_bytes=64)
+        w4_sc = keep.tile([P, PASSES * N], U8, name="w4_sc", align_bytes=64)
         nc.vector.tensor_copy(
             w4_codes[:].rearrange("p a (t m e) -> p a t m e", t=PACK, e=2),
             w4_raw[:].rearrange("p a (m t e) -> p a t m e", t=PACK, e=2),
         )
 
-        v2_win = [keep.tile([P, T2], I32, name="v2_win0", tag="slot_e", align_bytes=64)]
-        load_words(v2_win[0], tab2_words[0])
+        v2_table = [keep.tile([P, T2], I32, name="v2_table0", tag="slot_e", align_bytes=64)]
+        load_words(v2_table[0], tab2_words[0])
 
         turned = psum.tile([P, BANK], F32, name="a_bank")
-        nc.tensor.transpose(turned[:, 0:P], by_slot[:], ident[:])
-        lam_gain = keep.tile([P, 2, 2, PACK], F32, name="lam_gain")
-        nc.scalar.copy(lam_gain[:].rearrange("p v h t -> p (v h t)"), turned[:, 0:16])
-        gain = lam_gain[:, 1]
-        gain_lam = keep.tile([P, 2, PACK], F32, name="gain_lam")
-        cut = keep.tile([P, 2, PACK], F32, name="cut")
-        neg_cut = keep.tile([P, 2, PACK], F32, name="neg_cut")
-        neg_gain = keep.tile([P, 2, PACK], F32, name="neg_gain")
-        nc.vector.tensor_tensor(gain_lam[:], gain, lam_gain[:, 0], ALU.mult)
-        nc.scalar.activation(cut[:], gain_lam[:], ACT.Abs)
+        nc.tensor.transpose(turned[:, 0:P], by_place[:], ident[:])
+        lam_gain = keep.tile([P, 2 * places], F32, name="lam_gain")
+        nc.scalar.copy(lam_gain[:], turned[:, 0 : 2 * places])
+        gain = lam_gain[:, places : 2 * places]
+        cut = keep.tile([P, places], F32, name="cut")
+        neg_cut = keep.tile([P, places], F32, name="neg_cut")
+        neg_gain = keep.tile([P, places], F32, name="neg_gain")
+        for s in range(places):
+            nc.scalar.activation(cut[:, s : s + 1], gain[:, s : s + 1], ACT.Abs, scale=lam_gain[:, s : s + 1])
         nc.scalar.activation(neg_cut[:], cut[:], ACT.Copy, scale=-1.0)
         nc.scalar.activation(neg_gain[:], gain, ACT.Copy, scale=-1.0)
 
@@ -108,31 +111,35 @@ def tile_list_sparse_code_synthesis_kernel(
 
         def gather_v(a):
             nc.vector.tensor_copy(
-                v_codes[a][:].rearrange("p (s u q) -> p u s q", s=8, q=8),
-                v_win[a][:].bitcast(U32).indirect(idx[:]),
+                v_codes[a][:].rearrange("p (s u q) -> p u s q", s=places, q=BLOCK_P),
+                v_table[a][:].bitcast(U32).indirect(idx[:]),
             )
 
         def gather_v2(a, j0, j1):
             nc.vector.tensor_copy(
-                v2_codes[a][:, j0:j1], v2_win[a][:].bitcast(U32).indirect(idx2[:, j0 // 16 : j1 // 16])
+                v2_codes[a][:, j0:j1],
+                v2_table[a][:].bitcast(U32).indirect(idx2[:, j0 // LIST_ROWS : j1 // LIST_ROWS]),
             )
 
+        def shift_pass1(plane, gathered):
+            nc.scalar.dma_start(plane[0 : P - PASS_SHIFT, :].bitcast(I32), gathered[PASS_SHIFT:P, :].bitcast(I32))
+
         gather_v(0)
-        v_win.append(keep.tile([P, T], I32, name="v_win1", tag="slot_b", align_bytes=64))
-        load_words(v_win[1], tab_words[1])
+        v_table.append(keep.tile([P, T], I32, name="v_table1", tag="slot_b", align_bytes=64))
+        load_words(v_table[1], tab_words[1])
         v2s = keep.tile([P, S2], U8, name="v2s", align_bytes=64)
-        nc.vector.tensor_copy(v2s[:], v2s_win[:].indirect(idx2[:]))
-        nc.scalar.dma_start(v2s_one[0:112, :].bitcast(I32), v2s[16:P, :].bitcast(I32))
-        v2_win.append(keep.tile([P, T2], I32, name="v2_win1", tag="slot_a", align_bytes=64))
-        load_words(v2_win[1], tab2_words[1])
+        nc.vector.tensor_copy(v2s[:], v2s_table[:].indirect(idx2[:]))
+        shift_pass1(v2s_pass1, v2s)
+        v2_table.append(keep.tile([P, T2], I32, name="v2_table1", tag="slot_a", align_bytes=64))
+        load_words(v2_table[1], tab2_words[1])
         vs_listed = keep.tile([P, S], U8, name="vs_listed", tag="slot_d", align_bytes=64)
         vs = keep.tile([P, S], U8, name="vs", align_bytes=64)
-        nc.vector.tensor_copy(vs_listed[:], vs_win[:].indirect(idx[:]))
+        nc.vector.tensor_copy(vs_listed[:], vs_table[:].indirect(idx[:]))
         nc.vector.tensor_copy(
-            vs[:].bitcast(I32).rearrange("p (s u e) -> p s u e", s=8, e=2),
-            vs_listed[:].bitcast(I32).rearrange("p (u s e) -> p s u e", s=8, e=2),
+            vs[:].bitcast(I32).rearrange("p (s u e) -> p s u e", s=places, e=2),
+            vs_listed[:].bitcast(I32).rearrange("p (u s e) -> p s u e", s=places, e=2),
         )
-        nc.scalar.dma_start(vs_one[0:112, :].bitcast(I32), vs[16:P, :].bitcast(I32))
+        shift_pass1(vs_pass1, vs)
         v2_codes.append(keep.tile([P, S2], U32, name="v2_codes0", tag="slot_d", align_bytes=64))
         gather_v2(0, 0, S2)
         v_codes.append(keep.tile([P, S], U32, name="v_codes1", tag="slot_c", align_bytes=64))
@@ -149,40 +156,46 @@ def tile_list_sparse_code_synthesis_kernel(
             keep.tile([P, PACK, N], F32, name="w_raw0", tag="slot_e", align_bytes=64),
             keep.tile([P, PACK, N], F32, name="w_raw1", tag="slot_b", align_bytes=64),
         ]
-        w_rows = w.rearrange("(u h t q) n -> h t u q n", h=2, t=PACK, q=8)
-        for h in range(2):
+        w_rows = w.rearrange("(u h t q) n -> h t u q n", h=PASSES, t=PACK, q=BLOCK_P)
+        for h in range(PASSES):
             for t in range(PACK):
                 nc.sync.dma_start(w_raw[h][:, t, :], w_rows[h, t])
-        w_codes = [keep.tile([P, N], U32, name="w_codes%d" % h, align_bytes=64) for h in range(2)]
-        w_sc = [keep.tile([P, N], U8, name="w_sc%d" % h, align_bytes=64) for h in range(2)]
+        w_codes = [keep.tile([P, N], U32, name="w_codes%d" % h, align_bytes=64) for h in range(PASSES)]
+        w_sc = [keep.tile([P, N], U8, name="w_sc%d" % h, align_bytes=64) for h in range(PASSES)]
 
         def quantise_w(h):
             w_bf = keep.tile([P, PACK * N], BF16, name="w_bf", tag="slot_a", align_bytes=64)
-            dealt = w_bf[:].rearrange("p (t m e) -> p m e t", t=PACK, e=PACK)
-            rows = w_raw[h][:].rearrange("p e (m t) -> p m e t", t=PACK)
-            for t in (0, 2):
-                nc.vector.tensor_copy(dealt[:, :, :, t : t + 2], rows[:, :, :, t : t + 2])
+            dealt = w_bf[:].rearrange("p (c m t) -> p m t c", c=PACK, t=PACK)
+            loaded = w_raw[h][:].rearrange("p t (m c) -> p m t c", c=PACK)
+            for c in (0, 2):
+                nc.vector.tensor_copy(dealt[:, :, :, c : c + 2], loaded[:, :, :, c : c + 2])
             nc.vector.quantize_mx(w_codes[h][:].bitcast(FP8X4), w_sc[h][:], w_bf[:])
 
-        v_planes = [vs, vs_one]
-        v2_planes = [v2s, v2s_one]
+        v_planes = [vs, vs_pass1]
+        v2_planes = [v2s, v2s_pass1]
         y_sc = keep.tile([P, S2], U8, name="y_sc", align_bytes=64)
         y_rows = out_0.rearrange("(p t) j -> p t j", t=PACK)
         y_words = out_1[0].rearrange("p m t -> p (m t)").bitcast(I32)
 
-        def bank_views(tag, width):
+        def psum_results(tag, width):
             per_bank = BANK // width
-            views = []
-            for k in range(PACK // per_bank):
+            results = []
+            for first_t in range(0, PACK, per_bank):
                 bank = psum.tile([P, BANK], F32, name=tag)
-                views.extend([bank[:, width * s : width * (s + 1)] for s in range(per_bank)])
-            return views
+                results.extend([bank[:, width * s : width * (s + 1)] for s in range(per_bank)])
+            return results
+
+        def interleave(words, rows, run):
+            nc.vector.tensor_copy(
+                words[:].rearrange("p (c i t) -> p c t i", i=run, t=PACK),
+                rows[:].rearrange("p t (c i) -> p c t i", i=run),
+            )
 
         def open_y(j0, width):
-            acc = bank_views("y_bank", width)
+            acc = psum_results("y_bank", width)
             per_bank = BANK // width
             step = BANK if width == BANK else P
-            for a in range(2):
+            for a in range(PASSES):
                 for t in range(PACK):
                     for c in range(0, width, step):
                         nc.tensor.matmul_mx(
@@ -196,43 +209,40 @@ def tile_list_sparse_code_synthesis_kernel(
                         )
             return acc
 
-        def codes_of(j0, width, h, on_vector):
-            acc = bank_views("a_bank", width)
-            lhs = work.tile([P, PACK, width], F32, name="lhs", bufs=3)
-            rhs = work.tile([P, PACK, width], F32, name="rhs", bufs=3)
+        def quantised_h(j0, width, h):
+            clamp_on_vector = j0 == 0 and h == 0
+            acc = psum_results("a_bank", width)
+            dtype = F32 if clamp_on_vector else BF16
+            minuend = work.tile([P, PACK, width], dtype, name="minuend", bufs=3)
+            subtrahend = work.tile([P, PACK, width], dtype, name="subtrahend", bufs=3)
             for t in range(PACK):
                 cols = slice(PASS * h + P * t, PASS * h + P * (t + 1))
-                for a in range(2):
+                for a in range(PASSES):
                     nc.tensor.matmul_mx(
                         acc[t],
                         lhsT=v_codes[a][:, cols].bitcast(FP8X4),
-                        lhsT_scale=v_planes[a][8:P, cols],
+                        lhsT_scale=v_planes[a][V_ROW:P, cols],
                         rhs=v2_codes[a][:, j0 : j0 + width].bitcast(FP8X4),
                         rhs_scale=v2_planes[a][:, j0 : j0 + width],
                         start=(a == 0),
-                        stop=(a == 1),
+                        stop=(a == PASSES - 1),
                     )
             for t in range(PACK):
-                one = slice(t, t + 1)
-                if on_vector[t]:
-                    nc.scalar.activation(lhs[:, t, :], acc[t], ACT.Copy, scale=gain[:, h, one])
+                place = slice(PACK * h + t, PACK * h + t + 1)
+                if clamp_on_vector:
+                    nc.scalar.activation(minuend[:, t, :], acc[t], ACT.Copy, scale=gain[:, place])
                     nc.vector.tensor_scalar(
-                        rhs[:, t, :], lhs[:, t, :], neg_cut[:, h, one], cut[:, h, one], ALU.max, ALU.min
+                        subtrahend[:, t, :], minuend[:, t, :], neg_cut[:, place], cut[:, place], ALU.max, ALU.min
                     )
                 else:
-                    nc.scalar.activation(
-                        lhs[:, t, :], acc[t], ACT.Relu, bias=neg_cut[:, h, one], scale=gain[:, h, one]
-                    )
-                    nc.scalar.activation(
-                        rhs[:, t, :], acc[t], ACT.Relu, bias=neg_cut[:, h, one], scale=neg_gain[:, h, one]
-                    )
+                    for part, scale in ((minuend, gain), (subtrahend, neg_gain)):
+                        nc.scalar.activation(
+                            part[:, t, :], acc[t], ACT.Relu, bias=neg_cut[:, place], scale=scale[:, place]
+                        )
             h_bf = work.tile([P, PACK * width], BF16, name="h_bf", align_bytes=64)
-            nc.vector.tensor_tensor(
-                h_bf[:].rearrange("p (c i t) -> p c t i", i=2, t=PACK),
-                lhs[:].rearrange("p t (c i) -> p c t i", i=2),
-                rhs[:].rearrange("p t (c i) -> p c t i", i=2),
-                ALU.subtract,
-            )
+            h_rows = work.tile([P, PACK, width], BF16, name="h_rows")
+            nc.vector.tensor_tensor(h_rows[:], minuend[:], subtrahend[:], ALU.subtract)
+            interleave(h_bf, h_rows, 4)
             h_codes = work.tile([P, width], U32, name="h_codes", bufs=3, align_bytes=64)
             h_sc = work.tile([P, width], U8, name="h_sc", bufs=3, align_bytes=64)
             nc.vector.quantize_mx(h_codes[:].bitcast(FP8X4), h_sc[:], h_bf[:])
@@ -248,45 +258,43 @@ def tile_list_sparse_code_synthesis_kernel(
                     rhs=h_codes[:].bitcast(FP8X4),
                     rhs_scale=h_sc[:],
                     start=False,
-                    stop=(h == 1 and t % per_bank == per_bank - 1),
+                    stop=(h == PASSES - 1 and t % per_bank == per_bank - 1),
                 )
 
-        def finish(acc, j0, width, on_vector, round_y):
+        def finish(acc, j0, width):
+            last = j0 + width == S2
             y = work.tile([P, PACK, width], F32, name="y")
             for t in range(PACK):
-                if on_vector[t]:
+                if last and t >= 2:
                     nc.vector.tensor_scalar(y[:, t, :], acc[t], bias[:, t : t + 1], None, ALU.add)
                 else:
                     nc.scalar.activation(y[:, t, :], acc[t], ACT.Identity, bias=bias[:, t : t + 1])
                 if t % 2 == 1:
                     nc.sync.dma_start(y_rows[:, t - 1 : t + 1, j0 : j0 + width], y[:, t - 1 : t + 1, :])
             y_bf = work.tile([P, PACK * width], BF16, name="y_bf", align_bytes=64)
-            round_y(
-                y_bf[:].rearrange("p (c i t) -> p c t i", i=2, t=PACK),
-                y[:].rearrange("p t (c i) -> p c t i", i=2),
-            )
+            interleave(y_bf, y, 2)
             y_codes = work.tile([P, width], U32, name="y_codes", align_bytes=64)
             nc.vector.quantize_mx(y_codes[:].bitcast(FP8X4), y_sc[:, j0 : j0 + width], y_bf[:])
             nc.sync.dma_start(y_words[:, j0 : j0 + width], y_codes[:].bitcast(I32))
 
-        j0 = 0
-        pending = None
-        for n, width in enumerate(CHUNKS):
-            first = codes_of(j0, width, 0, CLAMP_ON_VECTOR[2 * n])
-            if pending is None:
-                acc = open_y(j0, width)
-                quantise_w(0)
-                add_codes(acc, width, 0, *first)
-                second = codes_of(j0, width, 1, CLAMP_ON_VECTOR[2 * n + 1])
-                quantise_w(1)
-            else:
-                second = codes_of(j0, width, 1, CLAMP_ON_VECTOR[2 * n + 1])
-                finish(*pending)
-                acc = open_y(j0, width)
-                add_codes(acc, width, 0, *first)
+        width = CHUNKS[0]
+        first = quantised_h(0, width, 0)
+        acc = open_y(0, width)
+        quantise_w(0)
+        add_codes(acc, width, 0, *first)
+        second = quantised_h(0, width, 1)
+        quantise_w(1)
+        add_codes(acc, width, 1, *second)
+        pending = (acc, 0, width)
+        j0 = width
+        for width in CHUNKS[1:]:
+            first = quantised_h(j0, width, 0)
+            second = quantised_h(j0, width, 1)
+            finish(*pending)
+            acc = open_y(j0, width)
+            add_codes(acc, width, 0, *first)
             add_codes(acc, width, 1, *second)
-            last = n == len(CHUNKS) - 1
-            pending = (acc, j0, width, Y_ON_VECTOR[n], nc.vector.tensor_copy if last else nc.scalar.copy)
+            pending = (acc, j0, width)
             j0 = j0 + width
         finish(*pending)
         for q in range(4):

@@ -50,48 +50,44 @@ def tile_list_sparse_code_synthesis_kernel(
         ident = keep.tile([P, P], F32, name="ident")
         places = PASSES * PACK
         nc.gpsimd.memset(by_place[:], 0.0)
+        make_identity(nc, ident[:])
         for k, vec in enumerate((lam, g)):
             nc.gpsimd.dma_start(
                 by_place[places * k : places * (k + 1), :].rearrange("s (u q) -> s u q", q=BLOCK_P),
                 vec.rearrange("(u s q) -> s u q", s=places, q=BLOCK_P),
             )
-        make_identity(nc, ident[:])
         nc.gpsimd.dma_start(bias[:], b.rearrange("(p t) -> p t", t=PACK))
 
-        v2s_table = keep.tile([P, T2], U8, name="v2s_table", tag="slot_a", align_bytes=64)
-        vs_table = keep.tile([P, T], U8, name="vs_table", tag="slot_c", align_bytes=64)
+        vs_table = keep.tile([P, T], U8, name="vs_table", tag="slot_b", align_bytes=64)
+        v2s_table = keep.tile([P, T2], U8, name="v2s_table", align_bytes=64)
         w4s_raw = keep.tile([P, PASSES * N], U8, name="w4s_raw", align_bytes=64)
+        v2s = keep.tile([P, S2], U8, name="v2s", align_bytes=64)
         v2s_pass1 = keep.tile([P, S2], U8, name="v2s_pass1", align_bytes=64)
-        vs_pass1 = keep.tile([P, S], U8, name="vs_pass1", align_bytes=64)
-        for plane in (v2s_table, vs_table, w4s_raw, v2s_pass1, vs_pass1):
-            nc.vector.memset(plane[:].bitcast(I32), 0)
+        vs_placed = keep.tile([P, S], U8, name="vs_placed", align_bytes=64)
+        for plane in (w4s_raw, v2s_pass1):
+            nc.gpsimd.memset(plane[:].bitcast(I32), 0)
 
         def load_words(table, words):
             nc.sync.dma_start(table[:], words.rearrange("p t i -> p (t i)").bitcast(I32))
 
-        w4_raw = keep.tile([P, PASSES, 2 * N], U8, name="w4_raw", tag="slot_e", align_bytes=64)
-        nc.sync.dma_start(w4_raw[:].bitcast(I32), w4_words.rearrange("a p c -> p a c").bitcast(I32))
-        v_table = [keep.tile([P, T], I32, name="v_table0", tag="slot_b", align_bytes=64)]
-        load_words(v_table[0], tab_words[0])
-        for table, first, scales in ((v2s_table, 0, tab2_scales), (vs_table, V_ROW, tab_scales)):
-            scale_rows = scales.rearrange("a (q r) t -> r q a t", r=4)
-            for r in range(4):
-                nc.scalar.dma_start(table[first + r : P : PASS_SHIFT, :].bitcast(I32), scale_rows[r].bitcast(I32))
+        for table, scales in ((vs_table, tab_scales), (v2s_table, tab2_scales)):
+            nc.sync.dma_start(table[0:32, :].bitcast(I32), scales.rearrange("a q t -> q a t").bitcast(I32))
+        for table in (vs_table, v2s_table):
+            nc.vector.memset(table[32:64, :].bitcast(I32), 0)
+            nc.vector.memset(table[64:P, :].bitcast(I32), 0)
+        v_table = [
+            keep.tile([P, T], I32, name="v_table0", tag="slot_c", align_bytes=64),
+            keep.tile([P, T], I32, name="v_table1", tag="slot_d", align_bytes=64),
+        ]
+        for a in range(PASSES):
+            load_words(v_table[a], tab_words[a])
+        v2_table = [keep.tile([P, T2], I32, name="v2_table0", tag="slot_a", align_bytes=64)]
+        load_words(v2_table[0], tab2_words[0])
         for q in range(4):
-            nc.scalar.dma_start(
+            nc.gpsimd.dma_start(
                 w4s_raw[32 * q : 32 * q + 4, :].bitcast(I32).rearrange("r (a c) -> r a c", a=PASSES),
                 w4_scales[:, 4 * q : 4 * q + 4, :].rearrange("a r c -> r a c").bitcast(I32),
             )
-
-        w4_codes = keep.tile([P, PASSES, 2 * N], U8, name="w4_codes", align_bytes=64)
-        w4_sc = keep.tile([P, PASSES * N], U8, name="w4_sc", align_bytes=64)
-        nc.vector.tensor_copy(
-            w4_codes[:].rearrange("p a (t m e) -> p a t m e", t=PACK, e=2),
-            w4_raw[:].rearrange("p a (m t e) -> p a t m e", t=PACK, e=2),
-        )
-
-        v2_table = [keep.tile([P, T2], I32, name="v2_table0", tag="slot_e", align_bytes=64)]
-        load_words(v2_table[0], tab2_words[0])
 
         turned = psum.tile([P, BANK], F32, name="a_bank")
         nc.tensor.transpose(turned[:, 0:P], by_place[:], ident[:])
@@ -106,8 +102,8 @@ def tile_list_sparse_code_synthesis_kernel(
         nc.scalar.activation(neg_cut[:], cut[:], ACT.Copy, scale=-1.0)
         nc.scalar.activation(neg_gain[:], gain, ACT.Copy, scale=-1.0)
 
-        v_codes = [keep.tile([P, S], U32, name="v_codes0", align_bytes=64)]
-        v2_codes = []
+        v_codes = [keep.tile([P, S], U32, name="v_codes%d" % a, align_bytes=64) for a in range(PASSES)]
+        v2_codes = [keep.tile([P, S2], U32, name="v2_codes%d" % a, align_bytes=64) for a in range(PASSES)]
 
         def gather_v(a):
             nc.vector.tensor_copy(
@@ -121,40 +117,46 @@ def tile_list_sparse_code_synthesis_kernel(
                 v2_table[a][:].bitcast(U32).indirect(idx2[:, j0 // LIST_ROWS : j1 // LIST_ROWS]),
             )
 
-        def shift_pass1(plane, gathered):
-            nc.scalar.dma_start(plane[0 : P - PASS_SHIFT, :].bitcast(I32), gathered[PASS_SHIFT:P, :].bitcast(I32))
+        def place_rows(queue, plane, rows):
+            for r in range(4):
+                queue.dma_start(plane[r:P:4, :].bitcast(I32), rows[2 * r : 2 * r + 32, :].bitcast(I32))
 
-        gather_v(0)
-        v_table.append(keep.tile([P, T], I32, name="v_table1", tag="slot_b", align_bytes=64))
-        load_words(v_table[1], tab_words[1])
-        v2s = keep.tile([P, S2], U8, name="v2s", align_bytes=64)
-        nc.vector.tensor_copy(v2s[:], v2s_table[:].indirect(idx2[:]))
-        shift_pass1(v2s_pass1, v2s)
-        v2_table.append(keep.tile([P, T2], I32, name="v2_table1", tag="slot_a", align_bytes=64))
-        load_words(v2_table[1], tab2_words[1])
-        vs_listed = keep.tile([P, S], U8, name="vs_listed", tag="slot_d", align_bytes=64)
+        vs_listed = keep.tile([P, S], U8, name="vs_listed", align_bytes=64)
         vs = keep.tile([P, S], U8, name="vs", align_bytes=64)
         nc.vector.tensor_copy(vs_listed[:], vs_table[:].indirect(idx[:]))
+        place_rows(nc.sync, vs_placed, vs_listed)
+        v2_table.append(keep.tile([P, T2], I32, name="v2_table1", tag="slot_b", align_bytes=64))
+        load_words(v2_table[1], tab2_words[1])
+        v2s_listed = keep.tile([P, S2], U8, name="v2s_listed", align_bytes=64)
+        nc.vector.tensor_copy(v2s_listed[:], v2s_table[:].indirect(idx2[:]))
+        place_rows(nc.sync, v2s, v2s_listed)
+        gather_v(0)
+        w4_raw = keep.tile([P, PASSES, 2 * N], U8, name="w4_raw", tag="slot_c", align_bytes=64)
+        nc.sync.dma_start(w4_raw[:].bitcast(I32), w4_words.rearrange("a p c -> p a c").bitcast(I32))
+        nc.sync.dma_start(v2s_pass1[0 : P - 16, :].bitcast(I32), v2s[4 : P - 12, :].bitcast(I32))
+        gather_v(1)
         nc.vector.tensor_copy(
             vs[:].bitcast(I32).rearrange("p (s u e) -> p s u e", s=places, e=2),
-            vs_listed[:].bitcast(I32).rearrange("p (u s e) -> p s u e", s=places, e=2),
+            vs_placed[:].bitcast(I32).rearrange("p (u s e) -> p s u e", s=places, e=2),
         )
-        shift_pass1(vs_pass1, vs)
-        v2_codes.append(keep.tile([P, S2], U32, name="v2_codes0", tag="slot_d", align_bytes=64))
         gather_v2(0, 0, S2)
-        v_codes.append(keep.tile([P, S], U32, name="v_codes1", tag="slot_c", align_bytes=64))
-        gather_v(1)
+        gather_v2(1, 0, S2 // 2)
+        gather_v2(1, S2 // 2, S2)
+
+        w4_codes = keep.tile([P, PASSES, 2 * N], U8, name="w4_codes", align_bytes=64)
+        w4_sc = keep.tile([P, PASSES * N], U8, name="w4_sc", tag="slot_b", align_bytes=64)
+        nc.vector.tensor_copy(
+            w4_codes[:].rearrange("p a (t m e) -> p a t m e", t=PACK, e=2),
+            w4_raw[:].rearrange("p a (m t e) -> p a t m e", t=PACK, e=2),
+        )
         nc.vector.tensor_copy(
             w4_sc[:].rearrange("p (a t m) -> p a t m", t=PACK, m=P),
             w4s_raw[:].rearrange("p (a m t) -> p a t m", t=PACK, m=P),
         )
-        v2_codes.append(keep.tile([P, S2], U32, name="v2_codes1", align_bytes=64))
-        gather_v2(1, 0, S2 // 2)
-        gather_v2(1, S2 // 2, S2)
 
         w_raw = [
-            keep.tile([P, PACK, N], F32, name="w_raw0", tag="slot_e", align_bytes=64),
-            keep.tile([P, PACK, N], F32, name="w_raw1", tag="slot_b", align_bytes=64),
+            keep.tile([P, PACK, N], F32, name="w_raw0", tag="slot_d", align_bytes=64)[:],
+            keep.tile([P, PACK, N], F32, name="w_raw1", tag="slot_a", align_bytes=64)[:],
         ]
         w_rows = w.rearrange("(u h t q) n -> h t u q n", h=PASSES, t=PACK, q=BLOCK_P)
         for h in range(PASSES):
@@ -162,17 +164,20 @@ def tile_list_sparse_code_synthesis_kernel(
                 nc.sync.dma_start(w_raw[h][:, t, :], w_rows[h, t])
         w_codes = [keep.tile([P, N], U32, name="w_codes%d" % h, align_bytes=64) for h in range(PASSES)]
         w_sc = [keep.tile([P, N], U8, name="w_sc%d" % h, align_bytes=64) for h in range(PASSES)]
+        w_bf = [keep.tile([P, PACK * N], BF16, name="w_bf%d" % h, align_bytes=64) for h in range(PASSES)]
+
+        def round_w(h):
+            nc.scalar.copy(
+                w_bf[h][:].rearrange("p (c m t) -> p m t c", c=PACK, t=PACK),
+                w_raw[h].rearrange("p t (m c) -> p m t c", c=PACK),
+            )
 
         def quantise_w(h):
-            w_bf = keep.tile([P, PACK * N], BF16, name="w_bf", tag="slot_a", align_bytes=64)
-            dealt = w_bf[:].rearrange("p (c m t) -> p m t c", c=PACK, t=PACK)
-            loaded = w_raw[h][:].rearrange("p t (m c) -> p m t c", c=PACK)
-            for c in (0, 2):
-                nc.vector.tensor_copy(dealt[:, :, :, c : c + 2], loaded[:, :, :, c : c + 2])
-            nc.vector.quantize_mx(w_codes[h][:].bitcast(FP8X4), w_sc[h][:], w_bf[:])
+            nc.vector.quantize_mx(w_codes[h][:].bitcast(FP8X4), w_sc[h][:], w_bf[h][:])
 
-        v_planes = [vs, vs_pass1]
         v2_planes = [v2s, v2s_pass1]
+        h_codes = [keep.tile([P, S2], U32, name="h_codes%d" % h, align_bytes=64) for h in range(PASSES)]
+        h_sc = [keep.tile([P, S2], U8, name="h_sc%d" % h, align_bytes=64) for h in range(PASSES)]
         y_sc = keep.tile([P, S2], U8, name="y_sc", align_bytes=64)
         y_rows = out_0.rearrange("(p t) j -> p t j", t=PACK)
         y_words = out_1[0].rearrange("p m t -> p (m t)").bitcast(I32)
@@ -185,11 +190,11 @@ def tile_list_sparse_code_synthesis_kernel(
                 results.extend([bank[:, width * s : width * (s + 1)] for s in range(per_bank)])
             return results
 
-        def interleave(words, rows, run):
-            nc.vector.tensor_copy(
-                words[:].rearrange("p (c i t) -> p c t i", i=run, t=PACK),
-                rows[:].rearrange("p t (c i) -> p c t i", i=run),
-            )
+        def as_words(words):
+            return words[:].rearrange("p (c i t) -> p c t i", i=2, t=PACK)
+
+        def as_rows(rows):
+            return rows[:].rearrange("p t (c i) -> p c t i", i=2)
 
         def open_y(j0, width):
             acc = psum_results("y_bank", width)
@@ -209,10 +214,9 @@ def tile_list_sparse_code_synthesis_kernel(
                         )
             return acc
 
-        def quantised_h(j0, width, h):
-            clamp_on_vector = j0 == 0 and h == 0
+        def threshold_parts(j0, width, h, two_relus):
             acc = psum_results("a_bank", width)
-            dtype = F32 if clamp_on_vector else BF16
+            dtype = BF16 if two_relus else F32
             minuend = work.tile([P, PACK, width], dtype, name="minuend", bufs=3)
             subtrahend = work.tile([P, PACK, width], dtype, name="subtrahend", bufs=3)
             for t in range(PACK):
@@ -221,82 +225,121 @@ def tile_list_sparse_code_synthesis_kernel(
                     nc.tensor.matmul_mx(
                         acc[t],
                         lhsT=v_codes[a][:, cols].bitcast(FP8X4),
-                        lhsT_scale=v_planes[a][V_ROW:P, cols],
+                        lhsT_scale=vs[4 * a : P, cols],
                         rhs=v2_codes[a][:, j0 : j0 + width].bitcast(FP8X4),
-                        rhs_scale=v2_planes[a][:, j0 : j0 + width],
+                        rhs_scale=v2s[4 * a : P, j0 : j0 + width],
                         start=(a == 0),
                         stop=(a == PASSES - 1),
                     )
             for t in range(PACK):
                 place = slice(PACK * h + t, PACK * h + t + 1)
-                if clamp_on_vector:
-                    nc.scalar.activation(minuend[:, t, :], acc[t], ACT.Copy, scale=gain[:, place])
-                    nc.vector.tensor_scalar(
-                        subtrahend[:, t, :], minuend[:, t, :], neg_cut[:, place], cut[:, place], ALU.max, ALU.min
-                    )
-                else:
+                if two_relus:
                     for part, scale in ((minuend, gain), (subtrahend, neg_gain)):
                         nc.scalar.activation(
                             part[:, t, :], acc[t], ACT.Relu, bias=neg_cut[:, place], scale=scale[:, place]
                         )
-            h_bf = work.tile([P, PACK * width], BF16, name="h_bf", align_bytes=64)
-            h_rows = work.tile([P, PACK, width], BF16, name="h_rows")
-            nc.vector.tensor_tensor(h_rows[:], minuend[:], subtrahend[:], ALU.subtract)
-            interleave(h_bf, h_rows, 4)
-            h_codes = work.tile([P, width], U32, name="h_codes", bufs=3, align_bytes=64)
-            h_sc = work.tile([P, width], U8, name="h_sc", bufs=3, align_bytes=64)
-            nc.vector.quantize_mx(h_codes[:].bitcast(FP8X4), h_sc[:], h_bf[:])
-            return h_codes, h_sc
+                else:
+                    nc.scalar.activation(minuend[:, t, :], acc[t], ACT.Copy, scale=gain[:, place])
+                    nc.vector.tensor_scalar(
+                        subtrahend[:, t, :], minuend[:, t, :], neg_cut[:, place], cut[:, place], ALU.max, ALU.min
+                    )
+            return minuend, subtrahend
 
-        def add_codes(acc, width, h, h_codes, h_sc):
-            per_bank = BANK // width
+        def subtract(width, minuend, subtrahend):
+            h_bf = work.tile([P, PACK * width], BF16, name="h_bf", bufs=3, align_bytes=64)
+            nc.vector.tensor_tensor(as_words(h_bf), as_rows(minuend), as_rows(subtrahend), ALU.subtract)
+            return h_bf
+
+        def quantise_h(j0, width, h, h_bf):
+            nc.vector.quantize_mx(h_codes[h][:, j0 : j0 + width].bitcast(FP8X4), h_sc[h][:, j0 : j0 + width], h_bf[:])
+
+        def add_codes(acc, y0, y_width, j0, width, h):
+            per_bank = BANK // y_width
+            last = h == PASSES - 1 and j0 + width == y0 + y_width
             for t in range(PACK):
                 nc.tensor.matmul_mx(
-                    acc[t],
+                    acc[t][:, j0 - y0 : j0 - y0 + width],
                     lhsT=w_codes[h][:, P * t : P * (t + 1)].bitcast(FP8X4),
                     lhsT_scale=w_sc[h][:, P * t : P * (t + 1)],
-                    rhs=h_codes[:].bitcast(FP8X4),
-                    rhs_scale=h_sc[:],
+                    rhs=h_codes[h][:, j0 : j0 + width].bitcast(FP8X4),
+                    rhs_scale=h_sc[h][:, j0 : j0 + width],
                     start=False,
-                    stop=(h == PASSES - 1 and t % per_bank == per_bank - 1),
+                    stop=(last and t % per_bank == per_bank - 1),
                 )
 
-        def finish(acc, j0, width):
-            last = j0 + width == S2
-            y = work.tile([P, PACK, width], F32, name="y")
+        def add_bias(acc, j0, width, shared):
+            y = work.tile([P, PACK, width], F32, name="y", bufs=3)
             for t in range(PACK):
-                if last and t >= 2:
+                if shared and t >= 2:
                     nc.vector.tensor_scalar(y[:, t, :], acc[t], bias[:, t : t + 1], None, ALU.add)
                 else:
                     nc.scalar.activation(y[:, t, :], acc[t], ACT.Identity, bias=bias[:, t : t + 1])
                 if t % 2 == 1:
                     nc.sync.dma_start(y_rows[:, t - 1 : t + 1, j0 : j0 + width], y[:, t - 1 : t + 1, :])
-            y_bf = work.tile([P, PACK * width], BF16, name="y_bf", align_bytes=64)
-            interleave(y_bf, y, 2)
-            y_codes = work.tile([P, width], U32, name="y_codes", align_bytes=64)
+            return y
+
+        def round_y(y, width, on_scalar):
+            y_bf = work.tile([P, PACK * width], BF16, name="y_bf", bufs=3, align_bytes=64)
+            if on_scalar:
+                nc.scalar.copy(as_words(y_bf), as_rows(y))
+            else:
+                nc.vector.tensor_copy(as_words(y_bf), as_rows(y))
+            return y_bf
+
+        def quantise_y(y_bf, j0, width):
+            y_codes = work.tile([P, width], U32, name="y_codes", bufs=3, align_bytes=64)
             nc.vector.quantize_mx(y_codes[:].bitcast(FP8X4), y_sc[:, j0 : j0 + width], y_bf[:])
             nc.sync.dma_start(y_words[:, j0 : j0 + width], y_codes[:].bitcast(I32))
 
-        width = CHUNKS[0]
-        first = quantised_h(0, width, 0)
-        acc = open_y(0, width)
+        W = 256
+        g0 = threshold_parts(0, W, 0, False)
+        acc0 = open_y(0, 512)
+        h0 = subtract(W, *g0)
+        g1 = threshold_parts(0, W, 1, False)
+        round_w(0)
+        quantise_h(0, W, 0, h0)
+        h1 = subtract(W, *g1)
+        g2 = threshold_parts(256, W, 0, False)
+        round_w(1)
+        quantise_h(0, W, 1, h1)
+        h2 = subtract(W, *g2)
         quantise_w(0)
-        add_codes(acc, width, 0, *first)
-        second = quantised_h(0, width, 1)
+        add_codes(acc0, 0, 512, 0, W, 0)
+        g3 = threshold_parts(256, W, 1, False)
+        quantise_h(256, W, 0, h2)
+        add_codes(acc0, 0, 512, 256, W, 0)
+        h3 = subtract(W, *g3)
         quantise_w(1)
-        add_codes(acc, width, 1, *second)
-        pending = (acc, 0, width)
-        j0 = width
-        for width in CHUNKS[1:]:
-            first = quantised_h(j0, width, 0)
-            second = quantised_h(j0, width, 1)
-            finish(*pending)
-            acc = open_y(j0, width)
-            add_codes(acc, width, 0, *first)
-            add_codes(acc, width, 1, *second)
-            pending = (acc, j0, width)
-            j0 = j0 + width
-        finish(*pending)
+        add_codes(acc0, 0, 512, 0, W, 1)
+        g4 = threshold_parts(512, W, 0, False)
+        quantise_h(256, W, 1, h3)
+        add_codes(acc0, 0, 512, 256, W, 1)
+        h4 = subtract(W, *g4)
+        g5 = threshold_parts(512, W, 1, False)
+        y0 = add_bias(acc0, 0, 512, False)
+        acc1 = open_y(512, W)
+        acc2 = open_y(768, W)
+        quantise_h(512, W, 0, h4)
+        add_codes(acc1, 512, W, 512, W, 0)
+        h5 = subtract(W, *g5)
+        g6 = threshold_parts(768, W, 0, False)
+        b0 = round_y(y0, 512, True)
+        quantise_h(512, W, 1, h5)
+        add_codes(acc1, 512, W, 512, W, 1)
+        h6 = subtract(W, *g6)
+        g7 = threshold_parts(768, W, 1, False)
+        y1 = add_bias(acc1, 512, W, False)
+        quantise_h(768, W, 0, h6)
+        add_codes(acc2, 768, W, 768, W, 0)
+        h7 = subtract(W, *g7)
+        quantise_y(b0, 0, 512)
+        quantise_h(768, W, 1, h7)
+        add_codes(acc2, 768, W, 768, W, 1)
+        b1 = round_y(y1, W, False)
+        y2 = add_bias(acc2, 768, W, True)
+        quantise_y(b1, 512, W)
+        b2 = round_y(y2, W, False)
+        quantise_y(b2, 768, W)
         for q in range(4):
             (nc.sync if q % 2 == 0 else nc.scalar).dma_start(
                 out_2[0, 4 * q : 4 * q + 4, :].bitcast(I32), y_sc[32 * q : 32 * q + 4, :].bitcast(I32)

@@ -60,12 +60,10 @@ def tile_list_sparse_code_synthesis_kernel(
 
         vs_table = keep.tile([P, T], U8, name="vs_table", tag="slot_b", align_bytes=64)
         v2s_table = keep.tile([P, T2], U8, name="v2s_table", align_bytes=64)
-        w4s_raw = keep.tile([P, PASSES * N], U8, name="w4s_raw", align_bytes=64)
         v2s = keep.tile([P, S2], U8, name="v2s", align_bytes=64)
         v2s_pass1 = keep.tile([P, S2], U8, name="v2s_pass1", align_bytes=64)
         vs_placed = keep.tile([P, S], U8, name="vs_placed", align_bytes=64)
-        for plane in (w4s_raw, v2s_pass1):
-            nc.gpsimd.memset(plane[:].bitcast(I32), 0)
+        nc.gpsimd.memset(v2s_pass1[:].bitcast(I32), 0)
 
         def load_words(table, words):
             nc.sync.dma_start(table[:], words.rearrange("p t i -> p (t i)").bitcast(I32))
@@ -83,11 +81,6 @@ def tile_list_sparse_code_synthesis_kernel(
             load_words(v_table[a], tab_words[a])
         v2_table = [keep.tile([P, T2], I32, name="v2_table0", tag="slot_a", align_bytes=64)]
         load_words(v2_table[0], tab2_words[0])
-        for q in range(4):
-            nc.gpsimd.dma_start(
-                w4s_raw[32 * q : 32 * q + 4, :].bitcast(I32).rearrange("r (a c) -> r a c", a=PASSES),
-                w4_scales[:, 4 * q : 4 * q + 4, :].rearrange("a r c -> r a c").bitcast(I32),
-            )
 
         turned = psum.tile([P, BANK], F32, name="a_bank")
         nc.tensor.transpose(turned[:, 0:P], by_place[:], ident[:])
@@ -139,12 +132,18 @@ def tile_list_sparse_code_synthesis_kernel(
             vs[:].bitcast(I32).rearrange("p (s u e) -> p s u e", s=places, e=2),
             vs_placed[:].bitcast(I32).rearrange("p (u s e) -> p s u e", s=places, e=2),
         )
+        w4s_raw = vs_placed
+        for q in range(4):
+            nc.sync.dma_start(
+                w4s_raw[32 * q : 32 * q + 4, :].bitcast(I32).rearrange("r (a c) -> r a c", a=PASSES),
+                w4_scales[:, 4 * q : 4 * q + 4, :].rearrange("a r c -> r a c").bitcast(I32),
+            )
         gather_v2(0, 0, S2)
         gather_v2(1, 0, S2 // 2)
         gather_v2(1, S2 // 2, S2)
 
         w4_codes = keep.tile([P, PASSES, 2 * N], U8, name="w4_codes", align_bytes=64)
-        w4_sc = keep.tile([P, PASSES * N], U8, name="w4_sc", tag="slot_b", align_bytes=64)
+        w4_sc = keep.tile([P, PASSES * N], U8, name="w4_sc", align_bytes=64)
         nc.vector.tensor_copy(
             w4_codes[:].rearrange("p a (t m e) -> p a t m e", t=PACK, e=2),
             w4_raw[:].rearrange("p a (m t e) -> p a t m e", t=PACK, e=2),
@@ -155,8 +154,8 @@ def tile_list_sparse_code_synthesis_kernel(
         )
 
         w_raw = [
-            keep.tile([P, PACK, N], F32, name="w_raw0", tag="slot_d", align_bytes=64)[:],
-            keep.tile([P, PACK, N], F32, name="w_raw1", tag="slot_a", align_bytes=64)[:],
+            keep.tile([P, PACK, N], F32, name="w_raw0", tag="slot_a", align_bytes=64)[:],
+            keep.tile([P, PACK, N], F32, name="w_raw1", tag="slot_b", align_bytes=64)[:],
         ]
         w_rows = w.rearrange("(u h t q) n -> h t u q n", h=PASSES, t=PACK, q=BLOCK_P)
         for h in range(PASSES):
@@ -292,46 +291,35 @@ def tile_list_sparse_code_synthesis_kernel(
             nc.sync.dma_start(y_words[:, j0 : j0 + width], y_codes[:].bitcast(I32))
 
         W = 256
-        g0 = threshold_parts(0, W, 0, False)
+        g0 = threshold_parts(0, 512, 0, False)
         acc0 = open_y(0, 512)
-        h0 = subtract(W, *g0)
-        g1 = threshold_parts(0, W, 1, False)
+        h0 = subtract(512, *g0)
+        g1 = threshold_parts(0, 512, 1, False)
         round_w(0)
-        quantise_h(0, W, 0, h0)
-        h1 = subtract(W, *g1)
-        g2 = threshold_parts(256, W, 0, False)
         round_w(1)
-        quantise_h(0, W, 1, h1)
-        h2 = subtract(W, *g2)
+        quantise_h(0, 512, 0, h0)
+        h1 = subtract(512, *g1)
         quantise_w(0)
-        add_codes(acc0, 0, 512, 0, W, 0)
-        g3 = threshold_parts(256, W, 1, False)
-        quantise_h(256, W, 0, h2)
-        add_codes(acc0, 0, 512, 256, W, 0)
-        h3 = subtract(W, *g3)
+        add_codes(acc0, 0, 512, 0, 512, 0)
+        g4 = threshold_parts(512, 512, 0, False)
+        quantise_h(0, 512, 1, h1)
         quantise_w(1)
-        add_codes(acc0, 0, 512, 0, W, 1)
-        g4 = threshold_parts(512, W, 0, False)
-        quantise_h(256, W, 1, h3)
-        add_codes(acc0, 0, 512, 256, W, 1)
-        h4 = subtract(W, *g4)
-        g5 = threshold_parts(512, W, 1, False)
+        add_codes(acc0, 0, 512, 0, 512, 1)
+        h4 = subtract(512, *g4)
+        g5 = threshold_parts(512, W, 1, True)
         y0 = add_bias(acc0, 0, 512, False)
         acc1 = open_y(512, W)
         acc2 = open_y(768, W)
-        quantise_h(512, W, 0, h4)
+        quantise_h(512, 512, 0, h4)
         add_codes(acc1, 512, W, 512, W, 0)
+        add_codes(acc2, 768, W, 768, W, 0)
         h5 = subtract(W, *g5)
-        g6 = threshold_parts(768, W, 0, False)
+        g7 = threshold_parts(768, W, 1, True)
         b0 = round_y(y0, 512, True)
         quantise_h(512, W, 1, h5)
         add_codes(acc1, 512, W, 512, W, 1)
-        h6 = subtract(W, *g6)
-        g7 = threshold_parts(768, W, 1, False)
-        y1 = add_bias(acc1, 512, W, False)
-        quantise_h(768, W, 0, h6)
-        add_codes(acc2, 768, W, 768, W, 0)
         h7 = subtract(W, *g7)
+        y1 = add_bias(acc1, 512, W, False)
         quantise_y(b0, 0, 512)
         quantise_h(768, W, 1, h7)
         add_codes(acc2, 768, W, 768, W, 1)

@@ -49,6 +49,8 @@ def tile_list_sparse_code_synthesis_kernel(
         by_place = keep.tile([P, P], F32, name="by_place")
         ident = keep.tile([P, P], F32, name="ident")
         places = PASSES * PACK
+        v2s_table = keep.tile([P, T2], U8, name="v2s_table", tag="slot_a", align_bytes=64)
+        nc.gpsimd.memset(v2s_table[64:P, :].bitcast(I32), 0)
         nc.gpsimd.memset(by_place[:], 0.0)
         make_identity(nc, ident[:])
         for k, vec in enumerate((lam, g)):
@@ -59,7 +61,6 @@ def tile_list_sparse_code_synthesis_kernel(
         nc.gpsimd.dma_start(bias[:], b.rearrange("(p t) -> p t", t=PACK))
 
         vs_table = keep.tile([P, T], U8, name="vs_table", tag="slot_b", align_bytes=64)
-        v2s_table = keep.tile([P, T2], U8, name="v2s_table", align_bytes=64)
         v2s = keep.tile([P, S2], U8, name="v2s", align_bytes=64)
         v2s_pass1 = keep.tile([P, S2], U8, name="v2s_pass1", align_bytes=64)
         vs_placed = keep.tile([P, S], U8, name="vs_placed", align_bytes=64)
@@ -70,17 +71,13 @@ def tile_list_sparse_code_synthesis_kernel(
 
         for table, scales in ((vs_table, tab_scales), (v2s_table, tab2_scales)):
             nc.sync.dma_start(table[0:32, :].bitcast(I32), scales.rearrange("a q t -> q a t").bitcast(I32))
-        for table in (vs_table, v2s_table):
-            nc.vector.memset(table[32:64, :].bitcast(I32), 0)
-            nc.vector.memset(table[64:P, :].bitcast(I32), 0)
-        v_table = [
-            keep.tile([P, T], I32, name="v_table0", tag="slot_c", align_bytes=64),
-            keep.tile([P, T], I32, name="v_table1", tag="slot_d", align_bytes=64),
-        ]
-        for a in range(PASSES):
-            load_words(v_table[a], tab_words[a])
-        v2_table = [keep.tile([P, T2], I32, name="v2_table0", tag="slot_a", align_bytes=64)]
+        nc.vector.memset(vs_table[32:64, :].bitcast(I32), 0)
+        nc.vector.memset(vs_table[64:P, :].bitcast(I32), 0)
+        nc.vector.memset(v2s_table[32:64, :].bitcast(I32), 0)
+        v2_table = [keep.tile([P, T2], I32, name="v2_table0", tag="slot_c", align_bytes=64)]
         load_words(v2_table[0], tab2_words[0])
+        v_table1 = keep.tile([P, T], I32, name="v_table1", tag="slot_d", align_bytes=64)
+        load_words(v_table1, tab_words[1])
 
         turned = psum.tile([P, BANK], F32, name="a_bank")
         nc.tensor.transpose(turned[:, 0:P], by_place[:], ident[:])
@@ -118,15 +115,17 @@ def tile_list_sparse_code_synthesis_kernel(
         vs = keep.tile([P, S], U8, name="vs", align_bytes=64)
         nc.vector.tensor_copy(vs_listed[:], vs_table[:].indirect(idx[:]))
         place_rows(nc.sync, vs_placed, vs_listed)
-        v2_table.append(keep.tile([P, T2], I32, name="v2_table1", tag="slot_b", align_bytes=64))
-        load_words(v2_table[1], tab2_words[1])
+        v_table = [keep.tile([P, T], I32, name="v_table0", tag="slot_b", align_bytes=64), v_table1]
+        load_words(v_table[0], tab_words[0])
         v2s_listed = keep.tile([P, S2], U8, name="v2s_listed", align_bytes=64)
         nc.vector.tensor_copy(v2s_listed[:], v2s_table[:].indirect(idx2[:]))
         place_rows(nc.sync, v2s, v2s_listed)
-        gather_v(0)
+        v2_table.append(keep.tile([P, T2], I32, name="v2_table1", tag="slot_a", align_bytes=64))
+        load_words(v2_table[1], tab2_words[1])
+        nc.sync.dma_start(v2s_pass1[0 : P - 16, :].bitcast(I32), v2s[4 : P - 12, :].bitcast(I32))
+        gather_v2(0, 0, S2)
         w4_raw = keep.tile([P, PASSES, 2 * N], U8, name="w4_raw", tag="slot_c", align_bytes=64)
         nc.sync.dma_start(w4_raw[:].bitcast(I32), w4_words.rearrange("a p c -> p a c").bitcast(I32))
-        nc.sync.dma_start(v2s_pass1[0 : P - 16, :].bitcast(I32), v2s[4 : P - 12, :].bitcast(I32))
         gather_v(1)
         nc.vector.tensor_copy(
             vs[:].bitcast(I32).rearrange("p (s u e) -> p s u e", s=places, e=2),
@@ -138,15 +137,15 @@ def tile_list_sparse_code_synthesis_kernel(
                 w4s_raw[32 * q : 32 * q + 4, :].bitcast(I32).rearrange("r (a c) -> r a c", a=PASSES),
                 w4_scales[:, 4 * q : 4 * q + 4, :].rearrange("a r c -> r a c").bitcast(I32),
             )
-        gather_v2(0, 0, S2)
+        gather_v(0)
         gather_v2(1, 0, S2 // 2)
         gather_v2(1, S2 // 2, S2)
 
         w4_codes = keep.tile([P, PASSES, 2 * N], U8, name="w4_codes", align_bytes=64)
         w4_sc = keep.tile([P, PASSES * N], U8, name="w4_sc", align_bytes=64)
         nc.vector.tensor_copy(
-            w4_codes[:].rearrange("p a (t m e) -> p a t m e", t=PACK, e=2),
-            w4_raw[:].rearrange("p a (m t e) -> p a t m e", t=PACK, e=2),
+            w4_codes[:].bitcast(U16).rearrange("p a (t m) -> p a t m", t=PACK),
+            w4_raw[:].bitcast(U16).rearrange("p a (m t) -> p a t m", t=PACK),
         )
         nc.vector.tensor_copy(
             w4_sc[:].rearrange("p (a t m) -> p a t m", t=PACK, m=P),
@@ -154,8 +153,8 @@ def tile_list_sparse_code_synthesis_kernel(
         )
 
         w_raw = [
-            keep.tile([P, PACK, N], F32, name="w_raw0", tag="slot_a", align_bytes=64)[:],
-            keep.tile([P, PACK, N], F32, name="w_raw1", tag="slot_b", align_bytes=64)[:],
+            keep.tile([P, PACK, N], F32, name="w_raw0", tag="slot_b", align_bytes=64)[:],
+            keep.tile([P, PACK, N], F32, name="w_raw1", tag="slot_a", align_bytes=64)[:],
         ]
         w_rows = w.rearrange("(u h t q) n -> h t u q n", h=PASSES, t=PACK, q=BLOCK_P)
         for h in range(PASSES):
@@ -218,9 +217,12 @@ def tile_list_sparse_code_synthesis_kernel(
             dtype = BF16 if two_relus else F32
             minuend = work.tile([P, PACK, width], dtype, name="minuend", bufs=3)
             subtrahend = work.tile([P, PACK, width], dtype, name="subtrahend", bufs=3)
-            for t in range(PACK):
+            passes = [(t, a) for t in range(PACK) for a in range(PASSES)]
+            if j0 == 0 and h == 0:
+                passes = [(t, a) for a in range(PASSES) for t in range(PACK)]
+            for t, a in passes:
                 cols = slice(PASS * h + P * t, PASS * h + P * (t + 1))
-                for a in range(PASSES):
+                if True:
                     nc.tensor.matmul_mx(
                         acc[t],
                         lhsT=v_codes[a][:, cols].bitcast(FP8X4),
@@ -306,7 +308,7 @@ def tile_list_sparse_code_synthesis_kernel(
         quantise_w(1)
         add_codes(acc0, 0, 512, 0, 512, 1)
         h4 = subtract(512, *g4)
-        g5 = threshold_parts(512, W, 1, True)
+        g5 = threshold_parts(512, W, 1, False)
         y0 = add_bias(acc0, 0, 512, False)
         acc1 = open_y(512, W)
         acc2 = open_y(768, W)
@@ -314,7 +316,7 @@ def tile_list_sparse_code_synthesis_kernel(
         add_codes(acc1, 512, W, 512, W, 0)
         add_codes(acc2, 768, W, 768, W, 0)
         h5 = subtract(W, *g5)
-        g7 = threshold_parts(768, W, 1, True)
+        g7 = threshold_parts(768, W, 1, False)
         b0 = round_y(y0, 512, True)
         quantise_h(512, W, 1, h5)
         add_codes(acc1, 512, W, 512, W, 1)

@@ -50,11 +50,11 @@ def tile_list_sparse_code_synthesis_kernel(
         ident = keep.tile([P, P], F32, name="ident")
         places = PASSES * PACK
         v2s_table = keep.tile([P, T2], U8, name="v2s_table", tag="slot_a", align_bytes=64)
-        nc.gpsimd.memset(v2s_table[64:P, :].bitcast(I32), 0)
         nc.gpsimd.memset(by_place[:], 0.0)
+        nc.gpsimd.memset(v2s_table[64:P, :].bitcast(I32), 0)
         make_identity(nc, ident[:])
         for k, vec in enumerate((lam, g)):
-            nc.gpsimd.dma_start(
+            nc.scalar.dma_start(
                 by_place[places * k : places * (k + 1), :].rearrange("s (u q) -> s u q", q=BLOCK_P),
                 vec.rearrange("(u s q) -> s u q", s=places, q=BLOCK_P),
             )

@@ -189,10 +189,10 @@ def tile_list_sparse_code_synthesis_kernel(
             return results
 
         def as_words(words):
-            return words[:].rearrange("p (c i t) -> p c t i", i=2, t=PACK)
+            return words[:].rearrange("p (c i t) -> p c t i", i=4, t=PACK)
 
         def as_rows(rows):
-            return rows[:].rearrange("p t (c i) -> p c t i", i=2)
+            return rows[:].rearrange("p t (c i) -> p c t i", i=4)
 
         def open_y(j0, width):
             acc = psum_results("y_bank", width)

@@ -166,8 +166,8 @@ def tile_list_sparse_code_synthesis_kernel(
 
         def round_w(h):
             nc.scalar.copy(
-                w_bf[h][:].rearrange("p (c m t) -> p m t c", c=PACK, t=PACK),
-                w_raw[h].rearrange("p t (m c) -> p m t c", c=PACK),
+                w_bf[h][:].rearrange("p (c m e t) -> p m t e c", c=PACK, e=2, t=PACK),
+                w_raw[h].rearrange("p t (m e c) -> p m t e c", c=PACK, e=2),
             )
 
         def quantise_w(h):
@@ -188,11 +188,11 @@ def tile_list_sparse_code_synthesis_kernel(
                 results.extend([bank[:, width * s : width * (s + 1)] for s in range(per_bank)])
             return results
 
-        def as_words(words):
-            return words[:].rearrange("p (c i t) -> p c t i", i=4, t=PACK)
+        def as_words(words, run=4):
+            return words[:].rearrange("p (c i t) -> p c t i", i=run, t=PACK)
 
-        def as_rows(rows):
-            return rows[:].rearrange("p t (c i) -> p c t i", i=4)
+        def as_rows(rows, run=4):
+            return rows[:].rearrange("p t (c i) -> p c t i", i=run)
 
         def open_y(j0, width):
             acc = psum_results("y_bank", width)
@@ -248,7 +248,7 @@ def tile_list_sparse_code_synthesis_kernel(
 
         def subtract(width, minuend, subtrahend):
             h_bf = work.tile([P, PACK * width], BF16, name="h_bf", bufs=3, align_bytes=64)
-            nc.vector.tensor_tensor(as_words(h_bf), as_rows(minuend), as_rows(subtrahend), ALU.subtract)
+            nc.vector.tensor_tensor(as_words(h_bf, 8), as_rows(minuend, 8), as_rows(subtrahend, 8), ALU.subtract)
             return h_bf
 
         def quantise_h(j0, width, h, h_bf):

@@ -21,12 +21,19 @@ P = 128
 PACK = 4
 PASS = P * PACK
 PASSES = 2
+PLACES = PASSES * PACK
 BLOCK_P = 8
+QUADRANT = 32
+QUADRANTS = P // QUADRANT
+PLANE_ROWS = QUADRANT // BLOCK_P
+SCALE_ROWS = PASSES * QUADRANTS * PLANE_ROWS
+SHIFTED = P - 16
 BANK = 512
 LIST_ROWS = 16
-PASS_SHIFT = 16
-V_ROW = 8
-CHUNKS = (256, 512, 256)
+WIDE = BANK
+NARROW = BANK // 2
+COPY_RUN = 4
+SUBTRACT_RUN = 8
 
 
 def tile_list_sparse_code_synthesis_kernel(
@@ -37,109 +44,112 @@ def tile_list_sparse_code_synthesis_kernel(
     with ExitStack() as ctx:
         lists = ctx.enter_context(tc.tile_pool(name="lists", bufs=1))
         keep = ctx.enter_context(tc.tile_pool(name="keep", bufs=1))
-        work = ctx.enter_context(tc.tile_pool(name="work", bufs=2))
+        work = ctx.enter_context(tc.tile_pool(name="work", bufs=3))
         psum = ctx.enter_context(tc.psum_pool(name="psum", bufs=4))
 
-        idx2 = lists.tile([P, S2 // LIST_ROWS], U16, name="idx2")
-        idx = lists.tile([P, S // LIST_ROWS], U16, name="idx")
-        nc.sync.dma_start(idx2[:], offs2)
-        nc.sync.dma_start(idx[:], offs)
-
-        bias = keep.tile([P, PACK], F32, name="bias")
-        by_place = keep.tile([P, P], F32, name="by_place")
         ident = keep.tile([P, P], F32, name="ident")
-        places = PASSES * PACK
-        v2s_table = keep.tile([P, T2], U8, name="v2s_table", tag="slot_a", align_bytes=64)
-        nc.gpsimd.memset(by_place[:], 0.0)
-        nc.gpsimd.memset(v2s_table[64:P, :].bitcast(I32), 0)
         make_identity(nc, ident[:])
-        for k, vec in enumerate((lam, g)):
-            nc.scalar.dma_start(
-                by_place[places * k : places * (k + 1), :].rearrange("s (u q) -> s u q", q=BLOCK_P),
-                vec.rearrange("(u s q) -> s u q", s=places, q=BLOCK_P),
-            )
-        nc.gpsimd.dma_start(bias[:], b.rearrange("(p t) -> p t", t=PACK))
 
-        vs_table = keep.tile([P, T], U8, name="vs_table", tag="slot_b", align_bytes=64)
-        v2s = keep.tile([P, S2], U8, name="v2s", align_bytes=64)
-        v2s_pass1 = keep.tile([P, S2], U8, name="v2s_pass1", align_bytes=64)
-        vs_placed = keep.tile([P, S], U8, name="vs_placed", align_bytes=64)
-        nc.gpsimd.memset(v2s_pass1[:].bitcast(I32), 0)
+        def load_scale_rows(table, scales):
+            nc.sync.dma_start(table[0:SCALE_ROWS, :].bitcast(I32), scales.rearrange("a q t -> q a t").bitcast(I32))
 
         def load_words(table, words):
             nc.sync.dma_start(table[:], words.rearrange("p t i -> p (t i)").bitcast(I32))
 
-        for table, scales in ((vs_table, tab_scales), (v2s_table, tab2_scales)):
-            nc.sync.dma_start(table[0:32, :].bitcast(I32), scales.rearrange("a q t -> q a t").bitcast(I32))
-        nc.vector.memset(vs_table[32:64, :].bitcast(I32), 0)
-        nc.vector.memset(vs_table[64:P, :].bitcast(I32), 0)
-        nc.vector.memset(v2s_table[32:64, :].bitcast(I32), 0)
-        v2_table = [keep.tile([P, T2], I32, name="v2_table0", tag="slot_c", align_bytes=64)]
-        load_words(v2_table[0], tab2_words[0])
+        idx = lists.tile([P, S // LIST_ROWS], U16, name="idx")
+        idx2 = lists.tile([P, S2 // LIST_ROWS], U16, name="idx2")
+        vs_table = keep.tile([P, T], U8, name="vs_table", tag="slot_b", align_bytes=64)
+        v2s_table = keep.tile([P, T2], U8, name="v2s_table", tag="slot_a", align_bytes=64)
+        nc.sync.dma_start(idx[:], offs)
+        load_scale_rows(vs_table, tab_scales)
+        nc.sync.dma_start(idx2[:], offs2)
+        load_scale_rows(v2s_table, tab2_scales)
+        v2_table0 = keep.tile([P, T2], I32, name="v2_table0", tag="slot_c", align_bytes=64)
+        load_words(v2_table0, tab2_words[0])
         v_table1 = keep.tile([P, T], I32, name="v_table1", tag="slot_d", align_bytes=64)
         load_words(v_table1, tab_words[1])
 
+        by_place = keep.tile([P, P], F32, name="by_place")
+        v2s_pass1 = keep.tile([P, S2], U8, name="v2s_pass1", align_bytes=64)
+        nc.vector.memset(by_place[:], 0.0)
+        for table in (vs_table, v2s_table):
+            nc.vector.memset(table[SCALE_ROWS : P // 2, :].bitcast(I32), 0)
+            nc.vector.memset(table[P // 2 : P, :].bitcast(I32), 0)
+        nc.vector.memset(v2s_pass1[:].bitcast(I32), 0)
+
+        for k, vec in enumerate((lam, g)):
+            nc.scalar.dma_start(
+                by_place[PLACES * k : PLACES * (k + 1), :].rearrange("s (u q) -> s u q", q=BLOCK_P),
+                vec.rearrange("(u s q) -> s u q", s=PLACES, q=BLOCK_P),
+            )
         turned = psum.tile([P, BANK], F32, name="a_bank")
         nc.tensor.transpose(turned[:, 0:P], by_place[:], ident[:])
-        lam_gain = keep.tile([P, 2 * places], F32, name="lam_gain")
-        nc.scalar.copy(lam_gain[:], turned[:, 0 : 2 * places])
-        gain = lam_gain[:, places : 2 * places]
-        cut = keep.tile([P, places], F32, name="cut")
-        neg_cut = keep.tile([P, places], F32, name="neg_cut")
-        neg_gain = keep.tile([P, places], F32, name="neg_gain")
-        for s in range(places):
+        lam_gain = keep.tile([P, 2 * PLACES], F32, name="lam_gain")
+        nc.scalar.copy(lam_gain[:], turned[:, 0 : 2 * PLACES])
+        gain = lam_gain[:, PLACES : 2 * PLACES]
+        cut = keep.tile([P, PLACES], F32, name="cut")
+        neg_cut = keep.tile([P, PLACES], F32, name="neg_cut")
+        for s in range(PLACES):
             nc.scalar.activation(cut[:, s : s + 1], gain[:, s : s + 1], ACT.Abs, scale=lam_gain[:, s : s + 1])
         nc.scalar.activation(neg_cut[:], cut[:], ACT.Copy, scale=-1.0)
-        nc.scalar.activation(neg_gain[:], gain, ACT.Copy, scale=-1.0)
 
         v_codes = [keep.tile([P, S], U32, name="v_codes%d" % a, align_bytes=64) for a in range(PASSES)]
         v2_codes = [keep.tile([P, S2], U32, name="v2_codes%d" % a, align_bytes=64) for a in range(PASSES)]
 
-        def gather_v(a):
+        def gather_v(a, table):
             nc.vector.tensor_copy(
-                v_codes[a][:].rearrange("p (s u q) -> p u s q", s=places, q=BLOCK_P),
-                v_table[a][:].bitcast(U32).indirect(idx[:]),
+                v_codes[a][:].rearrange("p (s u q) -> p u s q", s=PLACES, q=BLOCK_P),
+                table[:].bitcast(U32).indirect(idx[:]),
             )
 
-        def gather_v2(a, j0, j1):
+        def gather_v2(a, table, j0, j1):
             nc.vector.tensor_copy(
                 v2_codes[a][:, j0:j1],
-                v2_table[a][:].bitcast(U32).indirect(idx2[:, j0 // LIST_ROWS : j1 // LIST_ROWS]),
+                table[:].bitcast(U32).indirect(idx2[:, j0 // LIST_ROWS : j1 // LIST_ROWS]),
             )
 
-        def place_rows(queue, plane, rows):
-            for r in range(4):
-                queue.dma_start(plane[r:P:4, :].bitcast(I32), rows[2 * r : 2 * r + 32, :].bitcast(I32))
+        def place_rows(planes, rows):
+            for r in range(PLANE_ROWS):
+                nc.sync.dma_start(
+                    planes[r:P:PLANE_ROWS, :].bitcast(I32), rows[2 * r : 2 * r + SCALE_ROWS, :].bitcast(I32)
+                )
 
         vs_listed = keep.tile([P, S], U8, name="vs_listed", align_bytes=64)
-        vs = keep.tile([P, S], U8, name="vs", align_bytes=64)
+        vs_placed = keep.tile([P, S], U8, name="vs_placed", align_bytes=64)
         nc.vector.tensor_copy(vs_listed[:], vs_table[:].indirect(idx[:]))
-        place_rows(nc.sync, vs_placed, vs_listed)
-        v_table = [keep.tile([P, T], I32, name="v_table0", tag="slot_b", align_bytes=64), v_table1]
-        load_words(v_table[0], tab_words[0])
+        place_rows(vs_placed, vs_listed)
+        v_table0 = keep.tile([P, T], I32, name="v_table0", tag="slot_b", align_bytes=64)
+        load_words(v_table0, tab_words[0])
         v2s_listed = keep.tile([P, S2], U8, name="v2s_listed", align_bytes=64)
+        v2_sc = keep.tile([P, S2], U8, name="v2_sc", align_bytes=64)
         nc.vector.tensor_copy(v2s_listed[:], v2s_table[:].indirect(idx2[:]))
-        place_rows(nc.sync, v2s, v2s_listed)
-        v2_table.append(keep.tile([P, T2], I32, name="v2_table1", tag="slot_a", align_bytes=64))
-        load_words(v2_table[1], tab2_words[1])
-        nc.sync.dma_start(v2s_pass1[0 : P - 16, :].bitcast(I32), v2s[4 : P - 12, :].bitcast(I32))
-        gather_v2(0, 0, S2)
+        place_rows(v2_sc, v2s_listed)
+        v2_table1 = keep.tile([P, T2], I32, name="v2_table1", tag="slot_a", align_bytes=64)
+        load_words(v2_table1, tab2_words[1])
+        nc.sync.dma_start(
+            v2s_pass1[0:SHIFTED, :].bitcast(I32), v2_sc[PLANE_ROWS : PLANE_ROWS + SHIFTED, :].bitcast(I32)
+        )
+
+        gather_v2(0, v2_table0, 0, S2)
         w4_raw = keep.tile([P, PASSES, 2 * N], U8, name="w4_raw", tag="slot_c", align_bytes=64)
         nc.sync.dma_start(w4_raw[:].bitcast(I32), w4_words.rearrange("a p c -> p a c").bitcast(I32))
-        gather_v(1)
+        gather_v(1, v_table1)
+        bias = keep.tile([P, PACK], F32, name="bias", tag="slot_d", align_bytes=64)
+        nc.sync.dma_start(bias[:], b.rearrange("(p t) -> p t", t=PACK))
+        v_sc = keep.tile([P, S], U8, name="v_sc", align_bytes=64)
         nc.vector.tensor_copy(
-            vs[:].bitcast(I32).rearrange("p (s u e) -> p s u e", s=places, e=2),
-            vs_placed[:].bitcast(I32).rearrange("p (u s e) -> p s u e", s=places, e=2),
+            v_sc[:].bitcast(I32).rearrange("p (s u e) -> p s u e", s=PLACES, e=2),
+            vs_placed[:].bitcast(I32).rearrange("p (u s e) -> p s u e", s=PLACES, e=2),
         )
         w4s_raw = vs_placed
-        for q in range(4):
+        for q in range(QUADRANTS):
             nc.sync.dma_start(
-                w4s_raw[32 * q : 32 * q + 4, :].bitcast(I32).rearrange("r (a c) -> r a c", a=PASSES),
-                w4_scales[:, 4 * q : 4 * q + 4, :].rearrange("a r c -> r a c").bitcast(I32),
+                w4s_raw[QUADRANT * q : QUADRANT * q + PLANE_ROWS, :].bitcast(I32).rearrange("r (a c) -> r a c", a=PASSES),
+                w4_scales[:, PLANE_ROWS * q : PLANE_ROWS * (q + 1), :].rearrange("a r c -> r a c").bitcast(I32),
             )
-        gather_v(0)
-        gather_v2(1, 0, S2 // 2)
-        gather_v2(1, S2 // 2, S2)
+        gather_v(0, v_table0)
+        gather_v2(1, v2_table1, 0, WIDE)
+        gather_v2(1, v2_table1, WIDE, S2)
 
         w4_codes = keep.tile([P, PASSES, 2 * N], U8, name="w4_codes", align_bytes=64)
         w4_sc = keep.tile([P, PASSES * N], U8, name="w4_sc", align_bytes=64)
@@ -153,46 +163,81 @@ def tile_list_sparse_code_synthesis_kernel(
         )
 
         w_raw = [
-            keep.tile([P, PACK, N], F32, name="w_raw0", tag="slot_b", align_bytes=64)[:],
-            keep.tile([P, PACK, N], F32, name="w_raw1", tag="slot_a", align_bytes=64)[:],
+            keep.tile([P, PACK, N], F32, name="w_raw0", tag="slot_b", align_bytes=64),
+            keep.tile([P, PACK, N], F32, name="w_raw1", tag="slot_a", align_bytes=64),
         ]
         w_rows = w.rearrange("(u h t q) n -> h t u q n", h=PASSES, t=PACK, q=BLOCK_P)
         for h in range(PASSES):
             for t in range(PACK):
                 nc.sync.dma_start(w_raw[h][:, t, :], w_rows[h, t])
+        w_bf = [keep.tile([P, PACK * N], BF16, name="w_bf%d" % h, align_bytes=64) for h in range(PASSES)]
         w_codes = [keep.tile([P, N], U32, name="w_codes%d" % h, align_bytes=64) for h in range(PASSES)]
         w_sc = [keep.tile([P, N], U8, name="w_sc%d" % h, align_bytes=64) for h in range(PASSES)]
-        w_bf = [keep.tile([P, PACK * N], BF16, name="w_bf%d" % h, align_bytes=64) for h in range(PASSES)]
+        h_codes = [keep.tile([P, S2], U32, name="h_codes%d" % h, align_bytes=64) for h in range(PASSES)]
+        h_sc = [keep.tile([P, S2], U8, name="h_sc%d" % h, align_bytes=64) for h in range(PASSES)]
+        y_sc = keep.tile([P, S2], U8, name="y_sc", align_bytes=64)
+        v2_planes_from_row_0 = [v2_sc, v2s_pass1]
+        y_rows = out_0.rearrange("(p t) j -> p t j", t=PACK)
+        y_words = out_1[0].rearrange("p m t -> p (m t)").bitcast(I32)
 
         def round_w(h):
             nc.scalar.copy(
                 w_bf[h][:].rearrange("p (c m e t) -> p m t e c", c=PACK, e=2, t=PACK),
-                w_raw[h].rearrange("p t (m e c) -> p m t e c", c=PACK, e=2),
+                w_raw[h][:].rearrange("p t (m e c) -> p m t e c", c=PACK, e=2),
             )
 
         def quantise_w(h):
             nc.vector.quantize_mx(w_codes[h][:].bitcast(FP8X4), w_sc[h][:], w_bf[h][:])
-
-        v2_planes = [v2s, v2s_pass1]
-        h_codes = [keep.tile([P, S2], U32, name="h_codes%d" % h, align_bytes=64) for h in range(PASSES)]
-        h_sc = [keep.tile([P, S2], U8, name="h_sc%d" % h, align_bytes=64) for h in range(PASSES)]
-        y_sc = keep.tile([P, S2], U8, name="y_sc", align_bytes=64)
-        y_rows = out_0.rearrange("(p t) j -> p t j", t=PACK)
-        y_words = out_1[0].rearrange("p m t -> p (m t)").bitcast(I32)
 
         def psum_results(tag, width):
             per_bank = BANK // width
             results = []
             for first_t in range(0, PACK, per_bank):
                 bank = psum.tile([P, BANK], F32, name=tag)
-                results.extend([bank[:, width * s : width * (s + 1)] for s in range(per_bank)])
+                results.extend([bank[:, width * x : width * (x + 1)] for x in range(per_bank)])
             return results
 
-        def as_words(words, run=4):
+        def as_words(words, run):
             return words[:].rearrange("p (c i t) -> p c t i", i=run, t=PACK)
 
-        def as_rows(rows, run=4):
+        def as_rows(rows, run):
             return rows[:].rearrange("p t (c i) -> p c t i", i=run)
+
+        def gain_and_clamp(j0, width, h):
+            acc = psum_results("a_bank", width)
+            gained = work.tile([P, PACK, width], F32, name="gained")
+            clamped = work.tile([P, PACK, width], F32, name="clamped")
+            order = [(t, a) for t in range(PACK) for a in range(PASSES)]
+            if j0 == 0 and h == 0:
+                order = [(t, a) for a in range(PASSES) for t in range(PACK)]
+            for t, a in order:
+                cols = slice(PASS * h + P * t, PASS * h + P * (t + 1))
+                nc.tensor.matmul_mx(
+                    acc[t],
+                    lhsT=v_codes[a][:, cols].bitcast(FP8X4),
+                    lhsT_scale=v_sc[PLANE_ROWS * a : P, cols],
+                    rhs=v2_codes[a][:, j0 : j0 + width].bitcast(FP8X4),
+                    rhs_scale=v2_sc[PLANE_ROWS * a : P, j0 : j0 + width],
+                    start=(a == 0),
+                    stop=(a == PASSES - 1),
+                )
+            for t in range(PACK):
+                place = slice(PACK * h + t, PACK * h + t + 1)
+                nc.scalar.activation(gained[:, t, :], acc[t], ACT.Copy, scale=gain[:, place])
+                nc.vector.tensor_scalar(
+                    clamped[:, t, :], gained[:, t, :], neg_cut[:, place], cut[:, place], ALU.max, ALU.min
+                )
+            return gained, clamped
+
+        def subtract(width, gained, clamped):
+            h_bf = work.tile([P, PACK * width], BF16, name="h_bf", align_bytes=64)
+            nc.vector.tensor_tensor(
+                as_words(h_bf, SUBTRACT_RUN), as_rows(gained, SUBTRACT_RUN), as_rows(clamped, SUBTRACT_RUN), ALU.subtract
+            )
+            return h_bf
+
+        def quantise_h(j0, width, h, h_bf):
+            nc.vector.quantize_mx(h_codes[h][:, j0 : j0 + width].bitcast(FP8X4), h_sc[h][:, j0 : j0 + width], h_bf[:])
 
         def open_y(j0, width):
             acc = psum_results("y_bank", width)
@@ -206,72 +251,30 @@ def tile_list_sparse_code_synthesis_kernel(
                             lhsT=w4_codes[:, a, 2 * P * t : 2 * P * (t + 1)].bitcast(FP4X4),
                             lhsT_scale=w4_sc[:, N * a + P * t : N * a + P * (t + 1)],
                             rhs=v2_codes[a][:, j0 + c : j0 + c + step].bitcast(FP8X4),
-                            rhs_scale=v2_planes[a][:, j0 + c : j0 + c + step],
+                            rhs_scale=v2_planes_from_row_0[a][:, j0 + c : j0 + c + step],
                             start=(a == 0 and c == 0 and t % per_bank == 0),
                             stop=False,
                         )
             return acc
 
-        def threshold_parts(j0, width, h, two_relus):
-            acc = psum_results("a_bank", width)
-            dtype = BF16 if two_relus else F32
-            minuend = work.tile([P, PACK, width], dtype, name="minuend", bufs=3)
-            subtrahend = work.tile([P, PACK, width], dtype, name="subtrahend", bufs=3)
-            passes = [(t, a) for t in range(PACK) for a in range(PASSES)]
-            if j0 == 0 and h == 0:
-                passes = [(t, a) for a in range(PASSES) for t in range(PACK)]
-            for t, a in passes:
-                cols = slice(PASS * h + P * t, PASS * h + P * (t + 1))
-                if True:
-                    nc.tensor.matmul_mx(
-                        acc[t],
-                        lhsT=v_codes[a][:, cols].bitcast(FP8X4),
-                        lhsT_scale=vs[4 * a : P, cols],
-                        rhs=v2_codes[a][:, j0 : j0 + width].bitcast(FP8X4),
-                        rhs_scale=v2s[4 * a : P, j0 : j0 + width],
-                        start=(a == 0),
-                        stop=(a == PASSES - 1),
-                    )
-            for t in range(PACK):
-                place = slice(PACK * h + t, PACK * h + t + 1)
-                if two_relus:
-                    for part, scale in ((minuend, gain), (subtrahend, neg_gain)):
-                        nc.scalar.activation(
-                            part[:, t, :], acc[t], ACT.Relu, bias=neg_cut[:, place], scale=scale[:, place]
-                        )
-                else:
-                    nc.scalar.activation(minuend[:, t, :], acc[t], ACT.Copy, scale=gain[:, place])
-                    nc.vector.tensor_scalar(
-                        subtrahend[:, t, :], minuend[:, t, :], neg_cut[:, place], cut[:, place], ALU.max, ALU.min
-                    )
-            return minuend, subtrahend
-
-        def subtract(width, minuend, subtrahend):
-            h_bf = work.tile([P, PACK * width], BF16, name="h_bf", bufs=3, align_bytes=64)
-            nc.vector.tensor_tensor(as_words(h_bf, 8), as_rows(minuend, 8), as_rows(subtrahend, 8), ALU.subtract)
-            return h_bf
-
-        def quantise_h(j0, width, h, h_bf):
-            nc.vector.quantize_mx(h_codes[h][:, j0 : j0 + width].bitcast(FP8X4), h_sc[h][:, j0 : j0 + width], h_bf[:])
-
-        def add_codes(acc, y0, y_width, j0, width, h):
-            per_bank = BANK // y_width
-            last = h == PASSES - 1 and j0 + width == y0 + y_width
+        def add_codes(acc, j0, width, h):
+            per_bank = BANK // width
             for t in range(PACK):
                 nc.tensor.matmul_mx(
-                    acc[t][:, j0 - y0 : j0 - y0 + width],
+                    acc[t],
                     lhsT=w_codes[h][:, P * t : P * (t + 1)].bitcast(FP8X4),
                     lhsT_scale=w_sc[h][:, P * t : P * (t + 1)],
                     rhs=h_codes[h][:, j0 : j0 + width].bitcast(FP8X4),
                     rhs_scale=h_sc[h][:, j0 : j0 + width],
                     start=False,
-                    stop=(last and t % per_bank == per_bank - 1),
+                    stop=(h == PASSES - 1 and t % per_bank == per_bank - 1),
                 )
 
-        def add_bias(acc, j0, width, shared):
-            y = work.tile([P, PACK, width], F32, name="y", bufs=3)
+        def add_bias(acc, j0, width):
+            last = j0 + width == S2
+            y = work.tile([P, PACK, width], F32, name="y")
             for t in range(PACK):
-                if shared and t >= 2:
+                if last and t >= PACK // 2:
                     nc.vector.tensor_scalar(y[:, t, :], acc[t], bias[:, t : t + 1], None, ALU.add)
                 else:
                     nc.scalar.activation(y[:, t, :], acc[t], ACT.Identity, bias=bias[:, t : t + 1])
@@ -279,58 +282,63 @@ def tile_list_sparse_code_synthesis_kernel(
                     nc.sync.dma_start(y_rows[:, t - 1 : t + 1, j0 : j0 + width], y[:, t - 1 : t + 1, :])
             return y
 
-        def round_y(y, width, on_scalar):
-            y_bf = work.tile([P, PACK * width], BF16, name="y_bf", bufs=3, align_bytes=64)
-            if on_scalar:
-                nc.scalar.copy(as_words(y_bf), as_rows(y))
-            else:
-                nc.vector.tensor_copy(as_words(y_bf), as_rows(y))
+        def round_y(y, width):
+            y_bf = work.tile([P, PACK * width], BF16, name="y_bf", align_bytes=64)
+            copy = nc.scalar.copy if width == WIDE else nc.vector.tensor_copy
+            copy(as_words(y_bf, COPY_RUN), as_rows(y, COPY_RUN))
             return y_bf
 
         def quantise_y(y_bf, j0, width):
-            y_codes = work.tile([P, width], U32, name="y_codes", bufs=3, align_bytes=64)
+            y_codes = work.tile([P, width], U32, name="y_codes", align_bytes=64)
             nc.vector.quantize_mx(y_codes[:].bitcast(FP8X4), y_sc[:, j0 : j0 + width], y_bf[:])
             nc.sync.dma_start(y_words[:, j0 : j0 + width], y_codes[:].bitcast(I32))
 
-        W = 256
-        g0 = threshold_parts(0, 512, 0, False)
-        acc0 = open_y(0, 512)
-        h0 = subtract(512, *g0)
-        g1 = threshold_parts(0, 512, 1, False)
+        j_first, j_second, j_third = 0, WIDE, WIDE + NARROW
+
+        parts = gain_and_clamp(j_first, WIDE, 0)
+        acc_first = open_y(j_first, WIDE)
+        h_bf = subtract(WIDE, *parts)
+
+        parts = gain_and_clamp(j_first, WIDE, 1)
         round_w(0)
         round_w(1)
-        quantise_h(0, 512, 0, h0)
-        h1 = subtract(512, *g1)
+        quantise_h(j_first, WIDE, 0, h_bf)
+        h_bf = subtract(WIDE, *parts)
         quantise_w(0)
-        add_codes(acc0, 0, 512, 0, 512, 0)
-        g4 = threshold_parts(512, 512, 0, False)
-        quantise_h(0, 512, 1, h1)
+        add_codes(acc_first, j_first, WIDE, 0)
+
+        parts = gain_and_clamp(j_second, WIDE, 0)
+        quantise_h(j_first, WIDE, 1, h_bf)
         quantise_w(1)
-        add_codes(acc0, 0, 512, 0, 512, 1)
-        h4 = subtract(512, *g4)
-        g5 = threshold_parts(512, W, 1, False)
-        y0 = add_bias(acc0, 0, 512, False)
-        acc1 = open_y(512, W)
-        acc2 = open_y(768, W)
-        quantise_h(512, 512, 0, h4)
-        add_codes(acc1, 512, W, 512, W, 0)
-        add_codes(acc2, 768, W, 768, W, 0)
-        h5 = subtract(W, *g5)
-        g7 = threshold_parts(768, W, 1, False)
-        b0 = round_y(y0, 512, True)
-        quantise_h(512, W, 1, h5)
-        add_codes(acc1, 512, W, 512, W, 1)
-        h7 = subtract(W, *g7)
-        y1 = add_bias(acc1, 512, W, False)
-        quantise_y(b0, 0, 512)
-        quantise_h(768, W, 1, h7)
-        add_codes(acc2, 768, W, 768, W, 1)
-        b1 = round_y(y1, W, False)
-        y2 = add_bias(acc2, 768, W, True)
-        quantise_y(b1, 512, W)
-        b2 = round_y(y2, W, False)
-        quantise_y(b2, 768, W)
-        for q in range(4):
+        add_codes(acc_first, j_first, WIDE, 1)
+        h_bf = subtract(WIDE, *parts)
+
+        parts = gain_and_clamp(j_second, NARROW, 1)
+        y_first = add_bias(acc_first, j_first, WIDE)
+        acc_second = open_y(j_second, NARROW)
+        acc_third = open_y(j_third, NARROW)
+        quantise_h(j_second, WIDE, 0, h_bf)
+        add_codes(acc_second, j_second, NARROW, 0)
+        add_codes(acc_third, j_third, NARROW, 0)
+        h_bf = subtract(NARROW, *parts)
+
+        parts = gain_and_clamp(j_third, NARROW, 1)
+        y_bf_first = round_y(y_first, WIDE)
+        quantise_h(j_second, NARROW, 1, h_bf)
+        add_codes(acc_second, j_second, NARROW, 1)
+        h_bf = subtract(NARROW, *parts)
+
+        y_second = add_bias(acc_second, j_second, NARROW)
+        quantise_y(y_bf_first, j_first, WIDE)
+        quantise_h(j_third, NARROW, 1, h_bf)
+        add_codes(acc_third, j_third, NARROW, 1)
+        y_bf_second = round_y(y_second, NARROW)
+        y_third = add_bias(acc_third, j_third, NARROW)
+        quantise_y(y_bf_second, j_second, NARROW)
+        quantise_y(round_y(y_third, NARROW), j_third, NARROW)
+
+        for q in range(QUADRANTS):
             (nc.sync if q % 2 == 0 else nc.scalar).dma_start(
-                out_2[0, 4 * q : 4 * q + 4, :].bitcast(I32), y_sc[32 * q : 32 * q + 4, :].bitcast(I32)
+                out_2[0, PLANE_ROWS * q : PLANE_ROWS * (q + 1), :].bitcast(I32),
+                y_sc[QUADRANT * q : QUADRANT * q + PLANE_ROWS, :].bitcast(I32),
             )

@@ -66,8 +66,8 @@ def tile_list_sparse_code_synthesis_kernel(
         load_scale_rows(v2s_table, tab2_scales)
         v2_table0 = keep.tile([P, T2], I32, name="v2_table0", tag="slot_c", align_bytes=64)
         load_words(v2_table0, tab2_words[0])
-        v_table1 = keep.tile([P, T], I32, name="v_table1", tag="slot_d", align_bytes=64)
-        load_words(v_table1, tab_words[1])
+        v_first = keep.tile([P, T], I32, name="v_first", tag="slot_d", align_bytes=64)
+        load_words(v_first, tab_words[0])
 
         by_place = keep.tile([P, P], F32, name="by_place")
         v2s_pass1 = keep.tile([P, S2], U8, name="v2s_pass1", align_bytes=64)
@@ -118,8 +118,8 @@ def tile_list_sparse_code_synthesis_kernel(
         vs_placed = keep.tile([P, S], U8, name="vs_placed", align_bytes=64)
         nc.vector.tensor_copy(vs_listed[:], vs_table[:].indirect(idx[:]))
         place_rows(vs_placed, vs_listed)
-        v_table0 = keep.tile([P, T], I32, name="v_table0", tag="slot_b", align_bytes=64)
-        load_words(v_table0, tab_words[0])
+        v_second = keep.tile([P, T], I32, name="v_second", tag="slot_b", align_bytes=64)
+        load_words(v_second, tab_words[1])
         v2s_listed = keep.tile([P, S2], U8, name="v2s_listed", align_bytes=64)
         v2_sc = keep.tile([P, S2], U8, name="v2_sc", align_bytes=64)
         nc.vector.tensor_copy(v2s_listed[:], v2s_table[:].indirect(idx2[:]))
@@ -133,7 +133,7 @@ def tile_list_sparse_code_synthesis_kernel(
         gather_v2(0, v2_table0, 0, S2)
         w4_raw = keep.tile([P, PASSES, 2 * N], U8, name="w4_raw", tag="slot_c", align_bytes=64)
         nc.sync.dma_start(w4_raw[:].bitcast(I32), w4_words.rearrange("a p c -> p a c").bitcast(I32))
-        gather_v(1, v_table1)
+        gather_v(0, v_first)
         bias = keep.tile([P, PACK], F32, name="bias", tag="slot_d", align_bytes=64)
         nc.sync.dma_start(bias[:], b.rearrange("(p t) -> p t", t=PACK))
         v_sc = keep.tile([P, S], U8, name="v_sc", align_bytes=64)
@@ -147,7 +147,7 @@ def tile_list_sparse_code_synthesis_kernel(
                 w4s_raw[QUADRANT * q : QUADRANT * q + PLANE_ROWS, :].bitcast(I32).rearrange("r (a c) -> r a c", a=PASSES),
                 w4_scales[:, PLANE_ROWS * q : PLANE_ROWS * (q + 1), :].rearrange("a r c -> r a c").bitcast(I32),
             )
-        gather_v(0, v_table0)
+        gather_v(1, v_second)
         gather_v2(1, v2_table1, 0, WIDE)
         gather_v2(1, v2_table1, WIDE, S2)
 
@@ -203,24 +203,23 @@ def tile_list_sparse_code_synthesis_kernel(
         def as_rows(rows, run):
             return rows[:].rearrange("p t (c i) -> p c t i", i=run)
 
-        def gain_and_clamp(j0, width, h):
-            acc = psum_results("a_bank", width)
+        def correlate(acc, j0, width, h, passes):
+            for t in range(PACK):
+                for a in passes:
+                    cols = slice(PASS * h + P * t, PASS * h + P * (t + 1))
+                    nc.tensor.matmul_mx(
+                        acc[t],
+                        lhsT=v_codes[a][:, cols].bitcast(FP8X4),
+                        lhsT_scale=v_sc[PLANE_ROWS * a : P, cols],
+                        rhs=v2_codes[a][:, j0 : j0 + width].bitcast(FP8X4),
+                        rhs_scale=v2_sc[PLANE_ROWS * a : P, j0 : j0 + width],
+                        start=(a == 0),
+                        stop=(a == PASSES - 1),
+                    )
+
+        def gain_and_clamp(acc, width, h):
             gained = work.tile([P, PACK, width], F32, name="gained")
             clamped = work.tile([P, PACK, width], F32, name="clamped")
-            order = [(t, a) for t in range(PACK) for a in range(PASSES)]
-            if j0 == 0 and h == 0:
-                order = [(t, a) for a in range(PASSES) for t in range(PACK)]
-            for t, a in order:
-                cols = slice(PASS * h + P * t, PASS * h + P * (t + 1))
-                nc.tensor.matmul_mx(
-                    acc[t],
-                    lhsT=v_codes[a][:, cols].bitcast(FP8X4),
-                    lhsT_scale=v_sc[PLANE_ROWS * a : P, cols],
-                    rhs=v2_codes[a][:, j0 : j0 + width].bitcast(FP8X4),
-                    rhs_scale=v2_sc[PLANE_ROWS * a : P, j0 : j0 + width],
-                    start=(a == 0),
-                    stop=(a == PASSES - 1),
-                )
             for t in range(PACK):
                 place = slice(PACK * h + t, PACK * h + t + 1)
                 nc.scalar.activation(gained[:, t, :], acc[t], ACT.Copy, scale=gain[:, place])
@@ -239,8 +238,8 @@ def tile_list_sparse_code_synthesis_kernel(
         def quantise_h(j0, width, h, h_bf):
             nc.vector.quantize_mx(h_codes[h][:, j0 : j0 + width].bitcast(FP8X4), h_sc[h][:, j0 : j0 + width], h_bf[:])
 
-        def open_y(j0, width):
-            acc = psum_results("y_bank", width)
+        def open_y(j0, width, tag):
+            acc = psum_results(tag, width)
             per_bank = BANK // width
             step = BANK if width == BANK else P
             for a in range(PASSES):
@@ -295,34 +294,44 @@ def tile_list_sparse_code_synthesis_kernel(
 
         j_first, j_second, j_third = 0, WIDE, WIDE + NARROW
 
-        parts = gain_and_clamp(j_first, WIDE, 0)
-        acc_first = open_y(j_first, WIDE)
+        acc_a, acc_b = psum_results("y_bank", WIDE), psum_results("a_bank", WIDE)
+        for a in range(PASSES):
+            correlate(acc_a, j_first, WIDE, 0, [a])
+            correlate(acc_b, j_first, WIDE, 1, [a])
+        parts = gain_and_clamp(acc_a, WIDE, 0)
         h_bf = subtract(WIDE, *parts)
 
-        parts = gain_and_clamp(j_first, WIDE, 1)
+        parts = gain_and_clamp(acc_b, WIDE, 1)
+        acc_first = open_y(j_first, WIDE, "y_bank")
         round_w(0)
-        round_w(1)
         quantise_h(j_first, WIDE, 0, h_bf)
         h_bf = subtract(WIDE, *parts)
         quantise_w(0)
-        add_codes(acc_first, j_first, WIDE, 0)
 
-        parts = gain_and_clamp(j_second, WIDE, 0)
+        acc = psum_results("a_bank", WIDE)
+        correlate(acc, j_second, WIDE, 0, range(PASSES))
+        parts = gain_and_clamp(acc, WIDE, 0)
+        add_codes(acc_first, j_first, WIDE, 0)
+        round_w(1)
         quantise_h(j_first, WIDE, 1, h_bf)
         quantise_w(1)
-        add_codes(acc_first, j_first, WIDE, 1)
         h_bf = subtract(WIDE, *parts)
 
-        parts = gain_and_clamp(j_second, NARROW, 1)
-        y_first = add_bias(acc_first, j_first, WIDE)
-        acc_second = open_y(j_second, NARROW)
-        acc_third = open_y(j_third, NARROW)
+        acc = psum_results("a_bank", NARROW)
+        correlate(acc, j_second, NARROW, 1, range(PASSES))
+        parts = gain_and_clamp(acc, NARROW, 1)
         quantise_h(j_second, WIDE, 0, h_bf)
-        add_codes(acc_second, j_second, NARROW, 0)
-        add_codes(acc_third, j_third, NARROW, 0)
         h_bf = subtract(NARROW, *parts)
 
-        parts = gain_and_clamp(j_third, NARROW, 1)
+        acc = psum_results("a_bank", NARROW)
+        correlate(acc, j_third, NARROW, 1, range(PASSES))
+        add_codes(acc_first, j_first, WIDE, 1)
+        parts = gain_and_clamp(acc, NARROW, 1)
+        acc_second = open_y(j_second, NARROW, "a_bank")
+        acc_third = open_y(j_third, NARROW, "a_bank")
+        add_codes(acc_second, j_second, NARROW, 0)
+        add_codes(acc_third, j_third, NARROW, 0)
+        y_first = add_bias(acc_first, j_first, WIDE)
         y_bf_first = round_y(y_first, WIDE)
         quantise_h(j_second, NARROW, 1, h_bf)
         add_codes(acc_second, j_second, NARROW, 1)

@@ -92,6 +92,8 @@ def tile_list_sparse_code_synthesis_kernel(
         for s in range(PLACES):
             nc.scalar.activation(cut[:, s : s + 1], gain[:, s : s + 1], ACT.Abs, scale=lam_gain[:, s : s + 1])
         nc.scalar.activation(neg_cut[:], cut[:], ACT.Copy, scale=-1.0)
+        neg_gain = keep.tile([P, PLACES], F32, name="neg_gain")
+        nc.scalar.activation(neg_gain[:], gain, ACT.Copy, scale=-1.0)
 
         v_codes = [keep.tile([P, S], U32, name="v_codes%d" % a, align_bytes=64) for a in range(PASSES)]
         v2_codes = [keep.tile([P, S2], U32, name="v2_codes%d" % a, align_bytes=64) for a in range(PASSES)]
@@ -217,11 +219,17 @@ def tile_list_sparse_code_synthesis_kernel(
                         stop=(a == PASSES - 1),
                     )
 
-        def gain_and_clamp(acc, width, h):
+        def gain_and_clamp(acc, width, h, relus=False):
             gained = work.tile([P, PACK, width], F32, name="gained")
             clamped = work.tile([P, PACK, width], F32, name="clamped")
             for t in range(PACK):
                 place = slice(PACK * h + t, PACK * h + t + 1)
+                if relus:
+                    nc.scalar.activation(gained[:, t, :], acc[t], ACT.Relu, scale=gain[:, place], bias=neg_cut[:, place])
+                    nc.scalar.activation(
+                        clamped[:, t, :], acc[t], ACT.Relu, scale=neg_gain[:, place], bias=neg_cut[:, place]
+                    )
+                    continue
                 nc.scalar.activation(gained[:, t, :], acc[t], ACT.Copy, scale=gain[:, place])
                 nc.vector.tensor_scalar(
                     clamped[:, t, :], gained[:, t, :], neg_cut[:, place], cut[:, place], ALU.max, ALU.min
@@ -319,7 +327,7 @@ def tile_list_sparse_code_synthesis_kernel(
 
         acc = psum_results("a_bank", NARROW)
         correlate(acc, j_second, NARROW, 1, range(PASSES))
-        parts = gain_and_clamp(acc, NARROW, 1)
+        parts = gain_and_clamp(acc, NARROW, 1, relus=True)
         quantise_h(j_second, WIDE, 0, h_bf)
         h_bf = subtract(NARROW, *parts)
 

@@ -92,8 +92,8 @@ def tile_list_sparse_code_synthesis_kernel(
         for s in range(PLACES):
             nc.scalar.activation(cut[:, s : s + 1], gain[:, s : s + 1], ACT.Abs, scale=lam_gain[:, s : s + 1])
         nc.scalar.activation(neg_cut[:], cut[:], ACT.Copy, scale=-1.0)
-        neg_gain = keep.tile([P, PLACES], F32, name="neg_gain")
-        nc.scalar.activation(neg_gain[:], gain, ACT.Copy, scale=-1.0)
+        neg_gain_pass1 = keep.tile([P, PACK], F32, name="neg_gain_pass1")
+        nc.scalar.activation(neg_gain_pass1[:], gain[:, PACK:PLACES], ACT.Copy, scale=-1.0)
 
         v_codes = [keep.tile([P, S], U32, name="v_codes%d" % a, align_bytes=64) for a in range(PASSES)]
         v2_codes = [keep.tile([P, S2], U32, name="v2_codes%d" % a, align_bytes=64) for a in range(PASSES)]
@@ -138,34 +138,43 @@ def tile_list_sparse_code_synthesis_kernel(
         gather_v(0, v_first)
         bias = keep.tile([P, PACK], F32, name="bias", tag="slot_d", align_bytes=64)
         nc.sync.dma_start(bias[:], b.rearrange("(p t) -> p t", t=PACK))
-        v_sc = keep.tile([P, S], U8, name="v_sc", align_bytes=64)
-        nc.vector.tensor_copy(
-            v_sc[:].bitcast(I32).rearrange("p (s u e) -> p s u e", s=PLACES, e=2),
-            vs_placed[:].bitcast(I32).rearrange("p (u s e) -> p s u e", s=PLACES, e=2),
-        )
-        w4s_raw = vs_placed
+        def deal_v_scales(h, tag):
+            planes = keep.tile([P, PASS], U8, name="v_sc", tag=tag, align_bytes=64)
+            nc.vector.tensor_copy(
+                planes[:].bitcast(I32).rearrange("p (t u e) -> p t u e", t=PACK, e=2),
+                vs_placed[:].bitcast(I32).rearrange("p (u h t e) -> p h t u e", h=PASSES, t=PACK, e=2)[:, h],
+            )
+            return planes
+
+        v_sc = [deal_v_scales(0, "v_sc0")]
+        gather_v(1, v_second)
+        v_sc.extend([deal_v_scales(1, "slot_b")])
+        w4s_raw = vs_placed[:, 0:N]
         for q in range(QUADRANTS):
             nc.sync.dma_start(
-                w4s_raw[QUADRANT * q : QUADRANT * q + PLANE_ROWS, :].bitcast(I32).rearrange("r (a c) -> r a c", a=PASSES),
-                w4_scales[:, PLANE_ROWS * q : PLANE_ROWS * (q + 1), :].rearrange("a r c -> r a c").bitcast(I32),
+                w4s_raw[QUADRANT * q : QUADRANT * q + PASSES * PLANE_ROWS, :].bitcast(I32),
+                w4_scales[:, PLANE_ROWS * q : PLANE_ROWS * (q + 1), :].bitcast(I32),
             )
-        gather_v(1, v_second)
         gather_v2(1, v2_table1, 0, WIDE)
         gather_v2(1, v2_table1, WIDE, S2)
 
         w4_codes = keep.tile([P, PASSES, 2 * N], U8, name="w4_codes", align_bytes=64)
-        w4_sc = keep.tile([P, PASSES * N], U8, name="w4_sc", align_bytes=64)
+        w4_sc = keep.tile([P, N], U8, name="w4_sc", align_bytes=64)
         nc.vector.tensor_copy(
             w4_codes[:].bitcast(U16).rearrange("p a (t m) -> p a t m", t=PACK),
             w4_raw[:].bitcast(U16).rearrange("p a (m t) -> p a t m", t=PACK),
         )
         nc.vector.tensor_copy(
-            w4_sc[:].rearrange("p (a t m) -> p a t m", t=PACK, m=P),
-            w4s_raw[:].rearrange("p (a m t) -> p a t m", t=PACK, m=P),
+            w4_sc[:].rearrange("p (t m) -> p t m", t=PACK), w4s_raw.rearrange("p (m t) -> p t m", t=PACK)
         )
+        w4s_pass1 = vs_placed[:, N : 2 * N]
+        nc.sync.dma_start(
+            w4s_pass1[0:SHIFTED, :].bitcast(I32), w4_sc[PLANE_ROWS : PLANE_ROWS + SHIFTED, :].bitcast(I32)
+        )
+        w4_planes = [w4_sc[:], w4s_pass1]
 
         w_raw = [
-            keep.tile([P, PACK, N], F32, name="w_raw0", tag="slot_b", align_bytes=64),
+            keep.tile([P, PACK, N], F32, name="w_raw0", align_bytes=64),
             keep.tile([P, PACK, N], F32, name="w_raw1", tag="slot_a", align_bytes=64),
         ]
         w_rows = w.rearrange("(u h t q) n -> h t u q n", h=PASSES, t=PACK, q=BLOCK_P)
@@ -200,10 +209,10 @@ def tile_list_sparse_code_synthesis_kernel(
             return results
 
         def as_words(words, run):
-            return words[:].rearrange("p (c i t) -> p c t i", i=run, t=PACK)
+            return words.rearrange("p (c i t) -> p c t i", i=run, t=PACK)
 
         def as_rows(rows, run):
-            return rows[:].rearrange("p t (c i) -> p c t i", i=run)
+            return rows.rearrange("p t (c i) -> p c t i", i=run)
 
         def correlate(acc, j0, width, h, passes):
             for t in range(PACK):
@@ -212,7 +221,7 @@ def tile_list_sparse_code_synthesis_kernel(
                     nc.tensor.matmul_mx(
                         acc[t],
                         lhsT=v_codes[a][:, cols].bitcast(FP8X4),
-                        lhsT_scale=v_sc[PLANE_ROWS * a : P, cols],
+                        lhsT_scale=v_sc[h][PLANE_ROWS * a : P, P * t : P * (t + 1)],
                         rhs=v2_codes[a][:, j0 : j0 + width].bitcast(FP8X4),
                         rhs_scale=v2_sc[PLANE_ROWS * a : P, j0 : j0 + width],
                         start=(a == 0),
@@ -227,7 +236,7 @@ def tile_list_sparse_code_synthesis_kernel(
                 if relus:
                     nc.scalar.activation(gained[:, t, :], acc[t], ACT.Relu, scale=gain[:, place], bias=neg_cut[:, place])
                     nc.scalar.activation(
-                        clamped[:, t, :], acc[t], ACT.Relu, scale=neg_gain[:, place], bias=neg_cut[:, place]
+                        clamped[:, t, :], acc[t], ACT.Relu, scale=neg_gain_pass1[:, t : t + 1], bias=neg_cut[:, place]
                     )
                     continue
                 nc.scalar.activation(gained[:, t, :], acc[t], ACT.Copy, scale=gain[:, place])
@@ -239,7 +248,7 @@ def tile_list_sparse_code_synthesis_kernel(
         def subtract(width, gained, clamped):
             h_bf = work.tile([P, PACK * width], BF16, name="h_bf", align_bytes=64)
             nc.vector.tensor_tensor(
-                as_words(h_bf, SUBTRACT_RUN), as_rows(gained, SUBTRACT_RUN), as_rows(clamped, SUBTRACT_RUN), ALU.subtract
+                as_words(h_bf[:], SUBTRACT_RUN), as_rows(gained[:], SUBTRACT_RUN), as_rows(clamped[:], SUBTRACT_RUN), ALU.subtract
             )
             return h_bf
 
@@ -256,7 +265,7 @@ def tile_list_sparse_code_synthesis_kernel(
                         nc.tensor.matmul_mx(
                             acc[t][:, c : c + step],
                             lhsT=w4_codes[:, a, 2 * P * t : 2 * P * (t + 1)].bitcast(FP4X4),
-                            lhsT_scale=w4_sc[:, N * a + P * t : N * a + P * (t + 1)],
+                            lhsT_scale=w4_planes[a][:, P * t : P * (t + 1)],
                             rhs=v2_codes[a][:, j0 + c : j0 + c + step].bitcast(FP8X4),
                             rhs_scale=v2_planes_from_row_0[a][:, j0 + c : j0 + c + step],
                             start=(a == 0 and c == 0 and t % per_bank == 0),
@@ -291,8 +300,9 @@ def tile_list_sparse_code_synthesis_kernel(
 
         def round_y(y, width):
             y_bf = work.tile([P, PACK * width], BF16, name="y_bf", align_bytes=64)
-            copy = nc.scalar.copy if width == WIDE else nc.vector.tensor_copy
-            copy(as_words(y_bf, COPY_RUN), as_rows(y, COPY_RUN))
+            for c in range(0, width, NARROW):
+                copy = nc.scalar.copy if c + NARROW < width else nc.vector.tensor_copy
+                copy(as_words(y_bf[:, PACK * c : PACK * (c + NARROW)], COPY_RUN), as_rows(y[:, :, c : c + NARROW], COPY_RUN))
             return y_bf
 
         def quantise_y(y_bf, j0, width):

@@ -32,6 +32,7 @@ BANK = 512
 LIST_ROWS = 16
 WIDE = BANK
 NARROW = BANK // 2
+CHUNKS = ((0, NARROW), (NARROW, WIDE), (NARROW + WIDE, NARROW))
 COPY_RUN = 4
 SUBTRACT_RUN = 8
 
@@ -45,7 +46,7 @@ def tile_list_sparse_code_synthesis_kernel(
         lists = ctx.enter_context(tc.tile_pool(name="lists", bufs=1))
         keep = ctx.enter_context(tc.tile_pool(name="keep", bufs=1))
         work = ctx.enter_context(tc.tile_pool(name="work", bufs=3))
-        psum = ctx.enter_context(tc.psum_pool(name="psum", bufs=4))
+        psum = ctx.enter_context(tc.psum_pool(name="psum", bufs=1))
 
         ident = keep.tile([P, P], F32, name="ident")
         make_identity(nc, ident[:])
@@ -82,7 +83,7 @@ def tile_list_sparse_code_synthesis_kernel(
                 by_place[PLACES * k : PLACES * (k + 1), :].rearrange("s (u q) -> s u q", q=BLOCK_P),
                 vec.rearrange("(u s q) -> s u q", s=PLACES, q=BLOCK_P),
             )
-        turned = psum.tile([P, BANK], F32, name="a_bank")
+        turned = psum.tile([P, BANK], F32, name="bank7")
         nc.tensor.transpose(turned[:, 0:P], by_place[:], ident[:])
         lam_gain = keep.tile([P, 2 * PLACES], F32, name="lam_gain")
         nc.scalar.copy(lam_gain[:], turned[:, 0 : 2 * PLACES])
@@ -92,8 +93,6 @@ def tile_list_sparse_code_synthesis_kernel(
         for s in range(PLACES):
             nc.scalar.activation(cut[:, s : s + 1], gain[:, s : s + 1], ACT.Abs, scale=lam_gain[:, s : s + 1])
         nc.scalar.activation(neg_cut[:], cut[:], ACT.Copy, scale=-1.0)
-        neg_gain_pass1 = keep.tile([P, PACK], F32, name="neg_gain_pass1")
-        nc.scalar.activation(neg_gain_pass1[:], gain[:, PACK:PLACES], ACT.Copy, scale=-1.0)
 
         v_codes = [keep.tile([P, S], U32, name="v_codes%d" % a, align_bytes=64) for a in range(PASSES)]
         v2_codes = [keep.tile([P, S2], U32, name="v2_codes%d" % a, align_bytes=64) for a in range(PASSES)]
@@ -133,11 +132,13 @@ def tile_list_sparse_code_synthesis_kernel(
         )
 
         gather_v2(0, v2_table0, 0, S2)
-        w4_raw = keep.tile([P, PASSES, 2 * N], U8, name="w4_raw", tag="slot_c", align_bytes=64)
-        nc.sync.dma_start(w4_raw[:].bitcast(I32), w4_words.rearrange("a p c -> p a c").bitcast(I32))
+        w4_raw = [
+            keep.tile([P, 2 * N], U8, name="w4_raw0", tag="slot_c", align_bytes=64),
+            keep.tile([P, 2 * N], U8, name="w4_raw1", tag="slot_d", align_bytes=64),
+        ]
+        nc.sync.dma_start(w4_raw[0][:].bitcast(I32), w4_words[0].bitcast(I32))
         gather_v(0, v_first)
-        bias = keep.tile([P, PACK], F32, name="bias", tag="slot_d", align_bytes=64)
-        nc.sync.dma_start(bias[:], b.rearrange("(p t) -> p t", t=PACK))
+        nc.sync.dma_start(w4_raw[1][:].bitcast(I32), w4_words[1].bitcast(I32))
         def deal_v_scales(h, tag):
             planes = keep.tile([P, PASS], U8, name="v_sc", tag=tag, align_bytes=64)
             nc.vector.tensor_copy(
@@ -155,24 +156,19 @@ def tile_list_sparse_code_synthesis_kernel(
                 w4s_raw[QUADRANT * q : QUADRANT * q + PASSES * PLANE_ROWS, :].bitcast(I32),
                 w4_scales[:, PLANE_ROWS * q : PLANE_ROWS * (q + 1), :].bitcast(I32),
             )
-        gather_v2(1, v2_table1, 0, WIDE)
-        gather_v2(1, v2_table1, WIDE, S2)
+        for j0, width in CHUNKS:
+            gather_v2(1, v2_table1, j0, j0 + width)
 
-        w4_codes = keep.tile([P, PASSES, 2 * N], U8, name="w4_codes", align_bytes=64)
+        w4_codes = [keep.tile([P, 2 * N], U8, name="w4_codes%d" % a, align_bytes=64) for a in range(PASSES)]
         w4_sc = keep.tile([P, N], U8, name="w4_sc", align_bytes=64)
-        nc.vector.tensor_copy(
-            w4_codes[:].bitcast(U16).rearrange("p a (t m) -> p a t m", t=PACK),
-            w4_raw[:].bitcast(U16).rearrange("p a (m t) -> p a t m", t=PACK),
-        )
+        for a in range(PASSES):
+            nc.scalar.copy(
+                w4_codes[a][:].bitcast(U16).rearrange("p (t m) -> p t m", t=PACK),
+                w4_raw[a][:].bitcast(U16).rearrange("p (m t) -> p t m", t=PACK),
+            )
         nc.vector.tensor_copy(
             w4_sc[:].rearrange("p (t m) -> p t m", t=PACK), w4s_raw.rearrange("p (m t) -> p t m", t=PACK)
         )
-        w4s_pass1 = vs_placed[:, N : 2 * N]
-        nc.sync.dma_start(
-            w4s_pass1[0:SHIFTED, :].bitcast(I32), w4_sc[PLANE_ROWS : PLANE_ROWS + SHIFTED, :].bitcast(I32)
-        )
-        w4_planes = [w4_sc[:], w4s_pass1]
-
         w_raw = [
             keep.tile([P, PACK, N], F32, name="w_raw0", align_bytes=64),
             keep.tile([P, PACK, N], F32, name="w_raw1", tag="slot_a", align_bytes=64),
@@ -181,6 +177,14 @@ def tile_list_sparse_code_synthesis_kernel(
         for h in range(PASSES):
             for t in range(PACK):
                 nc.sync.dma_start(w_raw[h][:, t, :], w_rows[h, t])
+            if h == 0:
+                w4s_pass1 = vs_placed[:, N : 2 * N]
+                nc.sync.dma_start(
+                    w4s_pass1[0:SHIFTED, :].bitcast(I32), w4_sc[PLANE_ROWS : PLANE_ROWS + SHIFTED, :].bitcast(I32)
+                )
+        w4_planes = [w4_sc[:], w4s_pass1]
+        bias = keep.tile([P, PACK], F32, name="bias", tag="slot_c", align_bytes=64)
+        nc.sync.dma_start(bias[:], b.rearrange("(p t) -> p t", t=PACK))
         w_bf = [keep.tile([P, PACK * N], BF16, name="w_bf%d" % h, align_bytes=64) for h in range(PASSES)]
         w_codes = [keep.tile([P, N], U32, name="w_codes%d" % h, align_bytes=64) for h in range(PASSES)]
         w_sc = [keep.tile([P, N], U8, name="w_sc%d" % h, align_bytes=64) for h in range(PASSES)]
@@ -200,11 +204,11 @@ def tile_list_sparse_code_synthesis_kernel(
         def quantise_w(h):
             nc.vector.quantize_mx(w_codes[h][:].bitcast(FP8X4), w_sc[h][:], w_bf[h][:])
 
-        def psum_results(tag, width):
+        def psum_results(banks, width):
             per_bank = BANK // width
             results = []
-            for first_t in range(0, PACK, per_bank):
-                bank = psum.tile([P, BANK], F32, name=tag)
+            for number in banks:
+                bank = psum.tile([P, BANK], F32, name="bank%d" % number)
                 results.extend([bank[:, width * x : width * (x + 1)] for x in range(per_bank)])
             return results
 
@@ -214,31 +218,29 @@ def tile_list_sparse_code_synthesis_kernel(
         def as_rows(rows, run):
             return rows.rearrange("p t (c i) -> p c t i", i=run)
 
-        def correlate(acc, j0, width, h, passes):
-            for t in range(PACK):
+        def correlate(acc, chunk, h, passes):
+            j0, width = chunk
+            per_bank = BANK // width
+            for first_t in range(0, PACK, per_bank):
                 for a in passes:
-                    cols = slice(PASS * h + P * t, PASS * h + P * (t + 1))
-                    nc.tensor.matmul_mx(
-                        acc[t],
-                        lhsT=v_codes[a][:, cols].bitcast(FP8X4),
-                        lhsT_scale=v_sc[h][PLANE_ROWS * a : P, P * t : P * (t + 1)],
-                        rhs=v2_codes[a][:, j0 : j0 + width].bitcast(FP8X4),
-                        rhs_scale=v2_sc[PLANE_ROWS * a : P, j0 : j0 + width],
-                        start=(a == 0),
-                        stop=(a == PASSES - 1),
-                    )
+                    for t in range(first_t, first_t + per_bank):
+                        cols = slice(PASS * h + P * t, PASS * h + P * (t + 1))
+                        nc.tensor.matmul_mx(
+                            acc[t],
+                            lhsT=v_codes[a][:, cols].bitcast(FP8X4),
+                            lhsT_scale=v_sc[h][PLANE_ROWS * a : P, P * t : P * (t + 1)],
+                            rhs=v2_codes[a][:, j0 : j0 + width].bitcast(FP8X4),
+                            rhs_scale=v2_sc[PLANE_ROWS * a : P, j0 : j0 + width],
+                            start=(a == 0 and t == first_t),
+                            stop=(a == PASSES - 1 and t == first_t + per_bank - 1),
+                        )
 
-        def gain_and_clamp(acc, width, h, relus=False):
+        def gain_and_clamp(acc, chunk, h):
+            width = chunk[1]
             gained = work.tile([P, PACK, width], F32, name="gained")
             clamped = work.tile([P, PACK, width], F32, name="clamped")
             for t in range(PACK):
                 place = slice(PACK * h + t, PACK * h + t + 1)
-                if relus:
-                    nc.scalar.activation(gained[:, t, :], acc[t], ACT.Relu, scale=gain[:, place], bias=neg_cut[:, place])
-                    nc.scalar.activation(
-                        clamped[:, t, :], acc[t], ACT.Relu, scale=neg_gain_pass1[:, t : t + 1], bias=neg_cut[:, place]
-                    )
-                    continue
                 nc.scalar.activation(gained[:, t, :], acc[t], ACT.Copy, scale=gain[:, place])
                 nc.vector.tensor_scalar(
                     clamped[:, t, :], gained[:, t, :], neg_cut[:, place], cut[:, place], ALU.max, ALU.min
@@ -255,23 +257,20 @@ def tile_list_sparse_code_synthesis_kernel(
         def quantise_h(j0, width, h, h_bf):
             nc.vector.quantize_mx(h_codes[h][:, j0 : j0 + width].bitcast(FP8X4), h_sc[h][:, j0 : j0 + width], h_bf[:])
 
-        def open_y(j0, width, tag):
-            acc = psum_results(tag, width)
+        def open_y(acc, chunk, places):
+            j0, width = chunk
             per_bank = BANK // width
-            step = BANK if width == BANK else P
-            for a in range(PASSES):
-                for t in range(PACK):
-                    for c in range(0, width, step):
-                        nc.tensor.matmul_mx(
-                            acc[t][:, c : c + step],
-                            lhsT=w4_codes[:, a, 2 * P * t : 2 * P * (t + 1)].bitcast(FP4X4),
-                            lhsT_scale=w4_planes[a][:, P * t : P * (t + 1)],
-                            rhs=v2_codes[a][:, j0 + c : j0 + c + step].bitcast(FP8X4),
-                            rhs_scale=v2_planes_from_row_0[a][:, j0 + c : j0 + c + step],
-                            start=(a == 0 and c == 0 and t % per_bank == 0),
-                            stop=False,
-                        )
-            return acc
+            for t in places:
+                for a in range(PASSES):
+                    nc.tensor.matmul_mx(
+                        acc[t],
+                        lhsT=w4_codes[a][:, 2 * P * t : 2 * P * (t + 1)].bitcast(FP4X4),
+                        lhsT_scale=w4_planes[a][:, P * t : P * (t + 1)],
+                        rhs=v2_codes[a][:, j0 : j0 + width].bitcast(FP8X4),
+                        rhs_scale=v2_planes_from_row_0[a][:, j0 : j0 + width],
+                        start=(a == 0 and t % per_bank == 0),
+                        stop=False,
+                    )
 
         def add_codes(acc, j0, width, h):
             per_bank = BANK // width
@@ -310,59 +309,67 @@ def tile_list_sparse_code_synthesis_kernel(
             nc.vector.quantize_mx(y_codes[:].bitcast(FP8X4), y_sc[:, j0 : j0 + width], y_bf[:])
             nc.sync.dma_start(y_words[:, j0 : j0 + width], y_codes[:].bitcast(I32))
 
-        j_first, j_second, j_third = 0, WIDE, WIDE + NARROW
+        first, second, third = CHUNKS
+        acc_a0, acc_a1, acc_b0 = psum_results((0, 1), NARROW), psum_results((2, 3), NARROW), psum_results((4, 5, 6, 7), WIDE)
+        correlate(acc_a0, first, 0, [0])
+        correlate(acc_b0, second, 0, [0])
+        correlate(acc_a1, first, 1, [0])
+        correlate(acc_a0, first, 0, [1])
+        correlate(acc_a1, first, 1, [1])
+        correlate(acc_b0, second, 0, [1])
 
-        acc_a, acc_b = psum_results("y_bank", WIDE), psum_results("a_bank", WIDE)
-        for a in range(PASSES):
-            correlate(acc_a, j_first, WIDE, 0, [a])
-            correlate(acc_b, j_first, WIDE, 1, [a])
-        parts = gain_and_clamp(acc_a, WIDE, 0)
-        h_bf = subtract(WIDE, *parts)
+        h_bf = subtract(NARROW, *gain_and_clamp(acc_a0, first, 0))
+        parts = gain_and_clamp(acc_a1, first, 1)
+        quantise_h(*first, 0, h_bf)
+        h_bf = subtract(NARROW, *parts)
 
-        parts = gain_and_clamp(acc_b, WIDE, 1)
-        acc_first = open_y(j_first, WIDE, "y_bank")
+        acc_b1 = psum_results((0, 1, 2, 3), WIDE)
+        correlate(acc_b1, second, 1, range(PASSES))
+        parts = gain_and_clamp(acc_b0, second, 0)
+        quantise_h(*first, 1, h_bf)
         round_w(0)
-        quantise_h(j_first, WIDE, 0, h_bf)
         h_bf = subtract(WIDE, *parts)
+
+        acc_c0 = psum_results((4, 5), NARROW)
+        correlate(acc_c0, third, 0, range(PASSES))
+        y_first_acc = psum_results((6, 7), NARROW)
+        open_y(y_first_acc, first, range(PACK))
+        parts = gain_and_clamp(acc_b1, second, 1)
         quantise_w(0)
-
-        acc = psum_results("a_bank", WIDE)
-        correlate(acc, j_second, WIDE, 0, range(PASSES))
-        parts = gain_and_clamp(acc, WIDE, 0)
-        add_codes(acc_first, j_first, WIDE, 0)
-        round_w(1)
-        quantise_h(j_first, WIDE, 1, h_bf)
-        quantise_w(1)
+        quantise_h(*second, 0, h_bf)
+        add_codes(y_first_acc, *first, 0)
         h_bf = subtract(WIDE, *parts)
 
-        acc = psum_results("a_bank", NARROW)
-        correlate(acc, j_second, NARROW, 1, range(PASSES))
-        parts = gain_and_clamp(acc, NARROW, 1, relus=True)
-        quantise_h(j_second, WIDE, 0, h_bf)
+        y_second_acc = psum_results((0, 1, 2, 3), WIDE)
+        open_y(y_second_acc, second, range(PACK))
+        parts = gain_and_clamp(acc_c0, third, 0)
+        acc_c1 = psum_results((4, 5), NARROW)
+        correlate(acc_c1, third, 1, range(PASSES))
+        round_w(1)
+        add_codes(y_second_acc, *second, 0)
+        quantise_w(1)
+        add_codes(y_first_acc, *first, 1)
+        quantise_h(*second, 1, h_bf)
+        add_codes(y_second_acc, *second, 1)
         h_bf = subtract(NARROW, *parts)
 
-        acc = psum_results("a_bank", NARROW)
-        correlate(acc, j_third, NARROW, 1, range(PASSES))
-        add_codes(acc_first, j_first, WIDE, 1)
-        parts = gain_and_clamp(acc, NARROW, 1)
-        acc_second = open_y(j_second, NARROW, "a_bank")
-        acc_third = open_y(j_third, NARROW, "a_bank")
-        add_codes(acc_second, j_second, NARROW, 0)
-        add_codes(acc_third, j_third, NARROW, 0)
-        y_first = add_bias(acc_first, j_first, WIDE)
-        y_bf_first = round_y(y_first, WIDE)
-        quantise_h(j_second, NARROW, 1, h_bf)
-        add_codes(acc_second, j_second, NARROW, 1)
+        parts = gain_and_clamp(acc_c1, third, 1)
+        quantise_h(*third, 0, h_bf)
         h_bf = subtract(NARROW, *parts)
+        y_first = add_bias(y_first_acc, *first)
+        y_third_acc = psum_results((4, 5), NARROW)
+        open_y(y_third_acc, third, range(PACK))
+        add_codes(y_third_acc, *third, 0)
+        y_bf_first = round_y(y_first, NARROW)
+        quantise_h(*third, 1, h_bf)
+        add_codes(y_third_acc, *third, 1)
 
-        y_second = add_bias(acc_second, j_second, NARROW)
-        quantise_y(y_bf_first, j_first, WIDE)
-        quantise_h(j_third, NARROW, 1, h_bf)
-        add_codes(acc_third, j_third, NARROW, 1)
-        y_bf_second = round_y(y_second, NARROW)
-        y_third = add_bias(acc_third, j_third, NARROW)
-        quantise_y(y_bf_second, j_second, NARROW)
-        quantise_y(round_y(y_third, NARROW), j_third, NARROW)
+        y_second = add_bias(y_second_acc, *second)
+        quantise_y(y_bf_first, *first)
+        y_bf_second = round_y(y_second, WIDE)
+        y_third = add_bias(y_third_acc, *third)
+        quantise_y(y_bf_second, *second)
+        quantise_y(round_y(y_third, NARROW), *third)
 
         for q in range(QUADRANTS):
             (nc.sync if q % 2 == 0 else nc.scalar).dma_start(

@@ -93,6 +93,8 @@ def tile_list_sparse_code_synthesis_kernel(
         for s in range(PLACES):
             nc.scalar.activation(cut[:, s : s + 1], gain[:, s : s + 1], ACT.Abs, scale=lam_gain[:, s : s + 1])
         nc.scalar.activation(neg_cut[:], cut[:], ACT.Copy, scale=-1.0)
+        neg_gain = keep.tile([P, PACK], F32, name="neg_gain")
+        nc.scalar.activation(neg_gain[:], gain[:, 0:PACK], ACT.Copy, scale=-1.0)
 
         v_codes = [keep.tile([P, S], U32, name="v_codes%d" % a, align_bytes=64) for a in range(PASSES)]
         v2_codes = [keep.tile([P, S2], U32, name="v2_codes%d" % a, align_bytes=64) for a in range(PASSES)]
@@ -127,9 +129,6 @@ def tile_list_sparse_code_synthesis_kernel(
         place_rows(v2_sc, v2s_listed)
         v2_table1 = keep.tile([P, T2], I32, name="v2_table1", tag="slot_a", align_bytes=64)
         load_words(v2_table1, tab2_words[1])
-        nc.sync.dma_start(
-            v2s_pass1[0:SHIFTED, :].bitcast(I32), v2_sc[PLANE_ROWS : PLANE_ROWS + SHIFTED, :].bitcast(I32)
-        )
 
         gather_v2(0, v2_table0, 0, S2)
         w4_raw = [
@@ -156,6 +155,9 @@ def tile_list_sparse_code_synthesis_kernel(
                 w4s_raw[QUADRANT * q : QUADRANT * q + PASSES * PLANE_ROWS, :].bitcast(I32),
                 w4_scales[:, PLANE_ROWS * q : PLANE_ROWS * (q + 1), :].bitcast(I32),
             )
+        nc.sync.dma_start(
+            v2s_pass1[0:SHIFTED, :].bitcast(I32), v2_sc[PLANE_ROWS : PLANE_ROWS + SHIFTED, :].bitcast(I32)
+        )
         for j0, width in CHUNKS:
             gather_v2(1, v2_table1, j0, j0 + width)
 
@@ -235,9 +237,22 @@ def tile_list_sparse_code_synthesis_kernel(
                             stop=(a == PASSES - 1 and t == first_t + per_bank - 1),
                         )
 
-        def gain_and_clamp(acc, chunk, h):
+        def two_relus(acc, chunk, h):
             width = chunk[1]
-            gained = work.tile([P, PACK, width], F32, name="gained")
+            above = work.tile([P, PACK, width], F32, name="gained")
+            below = work.tile([P, PACK, width], F32, name="clamped")
+            for t in range(PACK):
+                place = slice(PACK * h + t, PACK * h + t + 1)
+                nc.scalar.activation(above[:, t, :], acc[t], ACT.Relu, scale=gain[:, place], bias=neg_cut[:, place])
+                nc.scalar.activation(below[:, t, :], acc[t], ACT.Relu, scale=neg_gain[:, t : t + 1], bias=neg_cut[:, place])
+            return above, below
+
+        def gain_and_clamp(acc, chunk, h, over=None):
+            width = chunk[1]
+            if over:
+                gained = keep.tile([P, PACK, width], F32, name="gained_over", tag=over, align_bytes=64)
+            else:
+                gained = work.tile([P, PACK, width], F32, name="gained")
             clamped = work.tile([P, PACK, width], F32, name="clamped")
             for t in range(PACK):
                 place = slice(PACK * h + t, PACK * h + t + 1)
@@ -318,7 +333,7 @@ def tile_list_sparse_code_synthesis_kernel(
         correlate(acc_a1, first, 1, [1])
         correlate(acc_b0, second, 0, [1])
 
-        h_bf = subtract(NARROW, *gain_and_clamp(acc_a0, first, 0))
+        h_bf = subtract(NARROW, *gain_and_clamp(acc_a0, first, 0, over="slot_d"))
         parts = gain_and_clamp(acc_a1, first, 1)
         quantise_h(*first, 0, h_bf)
         h_bf = subtract(NARROW, *parts)
@@ -342,10 +357,10 @@ def tile_list_sparse_code_synthesis_kernel(
 
         y_second_acc = psum_results((0, 1, 2, 3), WIDE)
         open_y(y_second_acc, second, range(PACK))
-        parts = gain_and_clamp(acc_c0, third, 0)
+        round_w(1)
+        parts = two_relus(acc_c0, third, 0)
         acc_c1 = psum_results((4, 5), NARROW)
         correlate(acc_c1, third, 1, range(PASSES))
-        round_w(1)
         add_codes(y_second_acc, *second, 0)
         quantise_w(1)
         add_codes(y_first_acc, *first, 1)

@@ -28,6 +28,7 @@ QUADRANTS = P // QUADRANT
 PLANE_ROWS = QUADRANT // BLOCK_P
 SCALE_ROWS = PASSES * QUADRANTS * PLANE_ROWS
 SHIFTED = P - 16
+HALF = P // 2
 BANK = 512
 LIST_ROWS = 16
 WIDE = BANK
@@ -48,11 +49,17 @@ def tile_list_sparse_code_synthesis_kernel(
         work = ctx.enter_context(tc.tile_pool(name="work", bufs=3))
         psum = ctx.enter_context(tc.psum_pool(name="psum", bufs=1))
 
+        v2s_pass1 = keep.tile([P, S2], U8, name="v2s_pass1", align_bytes=64)
+        w4s_both = keep.tile([P, 2 * N], U8, name="w4s_both", align_bytes=64)
+        nc.gpsimd.memset(v2s_pass1[:].bitcast(I32), 0)
+        nc.gpsimd.memset(w4s_both[:].bitcast(I32), 0)
         ident = keep.tile([P, P], F32, name="ident")
         make_identity(nc, ident[:])
 
-        def load_scale_rows(table, scales):
-            nc.sync.dma_start(table[0:SCALE_ROWS, :].bitcast(I32), scales.rearrange("a q t -> q a t").bitcast(I32))
+        def load_scale_rows(table, scales, first):
+            nc.sync.dma_start(
+                table[first : first + SCALE_ROWS, :].bitcast(I32), scales.rearrange("a q t -> q a t").bitcast(I32)
+            )
 
         def load_words(table, words):
             nc.sync.dma_start(table[:], words.rearrange("p t i -> p (t i)").bitcast(I32))
@@ -62,31 +69,37 @@ def tile_list_sparse_code_synthesis_kernel(
         vs_table = keep.tile([P, T], U8, name="vs_table", tag="slot_b", align_bytes=64)
         v2s_table = keep.tile([P, T2], U8, name="v2s_table", tag="slot_a", align_bytes=64)
         nc.sync.dma_start(idx[:], offs)
-        load_scale_rows(vs_table, tab_scales)
+        load_scale_rows(vs_table, tab_scales, HALF)
         nc.sync.dma_start(idx2[:], offs2)
-        load_scale_rows(v2s_table, tab2_scales)
+        load_scale_rows(v2s_table, tab2_scales, 0)
         v2_table0 = keep.tile([P, T2], I32, name="v2_table0", tag="slot_c", align_bytes=64)
         load_words(v2_table0, tab2_words[0])
         v_first = keep.tile([P, T], I32, name="v_first", tag="slot_d", align_bytes=64)
         load_words(v_first, tab_words[0])
 
-        by_place = keep.tile([P, P], F32, name="by_place")
-        v2s_pass1 = keep.tile([P, S2], U8, name="v2s_pass1", align_bytes=64)
-        nc.vector.memset(by_place[:], 0.0)
-        for table in (vs_table, v2s_table):
-            nc.vector.memset(table[SCALE_ROWS : P // 2, :].bitcast(I32), 0)
-            nc.vector.memset(table[P // 2 : P, :].bitcast(I32), 0)
-        nc.vector.memset(v2s_pass1[:].bitcast(I32), 0)
+        nc.vector.memset(vs_table[0:HALF, :].bitcast(I32), 0)
+        nc.vector.memset(vs_table[HALF + SCALE_ROWS : P, :].bitcast(I32), 0)
+        nc.vector.memset(v2s_table[SCALE_ROWS:HALF, :].bitcast(I32), 0)
+        nc.vector.memset(v2s_table[HALF:P, :].bitcast(I32), 0)
 
+        rows = keep.tile([P, PACK, P], F32, name="rows")
+        by_place = keep.tile([P, PACK, P], F32, name="by_place")
+        nc.scalar.activation(rows[:], ident[:].unsqueeze(1).to_broadcast([P, PACK, P]), ACT.Copy, scale=0.0)
         for k, vec in enumerate((lam, g)):
             nc.scalar.dma_start(
-                by_place[PLACES * k : PLACES * (k + 1), :].rearrange("s (u q) -> s u q", q=BLOCK_P),
-                vec.rearrange("(u s q) -> s u q", s=PLACES, q=BLOCK_P),
+                rows[PASSES * k : PASSES * (k + 1), :, :].rearrange("h x y -> h (x y)"), vec.rearrange("(h i) -> h i", h=PASSES)
             )
-        turned = psum.tile([P, BANK], F32, name="bank7")
-        nc.tensor.transpose(turned[:, 0:P], by_place[:], ident[:])
+        nc.scalar.copy(
+            by_place[:].rearrange("r t (u q) -> r t u q", q=BLOCK_P),
+            rows[:].rearrange("r x y -> r (x y)").rearrange("r (u t q) -> r t u q", t=PACK, q=BLOCK_P),
+        )
+        turned = psum.tile([P, PACK, P], F32, name="bank7")
+        for t in range(PACK):
+            nc.tensor.transpose(turned[:, t, :], by_place[:, t, :], ident[:])
         lam_gain = keep.tile([P, 2 * PLACES], F32, name="lam_gain")
-        nc.scalar.copy(lam_gain[:], turned[:, 0 : 2 * PLACES])
+        nc.scalar.copy(
+            lam_gain[:].rearrange("p (r t) -> p r t", t=PACK), turned[:, :, 0 : 2 * PASSES].rearrange("p t r -> p r t")
+        )
         gain = lam_gain[:, PLACES : 2 * PLACES]
         cut = keep.tile([P, PLACES], F32, name="cut")
         neg_cut = keep.tile([P, PLACES], F32, name="neg_cut")
@@ -99,9 +112,12 @@ def tile_list_sparse_code_synthesis_kernel(
         v_codes = [keep.tile([P, S], U32, name="v_codes%d" % a, align_bytes=64) for a in range(PASSES)]
         v2_codes = [keep.tile([P, S2], U32, name="v2_codes%d" % a, align_bytes=64) for a in range(PASSES)]
 
+        def dealt(columns):
+            return columns.rearrange("p (h t u q) -> p h u t q", h=PASSES, t=PACK, q=BLOCK_P)
+
         def gather_v(a, table):
             nc.vector.tensor_copy(
-                v_codes[a][:].rearrange("p (s u q) -> p u s q", s=PLACES, q=BLOCK_P),
+                dealt(v_codes[a][:]),
                 table[:].bitcast(U32).indirect(idx[:]),
             )
 
@@ -111,22 +127,22 @@ def tile_list_sparse_code_synthesis_kernel(
                 table[:].bitcast(U32).indirect(idx2[:, j0 // LIST_ROWS : j1 // LIST_ROWS]),
             )
 
-        def place_rows(planes, rows):
+        def place_rows(planes, rows, first):
             for r in range(PLANE_ROWS):
                 nc.sync.dma_start(
-                    planes[r:P:PLANE_ROWS, :].bitcast(I32), rows[2 * r : 2 * r + SCALE_ROWS, :].bitcast(I32)
+                    planes[r:P:PLANE_ROWS, :].bitcast(I32), rows[first + 2 * r : first + 2 * r + SCALE_ROWS, :].bitcast(I32)
                 )
 
         vs_listed = keep.tile([P, S], U8, name="vs_listed", align_bytes=64)
         vs_placed = keep.tile([P, S], U8, name="vs_placed", align_bytes=64)
-        nc.vector.tensor_copy(vs_listed[:], vs_table[:].indirect(idx[:]))
-        place_rows(vs_placed, vs_listed)
+        nc.vector.tensor_copy(dealt(vs_listed[:]), vs_table[:].indirect(idx[:]))
+        place_rows(vs_placed, vs_listed, HALF)
         v_second = keep.tile([P, T], I32, name="v_second", tag="slot_b", align_bytes=64)
         load_words(v_second, tab_words[1])
         v2s_listed = keep.tile([P, S2], U8, name="v2s_listed", align_bytes=64)
         v2_sc = keep.tile([P, S2], U8, name="v2_sc", align_bytes=64)
         nc.vector.tensor_copy(v2s_listed[:], v2s_table[:].indirect(idx2[:]))
-        place_rows(v2_sc, v2s_listed)
+        place_rows(v2_sc, v2s_listed, 0)
         v2_table1 = keep.tile([P, T2], I32, name="v2_table1", tag="slot_a", align_bytes=64)
         load_words(v2_table1, tab2_words[1])
 
@@ -138,18 +154,8 @@ def tile_list_sparse_code_synthesis_kernel(
         nc.sync.dma_start(w4_raw[0][:].bitcast(I32), w4_words[0].bitcast(I32))
         gather_v(0, v_first)
         nc.sync.dma_start(w4_raw[1][:].bitcast(I32), w4_words[1].bitcast(I32))
-        def deal_v_scales(h, tag):
-            planes = keep.tile([P, PASS], U8, name="v_sc", tag=tag, align_bytes=64)
-            nc.vector.tensor_copy(
-                planes[:].bitcast(I32).rearrange("p (t u e) -> p t u e", t=PACK, e=2),
-                vs_placed[:].bitcast(I32).rearrange("p (u h t e) -> p h t u e", h=PASSES, t=PACK, e=2)[:, h],
-            )
-            return planes
-
-        v_sc = [deal_v_scales(0, "v_sc0")]
         gather_v(1, v_second)
-        v_sc.extend([deal_v_scales(1, "slot_b")])
-        w4s_raw = vs_placed[:, 0:N]
+        w4s_raw = w4s_both[:, 0:N]
         for q in range(QUADRANTS):
             nc.sync.dma_start(
                 w4s_raw[QUADRANT * q : QUADRANT * q + PASSES * PLANE_ROWS, :].bitcast(I32),
@@ -175,12 +181,12 @@ def tile_list_sparse_code_synthesis_kernel(
             keep.tile([P, PACK, N], F32, name="w_raw0", align_bytes=64),
             keep.tile([P, PACK, N], F32, name="w_raw1", tag="slot_a", align_bytes=64),
         ]
-        w_rows = w.rearrange("(u h t q) n -> h t u q n", h=PASSES, t=PACK, q=BLOCK_P)
+        w_rows = w.rearrange("(h u t q) n -> h t u q n", h=PASSES, t=PACK, q=BLOCK_P)
         for h in range(PASSES):
             for t in range(PACK):
                 nc.sync.dma_start(w_raw[h][:, t, :], w_rows[h, t])
             if h == 0:
-                w4s_pass1 = vs_placed[:, N : 2 * N]
+                w4s_pass1 = w4s_both[:, N : 2 * N]
                 nc.sync.dma_start(
                     w4s_pass1[0:SHIFTED, :].bitcast(I32), w4_sc[PLANE_ROWS : PLANE_ROWS + SHIFTED, :].bitcast(I32)
                 )
@@ -230,7 +236,7 @@ def tile_list_sparse_code_synthesis_kernel(
                         nc.tensor.matmul_mx(
                             acc[t],
                             lhsT=v_codes[a][:, cols].bitcast(FP8X4),
-                            lhsT_scale=v_sc[h][PLANE_ROWS * a : P, P * t : P * (t + 1)],
+                            lhsT_scale=vs_placed[PLANE_ROWS * a : P, cols],
                             rhs=v2_codes[a][:, j0 : j0 + width].bitcast(FP8X4),
                             rhs_scale=v2_sc[PLANE_ROWS * a : P, j0 : j0 + width],
                             start=(a == 0 and t == first_t),
@@ -312,11 +318,12 @@ def tile_list_sparse_code_synthesis_kernel(
                     nc.sync.dma_start(y_rows[:, t - 1 : t + 1, j0 : j0 + width], y[:, t - 1 : t + 1, :])
             return y
 
-        def round_y(y, width):
+        def round_y(y, width, shared):
             y_bf = work.tile([P, PACK * width], BF16, name="y_bf", align_bytes=64)
-            for c in range(0, width, NARROW):
-                copy = nc.scalar.copy if c + NARROW < width else nc.vector.tensor_copy
-                copy(as_words(y_bf[:, PACK * c : PACK * (c + NARROW)], COPY_RUN), as_rows(y[:, :, c : c + NARROW], COPY_RUN))
+            part = width // 2 if shared else width
+            for c in range(0, width, part):
+                copy = nc.scalar.copy if c + part < width else nc.vector.tensor_copy
+                copy(as_words(y_bf[:, PACK * c : PACK * (c + part)], COPY_RUN), as_rows(y[:, :, c : c + part], COPY_RUN))
             return y_bf
 
         def quantise_y(y_bf, j0, width):
@@ -375,16 +382,16 @@ def tile_list_sparse_code_synthesis_kernel(
         y_third_acc = psum_results((4, 5), NARROW)
         open_y(y_third_acc, third, range(PACK))
         add_codes(y_third_acc, *third, 0)
-        y_bf_first = round_y(y_first, NARROW)
+        y_bf_first = round_y(y_first, NARROW, False)
         quantise_h(*third, 1, h_bf)
         add_codes(y_third_acc, *third, 1)
 
         y_second = add_bias(y_second_acc, *second)
         quantise_y(y_bf_first, *first)
-        y_bf_second = round_y(y_second, WIDE)
+        y_bf_second = round_y(y_second, WIDE, True)
         y_third = add_bias(y_third_acc, *third)
         quantise_y(y_bf_second, *second)
-        quantise_y(round_y(y_third, NARROW), *third)
+        quantise_y(round_y(y_third, NARROW, True), *third)
 
         for q in range(QUADRANTS):
             (nc.sync if q % 2 == 0 else nc.scalar).dma_start(

@@ -49,10 +49,6 @@ def tile_list_sparse_code_synthesis_kernel(
         work = ctx.enter_context(tc.tile_pool(name="work", bufs=3))
         psum = ctx.enter_context(tc.psum_pool(name="psum", bufs=1))
 
-        v2s_pass1 = keep.tile([P, S2], U8, name="v2s_pass1", align_bytes=64)
-        w4s_both = keep.tile([P, 2 * N], U8, name="w4s_both", align_bytes=64)
-        nc.gpsimd.memset(v2s_pass1[:].bitcast(I32), 0)
-        nc.gpsimd.memset(w4s_both[:].bitcast(I32), 0)
         ident = keep.tile([P, P], F32, name="ident")
         make_identity(nc, ident[:])
 
@@ -68,8 +64,8 @@ def tile_list_sparse_code_synthesis_kernel(
         idx2 = lists.tile([P, S2 // LIST_ROWS], U16, name="idx2")
         vs_table = keep.tile([P, T], U8, name="vs_table", tag="slot_b", align_bytes=64)
         v2s_table = keep.tile([P, T2], U8, name="v2s_table", tag="slot_a", align_bytes=64)
-        nc.sync.dma_start(idx[:], offs)
         load_scale_rows(vs_table, tab_scales, HALF)
+        nc.sync.dma_start(idx[:], offs)
         nc.sync.dma_start(idx2[:], offs2)
         load_scale_rows(v2s_table, tab2_scales, 0)
         v2_table0 = keep.tile([P, T2], I32, name="v2_table0", tag="slot_c", align_bytes=64)
@@ -82,8 +78,8 @@ def tile_list_sparse_code_synthesis_kernel(
         nc.vector.memset(v2s_table[SCALE_ROWS:HALF, :].bitcast(I32), 0)
         nc.vector.memset(v2s_table[HALF:P, :].bitcast(I32), 0)
 
-        rows = keep.tile([P, PACK, P], F32, name="rows")
-        by_place = keep.tile([P, PACK, P], F32, name="by_place")
+        rows = keep.tile([P, PACK, P], F32, name="rows", tag="slot_e", align_bytes=64)
+        by_place = keep.tile([P, PACK, P], F32, name="by_place", tag="slot_f", align_bytes=64)
         nc.scalar.activation(rows[:], ident[:].unsqueeze(1).to_broadcast([P, PACK, P]), ACT.Copy, scale=0.0)
         for k, vec in enumerate((lam, g)):
             nc.scalar.dma_start(
@@ -100,6 +96,10 @@ def tile_list_sparse_code_synthesis_kernel(
         nc.scalar.copy(
             lam_gain[:].rearrange("p (r t) -> p r t", t=PACK), turned[:, :, 0 : 2 * PASSES].rearrange("p t r -> p r t")
         )
+        v2s_pass1 = keep.tile([P, S2], U8, name="v2s_pass1", tag="slot_e", align_bytes=64)
+        w4s_both = keep.tile([P, 2 * N], U8, name="w4s_both", tag="slot_f", align_bytes=64)
+        nc.gpsimd.memset(v2s_pass1[:].bitcast(I32), 0)
+        nc.gpsimd.memset(w4s_both[:].bitcast(I32), 0)
         gain = lam_gain[:, PLACES : 2 * PLACES]
         cut = keep.tile([P, PLACES], F32, name="cut")
         neg_cut = keep.tile([P, PLACES], F32, name="neg_cut")

@@ -28,7 +28,9 @@ QUADRANTS = P // QUADRANT
 PLANE_ROWS = QUADRANT // BLOCK_P
 SCALE_ROWS = PASSES * QUADRANTS * PLANE_ROWS
 SHIFTED = P - 16
-HALF = P // 2
+ROW_STEP = 2
+FIRST_ROW = QUADRANT
+AHEAD = T2 // 4
 BANK = 512
 LIST_ROWS = 16
 WIDE = BANK
@@ -52,31 +54,32 @@ def tile_list_sparse_code_synthesis_kernel(
         ident = keep.tile([P, P], F32, name="ident")
         make_identity(nc, ident[:])
 
-        def load_scale_rows(table, scales, first):
+        def load_scale_rows(table, scales):
             nc.sync.dma_start(
-                table[first : first + SCALE_ROWS, :].bitcast(I32), scales.rearrange("a q t -> q a t").bitcast(I32)
+                table[FIRST_ROW : FIRST_ROW + ROW_STEP * SCALE_ROWS : ROW_STEP, :].bitcast(I32),
+                scales.rearrange("a q t -> q a t").bitcast(I32),
             )
 
-        def load_words(table, words):
-            nc.sync.dma_start(table[:], words.rearrange("p t i -> p (t i)").bitcast(I32))
+        def load_words(table, words, columns=slice(None)):
+            nc.sync.dma_start(table[:, columns], words.rearrange("p t i -> p (t i)").bitcast(I32)[:, columns])
 
         idx = lists.tile([P, S // LIST_ROWS], U16, name="idx")
         idx2 = lists.tile([P, S2 // LIST_ROWS], U16, name="idx2")
-        vs_table = keep.tile([P, T], U8, name="vs_table", tag="slot_b", align_bytes=64)
+        vs_table = keep.tile([P, T], U8, name="vs_table", align_bytes=64)
         v2s_table = keep.tile([P, T2], U8, name="v2s_table", tag="slot_a", align_bytes=64)
-        load_scale_rows(vs_table, tab_scales, HALF)
-        nc.sync.dma_start(idx[:], offs)
-        nc.sync.dma_start(idx2[:], offs2)
-        load_scale_rows(v2s_table, tab2_scales, 0)
+        nc.vector.memset(vs_table[:].bitcast(I32), 0)
+        nc.vector.memset(v2s_table[:].bitcast(I32), 0)
         v2_table0 = keep.tile([P, T2], I32, name="v2_table0", tag="slot_c", align_bytes=64)
-        load_words(v2_table0, tab2_words[0])
+        load_words(v2_table0, tab2_words[0], slice(0, AHEAD))
+        load_scale_rows(vs_table, tab_scales)
+        nc.sync.dma_start(idx[:], offs)
+        load_scale_rows(v2s_table, tab2_scales)
+        nc.sync.dma_start(idx2[:], offs2)
+        load_words(v2_table0, tab2_words[0], slice(AHEAD, T2))
         v_first = keep.tile([P, T], I32, name="v_first", tag="slot_d", align_bytes=64)
         load_words(v_first, tab_words[0])
-
-        nc.vector.memset(vs_table[0:HALF, :].bitcast(I32), 0)
-        nc.vector.memset(vs_table[HALF + SCALE_ROWS : P, :].bitcast(I32), 0)
-        nc.vector.memset(v2s_table[SCALE_ROWS:HALF, :].bitcast(I32), 0)
-        nc.vector.memset(v2s_table[HALF:P, :].bitcast(I32), 0)
+        v_second = keep.tile([P, T], I32, name="v_second", align_bytes=64)
+        load_words(v_second, tab_words[1])
 
         rows = keep.tile([P, PACK, P], F32, name="rows", tag="slot_e", align_bytes=64)
         by_place = keep.tile([P, PACK, P], F32, name="by_place", tag="slot_f", align_bytes=64)
@@ -127,22 +130,20 @@ def tile_list_sparse_code_synthesis_kernel(
                 table[:].bitcast(U32).indirect(idx2[:, j0 // LIST_ROWS : j1 // LIST_ROWS]),
             )
 
-        def place_rows(planes, rows, first):
+        def place_rows(planes, rows):
             for r in range(PLANE_ROWS):
+                first = FIRST_ROW + ROW_STEP * PASSES * r
                 nc.sync.dma_start(
-                    planes[r:P:PLANE_ROWS, :].bitcast(I32), rows[first + 2 * r : first + 2 * r + SCALE_ROWS, :].bitcast(I32)
+                    planes[r:P:PLANE_ROWS, :].bitcast(I32),
+                    rows[first : first + ROW_STEP * SCALE_ROWS : ROW_STEP, :].bitcast(I32),
                 )
 
-        vs_listed = keep.tile([P, S], U8, name="vs_listed", align_bytes=64)
-        vs_placed = keep.tile([P, S], U8, name="vs_placed", align_bytes=64)
-        nc.vector.tensor_copy(dealt(vs_listed[:]), vs_table[:].indirect(idx[:]))
-        place_rows(vs_placed, vs_listed, HALF)
-        v_second = keep.tile([P, T], I32, name="v_second", tag="slot_b", align_bytes=64)
-        load_words(v_second, tab_words[1])
-        v2s_listed = keep.tile([P, S2], U8, name="v2s_listed", align_bytes=64)
-        v2_sc = keep.tile([P, S2], U8, name="v2_sc", align_bytes=64)
-        nc.vector.tensor_copy(v2s_listed[:], v2s_table[:].indirect(idx2[:]))
-        place_rows(v2_sc, v2s_listed, 0)
+        listed = keep.tile([P, S + S2], U8, name="listed", align_bytes=64)
+        placed = keep.tile([P, S + S2], U8, name="placed", align_bytes=64)
+        vs_placed, v2_sc = placed[:, 0:S], placed[:, S : S + S2]
+        nc.vector.tensor_copy(dealt(listed[:, 0:S]), vs_table[:].indirect(idx[:]))
+        nc.vector.tensor_copy(listed[:, S : S + S2], v2s_table[:].indirect(idx2[:]))
+        place_rows(placed, listed)
         v2_table1 = keep.tile([P, T2], I32, name="v2_table1", tag="slot_a", align_bytes=64)
         load_words(v2_table1, tab2_words[1])
 

from contextlib import ExitStack

import concourse.mybir as mybir
from concourse.masks import make_identity

K, T, S, T2, S2, N = 1024, 2048, 1024, 4096, 1024, 512
FLOPS = 2 * (K * S * S2 + S * N * S2 + K * N * S2)

F32 = mybir.dt.float32
BF16 = mybir.dt.bfloat16
I32 = mybir.dt.int32
U32 = mybir.dt.uint32
U16 = mybir.dt.uint16
U8 = mybir.dt.uint8
FP8X4 = mybir.dt.float8_e4m3fn_x4
FP4X4 = mybir.dt.float4_e2m1fn_x4
ALU = mybir.AluOpType
ACT = mybir.ActivationFunctionType

P = 128
PACK = 4
PASS = P * PACK
PASSES = 2
PLACES = PASSES * PACK
BLOCK_P = 8
QUADRANT = 32
QUADRANTS = P // QUADRANT
PLANE_ROWS = QUADRANT // BLOCK_P
SCALE_ROWS = PASSES * QUADRANTS * PLANE_ROWS
SHIFTED = P - 16
ROW_STEP = 2
FIRST_ROW = QUADRANT
AHEAD = T2 // 4
BANK = 512
LIST_ROWS = 16
WIDE = BANK
NARROW = BANK // 2
CHUNKS = ((0, NARROW), (NARROW, WIDE), (NARROW + WIDE, NARROW))
COPY_RUN = 4
SUBTRACT_RUN = 8


def tile_list_sparse_code_synthesis_kernel(
    tc, tab_words, tab_scales, tab2_words, tab2_scales, w4_words, w4_scales, w, lam, g, b, offs, offs2,
    out_0, out_1, out_2,
):
    nc = tc.nc
    with ExitStack() as ctx:
        lists = ctx.enter_context(tc.tile_pool(name="lists", bufs=1))
        keep = ctx.enter_context(tc.tile_pool(name="keep", bufs=1))
        work = ctx.enter_context(tc.tile_pool(name="work", bufs=3))
        psum = ctx.enter_context(tc.psum_pool(name="psum", bufs=1))

        ident = keep.tile([P, P], F32, name="ident")
        make_identity(nc, ident[:])

        def load_scale_rows(table, scales):
            nc.sync.dma_start(
                table[FIRST_ROW : FIRST_ROW + ROW_STEP * SCALE_ROWS : ROW_STEP, :].bitcast(I32),
                scales.rearrange("a q t -> q a t").bitcast(I32),
            )

        def load_words(table, words, columns=slice(None)):
            nc.sync.dma_start(table[:, columns], words.rearrange("p t i -> p (t i)").bitcast(I32)[:, columns])

        idx = lists.tile([P, S // LIST_ROWS], U16, name="idx")
        idx2 = lists.tile([P, S2 // LIST_ROWS], U16, name="idx2")
        vs_table = keep.tile([P, T], U8, name="vs_table", align_bytes=64)
        v2s_table = keep.tile([P, T2], U8, name="v2s_table", tag="slot_a", align_bytes=64)
        nc.vector.memset(vs_table[:].bitcast(I32), 0)
        nc.vector.memset(v2s_table[:].bitcast(I32), 0)
        v2_table0 = keep.tile([P, T2], I32, name="v2_table0", tag="slot_c", align_bytes=64)
        load_words(v2_table0, tab2_words[0], slice(0, AHEAD))
        load_scale_rows(vs_table, tab_scales)
        nc.sync.dma_start(idx[:], offs)
        load_scale_rows(v2s_table, tab2_scales)
        nc.sync.dma_start(idx2[:], offs2)
        load_words(v2_table0, tab2_words[0], slice(AHEAD, T2))
        v_first = keep.tile([P, T], I32, name="v_first", tag="slot_d", align_bytes=64)
        load_words(v_first, tab_words[0])
        v_second = keep.tile([P, T], I32, name="v_second", align_bytes=64)
        load_words(v_second, tab_words[1])

        rows = keep.tile([P, PACK, P], F32, name="rows", tag="slot_e", align_bytes=64)
        by_place = keep.tile([P, PACK, P], F32, name="by_place", tag="slot_f", align_bytes=64)
        nc.scalar.activation(rows[:], ident[:].unsqueeze(1).to_broadcast([P, PACK, P]), ACT.Copy, scale=0.0)
        for k, vec in enumerate((lam, g)):
            nc.scalar.dma_start(
                rows[PASSES * k : PASSES * (k + 1), :, :].rearrange("h x y -> h (x y)"), vec.rearrange("(h i) -> h i", h=PASSES)
            )
        nc.scalar.copy(
            by_place[:].rearrange("r t (u q) -> r t u q", q=BLOCK_P),
            rows[:].rearrange("r x y -> r (x y)").rearrange("r (u t q) -> r t u q", t=PACK, q=BLOCK_P),
        )
        turned = psum.tile([P, PACK, P], F32, name="bank7")
        for t in range(PACK):
            nc.tensor.transpose(turned[:, t, :], by_place[:, t, :], ident[:])
        lam_gain = keep.tile([P, 2 * PLACES], F32, name="lam_gain")
        nc.scalar.copy(
            lam_gain[:].rearrange("p (r t) -> p r t", t=PACK), turned[:, :, 0 : 2 * PASSES].rearrange("p t r -> p r t")
        )
        v2s_pass1 = keep.tile([P, S2], U8, name="v2s_pass1", tag="slot_e", align_bytes=64)
        w4s_both = keep.tile([P, 2 * N], U8, name="w4s_both", tag="slot_f", align_bytes=64)
        nc.gpsimd.memset(v2s_pass1[:].bitcast(I32), 0)
        nc.gpsimd.memset(w4s_both[:].bitcast(I32), 0)
        gain = lam_gain[:, PLACES : 2 * PLACES]
        cut = keep.tile([P, PLACES], F32, name="cut")
        neg_cut = keep.tile([P, PLACES], F32, name="neg_cut")
        for s in range(PLACES):
            nc.scalar.activation(cut[:, s : s + 1], gain[:, s : s + 1], ACT.Abs, scale=lam_gain[:, s : s + 1])
        nc.scalar.activation(neg_cut[:], cut[:], ACT.Copy, scale=-1.0)
        neg_gain = keep.tile([P, PACK], F32, name="neg_gain")
        nc.scalar.activation(neg_gain[:], gain[:, 0:PACK], ACT.Copy, scale=-1.0)

        v_codes = [keep.tile([P, S], U32, name="v_codes%d" % a, align_bytes=64) for a in range(PASSES)]
        v2_codes = [keep.tile([P, S2], U32, name="v2_codes%d" % a, align_bytes=64) for a in range(PASSES)]

        def dealt(columns):
            return columns.rearrange("p (h t u q) -> p h u t q", h=PASSES, t=PACK, q=BLOCK_P)

        def gather_v(a, table):
            nc.vector.tensor_copy(
                dealt(v_codes[a][:]),
                table[:].bitcast(U32).indirect(idx[:]),
            )

        def gather_v2(a, table, j0, j1):
            nc.vector.tensor_copy(
                v2_codes[a][:, j0:j1],
                table[:].bitcast(U32).indirect(idx2[:, j0 // LIST_ROWS : j1 // LIST_ROWS]),
            )

        def place_rows(planes, rows):
            for r in range(PLANE_ROWS):
                first = FIRST_ROW + ROW_STEP * PASSES * r
                nc.sync.dma_start(
                    planes[r:P:PLANE_ROWS, :].bitcast(I32),
                    rows[first : first + ROW_STEP * SCALE_ROWS : ROW_STEP, :].bitcast(I32),
                )

        listed = keep.tile([P, S + S2], U8, name="listed", align_bytes=64)
        placed = keep.tile([P, S + S2], U8, name="placed", align_bytes=64)
        vs_placed, v2_sc = placed[:, 0:S], placed[:, S : S + S2]
        nc.vector.tensor_copy(dealt(listed[:, 0:S]), vs_table[:].indirect(idx[:]))
        nc.vector.tensor_copy(listed[:, S : S + S2], v2s_table[:].indirect(idx2[:]))
        place_rows(placed, listed)
        v2_table1 = keep.tile([P, T2], I32, name="v2_table1", tag="slot_a", align_bytes=64)
        load_words(v2_table1, tab2_words[1])

        gather_v2(0, v2_table0, 0, S2)
        w4_raw = [
            keep.tile([P, 2 * N], U8, name="w4_raw0", tag="slot_c", align_bytes=64),
            keep.tile([P, 2 * N], U8, name="w4_raw1", tag="slot_d", align_bytes=64),
        ]
        nc.sync.dma_start(w4_raw[0][:].bitcast(I32), w4_words[0].bitcast(I32))
        gather_v(0, v_first)
        nc.sync.dma_start(w4_raw[1][:].bitcast(I32), w4_words[1].bitcast(I32))
        gather_v(1, v_second)
        w4s_raw = w4s_both[:, 0:N]
        for q in range(QUADRANTS):
            nc.sync.dma_start(
                w4s_raw[QUADRANT * q : QUADRANT * q + PASSES * PLANE_ROWS, :].bitcast(I32),
                w4_scales[:, PLANE_ROWS * q : PLANE_ROWS * (q + 1), :].bitcast(I32),
            )
        nc.sync.dma_start(
            v2s_pass1[0:SHIFTED, :].bitcast(I32), v2_sc[PLANE_ROWS : PLANE_ROWS + SHIFTED, :].bitcast(I32)
        )
        for j0, width in CHUNKS:
            gather_v2(1, v2_table1, j0, j0 + width)

        w4_codes = [keep.tile([P, 2 * N], U8, name="w4_codes%d" % a, align_bytes=64) for a in range(PASSES)]
        w4_sc = keep.tile([P, N], U8, name="w4_sc", align_bytes=64)
        for a in range(PASSES):
            nc.scalar.copy(
                w4_codes[a][:].bitcast(U16).rearrange("p (t m) -> p t m", t=PACK),
                w4_raw[a][:].bitcast(U16).rearrange("p (m t) -> p t m", t=PACK),
            )
        nc.vector.tensor_copy(
            w4_sc[:].rearrange("p (t m) -> p t m", t=PACK), w4s_raw.rearrange("p (m t) -> p t m", t=PACK)
        )
        w_raw = [
            keep.tile([P, PACK, N], F32, name="w_raw0", align_bytes=64),
            keep.tile([P, PACK, N], F32, name="w_raw1", tag="slot_a", align_bytes=64),
        ]
        w_rows = w.rearrange("(h u t q) n -> h t u q n", h=PASSES, t=PACK, q=BLOCK_P)
        for h in range(PASSES):
            for t in range(PACK):
                nc.sync.dma_start(w_raw[h][:, t, :], w_rows[h, t])
            if h == 0:
                w4s_pass1 = w4s_both[:, N : 2 * N]
                nc.sync.dma_start(
                    w4s_pass1[0:SHIFTED, :].bitcast(I32), w4_sc[PLANE_ROWS : PLANE_ROWS + SHIFTED, :].bitcast(I32)
                )
        w4_planes = [w4_sc[:], w4s_pass1]
        bias = keep.tile([P, PACK], F32, name="bias", tag="slot_c", align_bytes=64)
        nc.sync.dma_start(bias[:], b.rearrange("(p t) -> p t", t=PACK))
        w_bf = [keep.tile([P, PACK * N], BF16, name="w_bf%d" % h, align_bytes=64) for h in range(PASSES)]
        w_codes = [keep.tile([P, N], U32, name="w_codes%d" % h, align_bytes=64) for h in range(PASSES)]
        w_sc = [keep.tile([P, N], U8, name="w_sc%d" % h, align_bytes=64) for h in range(PASSES)]
        h_codes = [keep.tile([P, S2], U32, name="h_codes%d" % h, align_bytes=64) for h in range(PASSES)]
        h_sc = [keep.tile([P, S2], U8, name="h_sc%d" % h, align_bytes=64) for h in range(PASSES)]
        y_sc = keep.tile([P, S2], U8, name="y_sc", align_bytes=64)
        v2_planes_from_row_0 = [v2_sc, v2s_pass1]
        y_rows = out_0.rearrange("(p t) j -> p t j", t=PACK)
        y_words = out_1[0].rearrange("p m t -> p (m t)").bitcast(I32)

        def round_w(h):
            nc.scalar.copy(
                w_bf[h][:].rearrange("p (c m e t) -> p m t e c", c=PACK, e=2, t=PACK),
                w_raw[h][:].rearrange("p t (m e c) -> p m t e c", c=PACK, e=2),
            )

        def quantise_w(h):
            nc.vector.quantize_mx(w_codes[h][:].bitcast(FP8X4), w_sc[h][:], w_bf[h][:])

        def psum_results(banks, width):
            per_bank = BANK // width
            results = []
            for number in banks:
                bank = psum.tile([P, BANK], F32, name="bank%d" % number)
                results.extend([bank[:, width * x : width * (x + 1)] for x in range(per_bank)])
            return results

        def as_words(words, run):
            return words.rearrange("p (c i t) -> p c t i", i=run, t=PACK)

        def as_rows(rows, run):
            return rows.rearrange("p t (c i) -> p c t i", i=run)

        def correlate(acc, chunk, h, passes):
            j0, width = chunk
            per_bank = BANK // width
            for first_t in range(0, PACK, per_bank):
                for a in passes:
                    for t in range(first_t, first_t + per_bank):
                        cols = slice(PASS * h + P * t, PASS * h + P * (t + 1))
                        nc.tensor.matmul_mx(
                            acc[t],
                            lhsT=v_codes[a][:, cols].bitcast(FP8X4),
                            lhsT_scale=vs_placed[PLANE_ROWS * a : P, cols],
                            rhs=v2_codes[a][:, j0 : j0 + width].bitcast(FP8X4),
                            rhs_scale=v2_sc[PLANE_ROWS * a : P, j0 : j0 + width],
                            start=(a == 0 and t == first_t),
                            stop=(a == PASSES - 1 and t == first_t + per_bank - 1),
                        )

        def two_relus(acc, chunk, h):
            width = chunk[1]
            above = work.tile([P, PACK, width], F32, name="gained")
            below = work.tile([P, PACK, width], F32, name="clamped")
            for t in range(PACK):
                place = slice(PACK * h + t, PACK * h + t + 1)
                nc.scalar.activation(above[:, t, :], acc[t], ACT.Relu, scale=gain[:, place], bias=neg_cut[:, place])
                nc.scalar.activation(below[:, t, :], acc[t], ACT.Relu, scale=neg_gain[:, t : t + 1], bias=neg_cut[:, place])
            return above, below

        def gain_and_clamp(acc, chunk, h, over=None):
            width = chunk[1]
            if over:
                gained = keep.tile([P, PACK, width], F32, name="gained_over", tag=over, align_bytes=64)
            else:
                gained = work.tile([P, PACK, width], F32, name="gained")
            clamped = work.tile([P, PACK, width], F32, name="clamped")
            for t in range(PACK):
                place = slice(PACK * h + t, PACK * h + t + 1)
                nc.scalar.activation(gained[:, t, :], acc[t], ACT.Copy, scale=gain[:, place])
                nc.vector.tensor_scalar(
                    clamped[:, t, :], gained[:, t, :], neg_cut[:, place], cut[:, place], ALU.max, ALU.min
                )
            return gained, clamped

        def subtract(width, gained, clamped):
            h_bf = work.tile([P, PACK * width], BF16, name="h_bf", align_bytes=64)
            nc.vector.tensor_tensor(
                as_words(h_bf[:], SUBTRACT_RUN), as_rows(gained[:], SUBTRACT_RUN), as_rows(clamped[:], SUBTRACT_RUN), ALU.subtract
            )
            return h_bf

        def quantise_h(j0, width, h, h_bf):
            nc.vector.quantize_mx(h_codes[h][:, j0 : j0 + width].bitcast(FP8X4), h_sc[h][:, j0 : j0 + width], h_bf[:])

        def open_y(acc, chunk, places):
            j0, width = chunk
            per_bank = BANK // width
            for t in places:
                for a in range(PASSES):
                    nc.tensor.matmul_mx(
                        acc[t],
                        lhsT=w4_codes[a][:, 2 * P * t : 2 * P * (t + 1)].bitcast(FP4X4),
                        lhsT_scale=w4_planes[a][:, P * t : P * (t + 1)],
                        rhs=v2_codes[a][:, j0 : j0 + width].bitcast(FP8X4),
                        rhs_scale=v2_planes_from_row_0[a][:, j0 : j0 + width],
                        start=(a == 0 and t % per_bank == 0),
                        stop=False,
                    )

        def add_codes(acc, j0, width, h):
            per_bank = BANK // width
            for t in range(PACK):
                nc.tensor.matmul_mx(
                    acc[t],
                    lhsT=w_codes[h][:, P * t : P * (t + 1)].bitcast(FP8X4),
                    lhsT_scale=w_sc[h][:, P * t : P * (t + 1)],
                    rhs=h_codes[h][:, j0 : j0 + width].bitcast(FP8X4),
                    rhs_scale=h_sc[h][:, j0 : j0 + width],
                    start=False,
                    stop=(h == PASSES - 1 and t % per_bank == per_bank - 1),
                )

        def add_bias(acc, j0, width):
            last = j0 + width == S2
            y = work.tile([P, PACK, width], F32, name="y")
            for t in range(PACK):
                if last and t >= PACK // 2:
                    nc.vector.tensor_scalar(y[:, t, :], acc[t], bias[:, t : t + 1], None, ALU.add)
                else:
                    nc.scalar.activation(y[:, t, :], acc[t], ACT.Identity, bias=bias[:, t : t + 1])
                if t % 2 == 1:
                    nc.sync.dma_start(y_rows[:, t - 1 : t + 1, j0 : j0 + width], y[:, t - 1 : t + 1, :])
            return y

        def round_y(y, width, shared):
            y_bf = work.tile([P, PACK * width], BF16, name="y_bf", align_bytes=64)
            part = width // 2 if shared else width
            for c in range(0, width, part):
                copy = nc.scalar.copy if c + part < width else nc.vector.tensor_copy
                copy(as_words(y_bf[:, PACK * c : PACK * (c + part)], COPY_RUN), as_rows(y[:, :, c : c + part], COPY_RUN))
            return y_bf

        def quantise_y(y_bf, j0, width):
            y_codes = work.tile([P, width], U32, name="y_codes", align_bytes=64)
            nc.vector.quantize_mx(y_codes[:].bitcast(FP8X4), y_sc[:, j0 : j0 + width], y_bf[:])
            nc.sync.dma_start(y_words[:, j0 : j0 + width], y_codes[:].bitcast(I32))

        first, second, third = CHUNKS
        acc_a0, acc_a1, acc_b0 = psum_results((0, 1), NARROW), psum_results((2, 3), NARROW), psum_results((4, 5, 6, 7), WIDE)
        correlate(acc_a0, first, 0, [0])
        correlate(acc_b0, second, 0, [0])
        correlate(acc_a1, first, 1, [0])
        correlate(acc_a0, first, 0, [1])
        correlate(acc_a1, first, 1, [1])
        correlate(acc_b0, second, 0, [1])

        h_bf = subtract(NARROW, *gain_and_clamp(acc_a0, first, 0, over="slot_d"))
        parts = gain_and_clamp(acc_a1, first, 1)
        quantise_h(*first, 0, h_bf)
        h_bf = subtract(NARROW, *parts)

        acc_b1 = psum_results((0, 1, 2, 3), WIDE)
        correlate(acc_b1, second, 1, range(PASSES))
        parts = gain_and_clamp(acc_b0, second, 0)
        quantise_h(*first, 1, h_bf)
        round_w(0)
        h_bf = subtract(WIDE, *parts)

        acc_c0 = psum_results((4, 5), NARROW)
        correlate(acc_c0, third, 0, range(PASSES))
        y_first_acc = psum_results((6, 7), NARROW)
        open_y(y_first_acc, first, range(PACK))
        parts = gain_and_clamp(acc_b1, second, 1)
        quantise_w(0)
        quantise_h(*second, 0, h_bf)
        add_codes(y_first_acc, *first, 0)
        h_bf = subtract(WIDE, *parts)

        y_second_acc = psum_results((0, 1, 2, 3), WIDE)
        open_y(y_second_acc, second, range(PACK))
        round_w(1)
        parts = two_relus(acc_c0, third, 0)
        acc_c1 = psum_results((4, 5), NARROW)
        correlate(acc_c1, third, 1, range(PASSES))
        add_codes(y_second_acc, *second, 0)
        quantise_w(1)
        add_codes(y_first_acc, *first, 1)
        quantise_h(*second, 1, h_bf)
        add_codes(y_second_acc, *second, 1)
        h_bf = subtract(NARROW, *parts)

        parts = gain_and_clamp(acc_c1, third, 1)
        quantise_h(*third, 0, h_bf)
        h_bf = subtract(NARROW, *parts)
        y_first = add_bias(y_first_acc, *first)
        y_third_acc = psum_results((4, 5), NARROW)
        open_y(y_third_acc, third, range(PACK))
        add_codes(y_third_acc, *third, 0)
        y_bf_first = round_y(y_first, NARROW, False)
        quantise_h(*third, 1, h_bf)
        add_codes(y_third_acc, *third, 1)

        y_second = add_bias(y_second_acc, *second)
        quantise_y(y_bf_first, *first)
        y_bf_second = round_y(y_second, WIDE, True)
        y_third = add_bias(y_third_acc, *third)
        quantise_y(y_bf_second, *second)
        quantise_y(round_y(y_third, NARROW, True), *third)

        for q in range(QUADRANTS):
            (nc.sync if q % 2 == 0 else nc.scalar).dma_start(
                out_2[0, PLANE_ROWS * q : PLANE_ROWS * (q + 1), :].bitcast(I32),
                y_sc[QUADRANT * q : QUADRANT * q + PLANE_ROWS, :].bitcast(I32),
            )
